import numpy as np
import ml_dtypes


def mxq(x, axis, fmt="e4m3"):
    dtype, down = {"e4m3": (ml_dtypes.float8_e4m3fn, 7), "e5m2": (ml_dtypes.float8_e5m2, 14)}[fmt]
    v = np.moveaxis(np.asarray(x, np.float32).astype(ml_dtypes.bfloat16).astype(np.float64), axis, -1)
    blocks = v.reshape(v.shape[:-1] + (-1, 32))
    amax = np.abs(blocks).max(-1, keepdims=True)
    byte = np.maximum(np.where(amax > 0, np.frexp(amax)[1] - 1 + 127, 0) - down, 1)
    scale = np.exp2(byte - 127.0)
    codes = (blocks / scale).astype(np.float32).astype(dtype).astype(np.float64)
    return np.moveaxis((codes * scale).reshape(v.shape), -1, axis)


WIDE = False


def mx_kscale(k):
    if not WIDE:
        return np.ones(k)
    levels = np.array([10, -10, 5, -5, 0])
    if k % 512:
        return np.exp2(np.random.permutation(np.resize(levels, k // 32))).repeat(32)
    a = np.empty((k // 512, 16))
    for p in range(k // 512):
        a[p, :8] = np.random.permutation(np.resize(levels, 8))
        for g in range(8):
            far = levels[np.abs(levels - a[p, g]) >= 10]
            a[p, g + 8] = far[np.random.randint(len(far))]
    return np.exp2(a.ravel()).repeat(32)


def f64(x):
    return np.asarray(x).astype(np.float64)


def striped(idx):
    return np.tile(idx.reshape(-1, 16).T, (8, 1)).astype(np.uint16)


def unstriped(offs):
    return offs[:16].T.reshape(-1).astype(np.int64)


def relu2(v):
    return np.maximum(v, 0.0) ** 2


K, T, E, C, N = 1024, 1024, 8, 256, 256


def by_expert(wq, xq):
    return np.concatenate([wq[e].T @ xq[:, e * C:(e + 1) * C] for e in range(E)], axis=1)


def setup_inputs():
    n = np.random.standard_normal
    s = mx_kscale(K)[:, None]
    first = np.random.permutation(np.repeat(np.arange(E), T // E))
    second = (first + 1 + np.random.permutation(np.repeat(np.arange(E - 1), -(-T // (E - 1)))[:T])) % E
    while np.bincount(second, minlength=E).max() != T // E:
        load = np.bincount(second, minlength=E); hi, lo = int(load.argmax()), int(load.argmin())
        t = np.flatnonzero((second == hi) & (first != lo))[0]; second[t] = lo
    slot_token = np.empty(E * C, np.int64); pos = np.empty((2, T), np.int64); fill = np.zeros(E, np.int64)
    place = np.stack([np.random.permutation(C) for _ in range(E)])
    for r, deal in enumerate((first, second)):
        for t in np.random.permutation(T):
            e = deal[t]; j = e * C + place[e, fill[e]]; fill[e] += 1; slot_token[j] = t; pos[r, t] = j
    g = np.random.uniform(0.2, 0.8, T)
    return {
        "xT": (n((K, T)) * s).astype(np.float32),
        "w": (n((E + 1, K, N)) / np.sqrt(K) / s[None]).astype(np.float32),
        "b": (0.3 * n((N, E + 1))).astype(np.float32),
        "gate": np.stack([np.tile(g, (N, 1)), np.tile(1.0 - g, (N, 1))]).astype(np.float32),
        "offs": striped(slot_token),
        "pos1": striped(pos[0]),
        "pos2": striped(pos[1]),
    }


def reference(xT, w, b, gate, offs, pos1, pos2):
    idx = unstriped(offs)
    wq = mxq(f64(w), 1, "e4m3")
    xs = mxq(f64(xT), 0, "e4m3")
    ys = relu2((wq[E].T @ xs) + f64(b)[:, E:])
    xq = mxq(f64(xT)[:, idx], 0, "e4m3")
    y = by_expert(wq, xq)
    y = relu2(y + np.repeat(f64(b)[:, :E], C, axis=1))
    return ys + f64(gate[0]) * y[:, unstriped(pos1)] + f64(gate[1]) * y[:, unstriped(pos2)]

@@ -1,0 +1,321 @@
+from contextlib import ExitStack
+
+import concourse.mybir as mybir
+
+K, T, E, C, N = 1024, 1024, 8, 256, 256
+S = E * C
+P = 128
+FLOPS = 2 * K * N * (S + T)
+
+F32 = mybir.dt.float32
+BF16 = mybir.dt.bfloat16
+U32 = mybir.dt.uint32
+U16 = mybir.dt.uint16
+U8 = mybir.dt.uint8
+FP8X4 = mybir.dt.float8_e4m3fn_x4
+
+RELU = mybir.ActivationFunctionType.Relu
+SQUARE = mybir.ActivationFunctionType.Square
+MULT, ADD = mybir.AluOpType.mult, mybir.AluOpType.add
+
+CHUNKS = ((0, 3), (3, 3), (6, 2))
+HALF = 512
+RAW_BUFS = 8
+AHEAD = 6
+UNITS = ((0, 0, 1024), (1, 0, 640), (1, 640, 1024))
+
+
+def tile_moe_shr_lin_relu2_kernel(tc, xT, w, b, gate, offs, pos1, pos2, out):
+    nc = tc.nc
+    with ExitStack() as ctx:
+        lists = ctx.enter_context(tc.tile_pool(name="lists", bufs=1))
+        keep = ctx.enter_context(tc.tile_pool(name="keep", bufs=1))
+        stage = ctx.enter_context(tc.tile_pool(name="stage", bufs=RAW_BUFS))
+        group = ctx.enter_context(tc.tile_pool(name="group", bufs=1))
+        psum = ctx.enter_context(tc.psum_pool(name="psum", bufs=8))
+
+        offs_t = lists.tile([P, S // 16], U16, name="offs_t")
+        pos1_t = lists.tile([P, T // 16], U16, name="pos1_t")
+        pos2_t = lists.tile([P, T // 16], U16, name="pos2_t")
+        pos = (pos1_t, pos2_t)
+
+        bias = keep.tile([P, 2, E + 1], F32, name="bias")
+        plane0 = keep.tile([P, T], U32, name="plane0")
+        plane1 = keep.tile([P, T], U32, name="plane1")
+        planes23 = keep.tile([P, 2, T], U32, name="planes23")
+        planes = (plane0[:], plane1[:], planes23[:, 0, :], planes23[:, 1, :])
+        picked = [keep.tile([P, 4, n * C], U32, name=f"picked{i}") for i, (e0, n) in enumerate(CHUNKS)]
+        y = [keep.tile([P, S], F32, name=f"y{m}") for m in range(2)]
+        ys = [keep.tile([P, T], F32, name=f"ys{m}") for m in range(2)]
+        wcodes = [keep.tile([P, 4 * N], U32, name=f"wcodes{k}", align_bytes=64) for k in range(E // 2)]
+        wscales = [keep.tile([P, 4 * N], U8, name=f"wscales{k}", align_bytes=64) for k in range(E // 2)]
+        wcodes.append(keep.tile([P, 2 * N], U32, name="wcodes8", align_bytes=64))
+        wscales.append(keep.tile([P, 2 * N], U8, name="wscales8", align_bytes=64))
+        scodes = [keep.tile([P, T], U32, name=f"scodes{g}", align_bytes=64) for g in range(2)]
+        sscales = [keep.tile([P, T], U8, name=f"sscales{g}", align_bytes=64) for g in range(2)]
+
+        nc.sync.dma_start(offs_t[:], offs)
+        rows = [xT[HALF * g : HALF * (g + 1), :].rearrange("(p j) t -> p j t", j=4) for g in range(2)]
+        raw01 = []
+        for h in range(2):
+            t = stage.tile([P, 2048], F32, name="raw")
+            raw01.append(t[:].rearrange("p (j t) -> p j t", j=4))
+        for q in range(2):
+            for h in range(2):
+                cols = slice(h * HALF, (h + 1) * HALF)
+                nc.sync.dma_start(raw01[h][:, 2 * q : 2 * q + 2, :], rows[0][:, 2 * q : 2 * q + 2, cols])
+
+        ring = [("x", 2), ("x", 3)] + [("w", e) for e in range(E + 1)] + [("gate", 0), ("gate", 1)]
+        raw = {}
+
+        def load(unit):
+            kind, j = unit
+            t = stage.tile([P, 2048], F32, name="raw")
+            raw[unit] = t
+            if kind == "x":
+                nc.sync.dma_start(t[:].rearrange("p (j t) -> p j t", j=2), rows[1][:, 2 * j - 4 : 2 * j - 2, :])
+            elif kind == "w":
+                nc.sync.dma_start(
+                    t[:].rearrange("p (g j n) -> p g j n", g=2, j=4),
+                    w[j].rearrange("(g p j) n -> p g j n", p=P, j=4),
+                )
+            else:
+                nc.sync.dma_start(
+                    t[:].rearrange("p (r t) -> p r t", r=2),
+                    gate[:, j * P : (j + 1) * P, :].rearrange("r p t -> p r t"),
+                )
+            if unit == ("w", E):
+                nc.sync.dma_start(bias[:], b.rearrange("(m p) e -> p m e", p=P))
+            if unit == ("w", 2):
+                nc.sync.dma_start(pos1_t[:], pos1)
+                nc.sync.dma_start(pos2_t[:], pos2)
+
+        def load_ahead(unit):
+            for u in ring[: ring.index(unit) + AHEAD]:
+                if u not in raw:
+                    load(u)
+
+        def cast_plane(q):
+            dst = planes[q].bitcast(BF16).rearrange("p (t e) -> p t e", e=2)
+            if q < 2:
+                for h in range(2):
+                    half = dst[:, h * HALF : (h + 1) * HALF, :]
+                    src = raw01[h][:, 2 * q : 2 * q + 2, :].rearrange("p e t -> p t e")
+                    if q == 0:
+                        nc.vector.tensor_copy(half, src)
+                    else:
+                        nc.scalar.copy(half, src)
+            else:
+                load_ahead(("x", q))
+                nc.scalar.copy(dst, raw[("x", q)][:].rearrange("p (e t) -> p t e", e=2))
+
+        wbf = {}
+
+        def cast_w(e):
+            load_ahead(("w", e))
+            if e in (6, 7):
+                if e == 6:
+                    t = group.tile([P, 16 * N], BF16, name="tail", align_bytes=64)
+                    wbf[3] = t
+            elif e % 2 == 0:
+                t = group.tile([P, 16 * N], BF16, name="wbf", align_bytes=64, bufs=3)
+                wbf[e // 2] = t
+            for g in range(2):
+                src = raw[("w", e)][:, 4 * N * g : 4 * N * (g + 1)].rearrange("p (j c i) -> p c j i", j=4, i=4)
+                c0 = 8 * N * (e % 2) + 4 * N * g
+                dst = wbf[e // 2][:, c0 : c0 + 4 * N].rearrange("p (c i j) -> p c j i", i=4, j=4)
+                nc.scalar.copy(dst, src)
+
+        def quant_w(k):
+            n = 4 * N if k < E // 2 else 2 * N
+            nc.vector.quantize_mx(out=wcodes[k][:].bitcast(FP8X4), scales=wscales[k][:], in_=wbf[k][:, 0 : 4 * n])
+
+        def gather(q, chunks=(0, 1, 2)):
+            for i in chunks:
+                e0, n = CHUNKS[i]
+                nc.vector.tensor_copy(picked[i][:, q, :], planes[q].indirect(offs_t[:, 16 * e0 : 16 * (e0 + n)]))
+
+        xbf, xcodes, xscales = {}, {}, {}
+
+        def group_x(i, g):
+            n = CHUNKS[i][1] * C
+            if g == 0:
+                t = group.tile([P, 8 * n], BF16, name="xbf", align_bytes=64)
+                xbf[i] = t
+            src = picked[i][:, 2 * g : 2 * g + 2, :].bitcast(BF16).rearrange("p h (c e) -> p c h e", e=2)
+            nc.vector.tensor_copy(xbf[i][:, 4 * n * g : 4 * n * (g + 1)].rearrange("p (c h e) -> p c h e", h=2, e=2), src)
+
+        def quant_x(i):
+            n = CHUNKS[i][1] * C
+            xc = group.tile([P, 2 * n], U32, name="xc", align_bytes=64, bufs=2)
+            xs = group.tile([P, 2 * n], U8, name="xs", align_bytes=64, bufs=2)
+            xcodes[i], xscales[i] = xc, xs
+            for c0 in range(0, 2 * n, 1024):
+                c1 = min(c0 + 1024, 2 * n)
+                nc.vector.quantize_mx(out=xc[:, c0:c1].bitcast(FP8X4), scales=xs[:, c0:c1], in_=xbf[i][:, 4 * c0 : 4 * c1])
+
+        banks = {}
+
+        def multiply(k):
+            for e in (2 * k, 2 * k + 1):
+                ps = psum.tile([P, 2 * C], F32, name="ps")
+                banks[e] = ps
+            for m in range(2):
+                for e in (2 * k, 2 * k + 1):
+                    i = min(e // 3, 2)
+                    e0, n = CHUNKS[i]
+                    for g in range(2):
+                        w0 = 2 * N * (e % 2) + N * g + P * m
+                        x0 = C * (n * g + e - e0)
+                        nc.tensor.matmul_mx(
+                            out=banks[e][:, C * m : C * (m + 1)],
+                            lhsT=wcodes[k][:, w0 : w0 + P].bitcast(FP8X4),
+                            lhsT_scale=wscales[k][:, w0 : w0 + P],
+                            rhs=xcodes[i][:, x0 : x0 + C].bitcast(FP8X4),
+                            rhs_scale=xscales[i][:, x0 : x0 + C],
+                            start=(g == 0),
+                            stop=(g == 1),
+                        )
+
+        def relu(k, m):
+            for e in (2 * k, 2 * k + 1):
+                v = y[m][:, C * e : C * (e + 1)]
+                nc.scalar.activation(v, banks[e][:, C * m : C * (m + 1)], RELU, bias=bias[:, m, e : e + 1])
+
+        def square(k, m):
+            v = y[m][:, 2 * C * k : 2 * C * (k + 1)]
+            nc.scalar.activation(v, v, SQUARE)
+
+        sbf = {}
+
+        def group_s(g, h=0):
+            if g == 0:
+                t = group.tile([P, 4 * HALF], BF16, name="sbf", align_bytes=64, bufs=2)
+                src = raw01[h].rearrange("p j (c i) -> p c j i", i=4)
+                dst = t[:].rearrange("p (c i j) -> p c j i", i=4, j=4)
+                nc.scalar.copy(dst, src)
+            else:
+                t = group.tile([P, 4 * T], BF16, name="tail", align_bytes=64)
+                src = planes23[:].bitcast(BF16).rearrange("p q (c e) -> p c q e", e=2)
+                nc.vector.tensor_copy(t[:].rearrange("p (c q e) -> p c q e", q=2, e=2), src)
+            sbf[(g, h)] = t
+
+        def quant_s(g, h=0):
+            cols = slice(h * HALF, (h + 1) * HALF) if g == 0 else slice(0, T)
+            nc.vector.quantize_mx(out=scodes[g][:, cols].bitcast(FP8X4), scales=sscales[g][:, cols], in_=sbf[(g, h)][:])
+
+        def shared(m, h):
+            ps = psum.tile([P, HALF], F32, name="ps")
+            for g in range(2):
+                w0 = N * g + P * m
+                nc.tensor.matmul_mx(
+                    out=ps[:],
+                    lhsT=wcodes[E // 2][:, w0 : w0 + P].bitcast(FP8X4),
+                    lhsT_scale=wscales[E // 2][:, w0 : w0 + P],
+                    rhs=scodes[g][:, HALF * h : HALF * (h + 1)].bitcast(FP8X4),
+                    rhs_scale=sscales[g][:, HALF * h : HALF * (h + 1)],
+                    start=(g == 0),
+                    stop=(g == 1),
+                )
+            v = ys[m][:, HALF * h : HALF * (h + 1)]
+            nc.scalar.activation(v, ps[:], RELU, bias=bias[:, m, E : E + 1])
+
+        def square_shared(m, h):
+            v = ys[m][:, HALF * h : HALF * (h + 1)]
+            nc.scalar.activation(v, v, SQUARE)
+
+        part = {}
+
+        def fetch(u, r):
+            m, c0, c1 = UNITS[u]
+            if r == 0:
+                t = stage.tile([P, 2048], F32, name="raw")
+                part[u] = t[:].rearrange("p (r c) -> p r c", r=2)
+            weight = raw[("gate", m)][:, T * r + c0 : T * r + c1]
+            nc.vector.tensor_tensor(
+                part[u][:, r, 0 : c1 - c0], y[m][:].indirect(pos[r][:, c0 // 16 : c1 // 16]), weight, MULT
+            )
+
+        def add_parts(u):
+            m, c0, c1 = UNITS[u]
+            v = part[u][:, :, 0 : c1 - c0]
+            nc.vector.tensor_tensor(v[:, 0], v[:, 0], v[:, 1], ADD)
+
+        def finish(u):
+            m, c0, c1 = UNITS[u]
+            v = part[u][:, 0, 0 : c1 - c0]
+            nc.vector.tensor_tensor(v, v, ys[m][:, c0:c1], ADD)
+            nc.sync.dma_start(out[m * P : (m + 1) * P, c0:c1], v)
+
+        cast_plane(0)
+        cast_plane(1)
+        group_s(0, 0)
+        gather(0)
+        cast_plane(2)
+        cast_plane(3)
+        group_s(0, 1)
+        cast_w(0)
+        gather(1)
+        cast_w(1)
+        gather(2)
+        cast_w(2)
+        gather(3)
+        for e in range(3, E):
+            cast_w(e)
+        group_x(0, 0)
+        group_x(0, 1)
+        quant_s(0, 0)
+        quant_x(0)
+        group_x(1, 0)
+        quant_s(0, 1)
+        group_x(1, 1)
+        quant_w(0)
+        cast_w(E)
+        load_ahead(ring[-1])
+        quant_x(1)
+        multiply(0)
+        relu(0, 0)
+        quant_w(1)
+        multiply(1)
+        relu(1, 0)
+        square(0, 0)
+        quant_w(2)
+        multiply(2)
+        relu(2, 0)
+        square(1, 0)
+        square(2, 0)
+        group_x(2, 0)
+        group_x(2, 1)
+        quant_w(3)
+        quant_x(2)
+        multiply(3)
+        relu(3, 0)
+        square(3, 0)
+        relu(0, 1)
+        relu(1, 1)
+        square(0, 1)
+        relu(2, 1)
+        square(1, 1)
+        relu(3, 1)
+        square(2, 1)
+        square(3, 1)
+        group_s(1)
+        quant_w(4)
+        fetch(0, 0)
+        quant_s(1)
+        fetch(0, 1)
+        for m in range(2):
+            shared(m, 0)
+            shared(m, 1)
+            square_shared(m, 0)
+            square_shared(m, 1)
+        add_parts(0)
+        fetch(1, 0)
+        fetch(1, 1)
+        finish(0)
+        fetch(2, 0)
+        add_parts(1)
+        fetch(2, 1)
+        finish(1)
+        add_parts(2)
+        finish(2)

@@ -18,10 +18,9 @@ RELU = mybir.ActivationFunctionType.Relu
 SQUARE = mybir.ActivationFunctionType.Square
 MULT, ADD = mybir.AluOpType.mult, mybir.AluOpType.add
 
-CHUNKS = ((0, 3), (3, 3), (6, 2))
 HALF = 512
-RAW_BUFS = 8
-AHEAD = 6
+CHUNKS = ((0, 1024), (1024, 512), (1536, 512))
+RAW_BUFS = 7
 UNITS = ((0, 0, 1024), (1, 0, 640), (1, 640, 1024))
 
 
@@ -39,188 +38,198 @@ def tile_moe_shr_lin_relu2_kernel(tc, xT, w, b, gate, offs, pos1, pos2, out):
         pos2_t = lists.tile([P, T // 16], U16, name="pos2_t")
         pos = (pos1_t, pos2_t)
 
-        bias = keep.tile([P, 2, E + 1], F32, name="bias")
-        plane0 = keep.tile([P, T], U32, name="plane0")
-        plane1 = keep.tile([P, T], U32, name="plane1")
-        planes23 = keep.tile([P, 2, T], U32, name="planes23")
-        planes = (plane0[:], plane1[:], planes23[:, 0, :], planes23[:, 1, :])
-        picked = [keep.tile([P, 4, n * C], U32, name=f"picked{i}") for i, (e0, n) in enumerate(CHUNKS)]
-        y = [keep.tile([P, S], F32, name=f"y{m}") for m in range(2)]
-        ys = [keep.tile([P, T], F32, name=f"ys{m}") for m in range(2)]
-        wcodes = [keep.tile([P, 4 * N], U32, name=f"wcodes{k}", align_bytes=64) for k in range(E // 2)]
-        wscales = [keep.tile([P, 4 * N], U8, name=f"wscales{k}", align_bytes=64) for k in range(E // 2)]
-        wcodes.append(keep.tile([P, 2 * N], U32, name="wcodes8", align_bytes=64))
-        wscales.append(keep.tile([P, 2 * N], U8, name="wscales8", align_bytes=64))
-        scodes = [keep.tile([P, T], U32, name=f"scodes{g}", align_bytes=64) for g in range(2)]
+        planes = keep.tile([P, 4 * T], U32, name="planes")
+        y, ys = {}, {}
+        wcodes, wscales = {}, {}
+        for k in range(E // 2 + 1):
+            for m in range(2 if k < E // 2 else 1):
+                wcodes[k, m] = keep.tile([P, 4 * P], U32, name=f"wcodes{k}{m}", align_bytes=64)
+                wscales[k, m] = keep.tile([P, 4 * P], U8, name=f"wscales{k}{m}", align_bytes=64)
+        xcodes = [keep.tile([P, S], U32, name=f"xcodes{g}", align_bytes=64) for g in range(2)]
+        xscales = [keep.tile([P, S], U8, name=f"xscales{g}", align_bytes=64) for g in range(2)]
+        scodes = {}
         sscales = [keep.tile([P, T], U8, name=f"sscales{g}", align_bytes=64) for g in range(2)]
 
-        nc.sync.dma_start(offs_t[:], offs)
-        rows = [xT[HALF * g : HALF * (g + 1), :].rearrange("(p j) t -> p j t", j=4) for g in range(2)]
-        raw01 = []
-        for h in range(2):
-            t = stage.tile([P, 2048], F32, name="raw")
-            raw01.append(t[:].rearrange("p (j t) -> p j t", j=4))
-        for q in range(2):
-            for h in range(2):
-                cols = slice(h * HALF, (h + 1) * HALF)
-                nc.sync.dma_start(raw01[h][:, 2 * q : 2 * q + 2, :], rows[0][:, 2 * q : 2 * q + 2, cols])
-
-        ring = [("x", 2), ("x", 3)] + [("w", e) for e in range(E + 1)] + [("gate", 0), ("gate", 1)]
         raw = {}
 
-        def load(unit):
-            kind, j = unit
+        def rows(s):
+            g, h = divmod(s, 2)
+            return xT[HALF * g : HALF * (g + 1), :].rearrange("(p j) t -> p j t", j=4)[:, 2 * h : 2 * h + 2, :]
+
+        def load_half(s, h):
+            t = group.tile([P, 2, HALF], F32, name="quarter", align_bytes=64, bufs=7)
+            raw[s, h] = t
+            nc.sync.dma_start(t[:], rows(s)[:, :, h * HALF : (h + 1) * HALF])
+
+        def load_plane(s):
             t = stage.tile([P, 2048], F32, name="raw")
-            raw[unit] = t
-            if kind == "x":
-                nc.sync.dma_start(t[:].rearrange("p (j t) -> p j t", j=2), rows[1][:, 2 * j - 4 : 2 * j - 2, :])
-            elif kind == "w":
-                nc.sync.dma_start(
-                    t[:].rearrange("p (g j n) -> p g j n", g=2, j=4),
-                    w[j].rearrange("(g p j) n -> p g j n", p=P, j=4),
-                )
-            else:
-                nc.sync.dma_start(
-                    t[:].rearrange("p (r t) -> p r t", r=2),
-                    gate[:, j * P : (j + 1) * P, :].rearrange("r p t -> p r t"),
-                )
-            if unit == ("w", E):
-                nc.sync.dma_start(bias[:], b.rearrange("(m p) e -> p m e", p=P))
-            if unit == ("w", 2):
-                nc.sync.dma_start(pos1_t[:], pos1)
-                nc.sync.dma_start(pos2_t[:], pos2)
+            raw[s] = t
+            nc.sync.dma_start(t[:].rearrange("p (j t) -> p j t", j=2), rows(s))
 
-        def load_ahead(unit):
-            for u in ring[: ring.index(unit) + AHEAD]:
-                if u not in raw:
-                    load(u)
+        def load_w(e):
+            t = stage.tile([P, 2048], F32, name="raw")
+            raw["w", e] = t
+            nc.sync.dma_start(
+                t[:].rearrange("p (g j n) -> p g j n", g=2, j=4),
+                w[e].rearrange("(g p j) n -> p g j n", p=P, j=4),
+            )
 
-        def cast_plane(q):
-            dst = planes[q].bitcast(BF16).rearrange("p (t e) -> p t e", e=2)
-            if q < 2:
-                for h in range(2):
-                    half = dst[:, h * HALF : (h + 1) * HALF, :]
-                    src = raw01[h][:, 2 * q : 2 * q + 2, :].rearrange("p e t -> p t e")
-                    if q == 0:
-                        nc.vector.tensor_copy(half, src)
-                    else:
-                        nc.scalar.copy(half, src)
+        def load_gate():
+            t = stage.tile([P, 2048], F32, name="raw")
+            raw["gate"] = t
+            nc.sync.dma_start(t[:].rearrange("p (r t) -> p r t", r=2), gate[:, 0:P, :].rearrange("r p t -> p r t"))
+
+        def load_bias():
+            t = stage.tile([P, 2, E + 1], F32, name="raw")
+            raw["bias"] = t
+            nc.sync.dma_start(t[:], b.rearrange("(m p) e -> p m e", p=P))
+
+        def load_pos():
+            nc.sync.dma_start(pos1_t[:], pos1)
+            nc.sync.dma_start(pos2_t[:], pos2)
+
+        def copy_on(eng, dst, src):
+            if eng == "v":
+                nc.vector.tensor_copy(dst, src)
+            elif eng == "s":
+                nc.scalar.copy(dst, src)
             else:
-                load_ahead(("x", q))
-                nc.scalar.copy(dst, raw[("x", q)][:].rearrange("p (e t) -> p t e", e=2))
+                nc.gpsimd.tensor_scalar(dst, src, 1.0, 0.0, MULT, ADD)
+
+        def cast_half(s, h, eng):
+            dst = planes[:, s * T + h * HALF : s * T + (h + 1) * HALF].bitcast(BF16).rearrange("p (t e) -> p t e", e=2)
+            copy_on(eng, dst, raw[s, h][:].rearrange("p e t -> p t e"))
+
+        def cast_plane(s, eng):
+            dst = planes[:, s * T : (s + 1) * T].bitcast(BF16).rearrange("p (t e) -> p t e", e=2)
+            copy_on(eng, dst, raw[s][:].rearrange("p (e t) -> p t e", e=2))
 
         wbf = {}
 
-        def cast_w(e):
-            load_ahead(("w", e))
-            if e in (6, 7):
-                if e == 6:
-                    t = group.tile([P, 16 * N], BF16, name="tail", align_bytes=64)
-                    wbf[3] = t
-            elif e % 2 == 0:
-                t = group.tile([P, 16 * N], BF16, name="wbf", align_bytes=64, bufs=3)
-                wbf[e // 2] = t
-            for g in range(2):
-                src = raw[("w", e)][:, 4 * N * g : 4 * N * (g + 1)].rearrange("p (j c i) -> p c j i", j=4, i=4)
-                c0 = 8 * N * (e % 2) + 4 * N * g
-                dst = wbf[e // 2][:, c0 : c0 + 4 * N].rearrange("p (c i j) -> p c j i", i=4, j=4)
-                nc.scalar.copy(dst, src)
+        def cast_w(e, m, eng="s"):
+            key = (e // 2, m) if e < E else (E // 2, 0)
+            if key not in wbf and key in ((2, 0), (3, 0)):
+                wbf[key] = group.tile([P, 16 * P], BF16, name=f"late{key[0]}", align_bytes=64)
+            elif key not in wbf:
+                wbf[key] = group.tile([P, 16 * P], BF16, name="quarter", align_bytes=64, bufs=7)
+            c0 = 8 * P * (e % 2 if e < E else m)
+            src = raw["w", e][:].rearrange("p (g j m c i) -> p m g c j i", g=2, j=4, m=2, i=4)[:, m]
+            dst = wbf[key][:, c0 : c0 + 8 * P].rearrange("p (g c i j) -> p g c j i", g=2, i=4, j=4)
+            if eng == "s":
+                copy_on(eng, dst, src)
+            else:
+                for g in range(2):
+                    copy_on(eng, dst[:, g], src[:, g])
 
-        def quant_w(k):
-            n = 4 * N if k < E // 2 else 2 * N
-            nc.vector.quantize_mx(out=wcodes[k][:].bitcast(FP8X4), scales=wscales[k][:], in_=wbf[k][:, 0 : 4 * n])
+        def quant_w(k, m):
+            nc.vector.quantize_mx(out=wcodes[k, m][:].bitcast(FP8X4), scales=wscales[k, m][:], in_=wbf[k, m][:])
 
-        def gather(q, chunks=(0, 1, 2)):
-            for i in chunks:
-                e0, n = CHUNKS[i]
-                nc.vector.tensor_copy(picked[i][:, q, :], planes[q].indirect(offs_t[:, 16 * e0 : 16 * (e0 + n)]))
+        picked = {}
 
-        xbf, xcodes, xscales = {}, {}, {}
+        def gather(s, c0, n):
+            g, h = divmod(s, 2)
+            i = c0 // 1024
+            if (g, i) not in picked:
+                picked[g, i] = group.tile([P, 2048], U32, name="big", bufs=4)
+            window = planes[:, s * T : min(s + 2, 4) * T]
+            d0 = 1024 * h + c0 - 1024 * i
+            nc.vector.tensor_copy(picked[g, i][:, d0 : d0 + n], window.indirect(offs_t[:, c0 // 16 : (c0 + n) // 16]))
 
-        def group_x(i, g):
-            n = CHUNKS[i][1] * C
-            if g == 0:
-                t = group.tile([P, 8 * n], BF16, name="xbf", align_bytes=64)
-                xbf[i] = t
-            src = picked[i][:, 2 * g : 2 * g + 2, :].bitcast(BF16).rearrange("p h (c e) -> p c h e", e=2)
-            nc.vector.tensor_copy(xbf[i][:, 4 * n * g : 4 * n * (g + 1)].rearrange("p (c h e) -> p c h e", h=2, e=2), src)
+        xbf = {}
 
-        def quant_x(i):
-            n = CHUNKS[i][1] * C
-            xc = group.tile([P, 2 * n], U32, name="xc", align_bytes=64, bufs=2)
-            xs = group.tile([P, 2 * n], U8, name="xs", align_bytes=64, bufs=2)
-            xcodes[i], xscales[i] = xc, xs
-            for c0 in range(0, 2 * n, 1024):
-                c1 = min(c0 + 1024, 2 * n)
-                nc.vector.quantize_mx(out=xc[:, c0:c1].bitcast(FP8X4), scales=xs[:, c0:c1], in_=xbf[i][:, 4 * c0 : 4 * c1])
+        def regroup(g, c0, n, eng="v"):
+            if n == 512:
+                t = group.tile([P, 4 * n], BF16, name=f"late{c0 // 512}", align_bytes=64)
+            else:
+                t = group.tile([P, 4 * n], BF16, name="xbf", align_bytes=64, bufs=2)
+            xbf[g, c0] = t
+            i = c0 // 1024
+            both = picked[g, i][:].rearrange("p (h c) -> p h c", h=2)[:, :, c0 - 1024 * i : c0 - 1024 * i + n]
+            if eng == "v":
+                src = both.bitcast(BF16).rearrange("p h (c e) -> p c h e", e=2)
+                nc.vector.tensor_copy(t[:].rearrange("p (c h e) -> p c h e", h=2, e=2), src)
+            else:
+                nc.scalar.copy(t[:].bitcast(U32).rearrange("p (c h) -> p c h", h=2), both.rearrange("p h c -> p c h"))
+
+        def quant_x(g, c0, n):
+            cols = slice(c0, c0 + n)
+            nc.vector.quantize_mx(out=xcodes[g][:, cols].bitcast(FP8X4), scales=xscales[g][:, cols], in_=xbf[g, c0][:])
 
         banks = {}
 
-        def multiply(k):
-            for e in (2 * k, 2 * k + 1):
-                ps = psum.tile([P, 2 * C], F32, name="ps")
-                banks[e] = ps
-            for m in range(2):
-                for e in (2 * k, 2 * k + 1):
-                    i = min(e // 3, 2)
-                    e0, n = CHUNKS[i]
-                    for g in range(2):
-                        w0 = 2 * N * (e % 2) + N * g + P * m
-                        x0 = C * (n * g + e - e0)
-                        nc.tensor.matmul_mx(
-                            out=banks[e][:, C * m : C * (m + 1)],
-                            lhsT=wcodes[k][:, w0 : w0 + P].bitcast(FP8X4),
-                            lhsT_scale=wscales[k][:, w0 : w0 + P],
-                            rhs=xcodes[i][:, x0 : x0 + C].bitcast(FP8X4),
-                            rhs_scale=xscales[i][:, x0 : x0 + C],
-                            start=(g == 0),
-                            stop=(g == 1),
-                        )
+        def multiply(k, m):
+            ps = psum.tile([P, 2 * C], F32, name="ps")
+            banks[k, m] = ps
+            for e in range(2):
+                for g in (1, 0):
+                    w0 = 2 * P * e + P * g
+                    x0 = C * (2 * k + e)
+                    nc.tensor.matmul_mx(
+                        out=ps[:, C * e : C * (e + 1)],
+                        lhsT=wcodes[k, m][:, w0 : w0 + P].bitcast(FP8X4),
+                        lhsT_scale=wscales[k, m][:, w0 : w0 + P],
+                        rhs=xcodes[g][:, x0 : x0 + C].bitcast(FP8X4),
+                        rhs_scale=xscales[g][:, x0 : x0 + C],
+                        start=(g == 1),
+                        stop=(g == 0),
+                    )
 
         def relu(k, m):
-            for e in (2 * k, 2 * k + 1):
-                v = y[m][:, C * e : C * (e + 1)]
-                nc.scalar.activation(v, banks[e][:, C * m : C * (m + 1)], RELU, bias=bias[:, m, e : e + 1])
+            if m not in y:
+                y[m] = group.tile([P, S], F32, name=f"y{m}", align_bytes=64)
+            for e in range(2):
+                v = y[m][:, C * (2 * k + e) : C * (2 * k + e + 1)]
+                nc.scalar.activation(
+                    v, banks[k, m][:, C * e : C * (e + 1)], RELU, bias=raw["bias"][:, m, 2 * k + e : 2 * k + e + 1]
+                )
 
-        def square(k, m):
-            v = y[m][:, 2 * C * k : 2 * C * (k + 1)]
+        def square(k, m, n=1):
+            v = y[m][:, 2 * C * k : 2 * C * (k + n)]
             nc.scalar.activation(v, v, SQUARE)
 
         sbf = {}
 
-        def group_s(g, h=0):
-            if g == 0:
-                t = group.tile([P, 4 * HALF], BF16, name="sbf", align_bytes=64, bufs=2)
-                src = raw01[h].rearrange("p j (c i) -> p c j i", i=4)
-                dst = t[:].rearrange("p (c i j) -> p c j i", i=4, j=4)
-                nc.scalar.copy(dst, src)
+        def regroup_s(g, eng="s"):
+            t = group.tile([P, 4 * T], BF16, name=("ys", "y1")[g], align_bytes=64)
+            sbf[g] = t
+            both = planes[:, 2 * g * T : 2 * (g + 1) * T].rearrange("p (h c) -> p h c", h=2)
+            if eng == "v":
+                src = both.bitcast(BF16).rearrange("p h (c e) -> p c h e", e=2)
+                nc.vector.tensor_copy(t[:].rearrange("p (c h e) -> p c h e", h=2, e=2), src)
             else:
-                t = group.tile([P, 4 * T], BF16, name="tail", align_bytes=64)
-                src = planes23[:].bitcast(BF16).rearrange("p q (c e) -> p c q e", e=2)
-                nc.vector.tensor_copy(t[:].rearrange("p (c q e) -> p c q e", q=2, e=2), src)
-            sbf[(g, h)] = t
+                nc.scalar.copy(t[:].bitcast(U32).rearrange("p (c h) -> p c h", h=2), both.rearrange("p h c -> p c h"))
 
-        def quant_s(g, h=0):
-            cols = slice(h * HALF, (h + 1) * HALF) if g == 0 else slice(0, T)
-            nc.vector.quantize_mx(out=scodes[g][:, cols].bitcast(FP8X4), scales=sscales[g][:, cols], in_=sbf[(g, h)][:])
+        def quant_s(g):
+            if g not in scodes:
+                t = group.tile([P, 2 * T], U32, name="late3", align_bytes=64)
+                scodes[0], scodes[1] = t[:, 0:T], t[:, T : 2 * T]
+            nc.vector.quantize_mx(out=scodes[g].bitcast(FP8X4), scales=sscales[g][:], in_=sbf[g][:])
 
-        def shared(m, h):
+        sbanks = {}
+
+        def multiply_s(m, h):
             ps = psum.tile([P, HALF], F32, name="ps")
-            for g in range(2):
-                w0 = N * g + P * m
+            sbanks[m, h] = ps
+            for g in (1, 0):
+                w0 = 2 * P * m + P * g
                 nc.tensor.matmul_mx(
                     out=ps[:],
-                    lhsT=wcodes[E // 2][:, w0 : w0 + P].bitcast(FP8X4),
-                    lhsT_scale=wscales[E // 2][:, w0 : w0 + P],
+                    lhsT=wcodes[E // 2, 0][:, w0 : w0 + P].bitcast(FP8X4),
+                    lhsT_scale=wscales[E // 2, 0][:, w0 : w0 + P],
                     rhs=scodes[g][:, HALF * h : HALF * (h + 1)].bitcast(FP8X4),
                     rhs_scale=sscales[g][:, HALF * h : HALF * (h + 1)],
-                    start=(g == 0),
-                    stop=(g == 1),
+                    start=(g == 1),
+                    stop=(g == 0),
                 )
-            v = ys[m][:, HALF * h : HALF * (h + 1)]
-            nc.scalar.activation(v, ps[:], RELU, bias=bias[:, m, E : E + 1])
 
-        def square_shared(m, h):
+        def relu_s(m, h):
+            if m not in ys:
+                t = group.tile([P, 2 * T], F32, name="ys", align_bytes=64)
+                ys[0], ys[1] = t[:, 0:T], t[:, T : 2 * T]
+            v = ys[m][:, HALF * h : HALF * (h + 1)]
+            nc.scalar.activation(v, sbanks[m, h][:], RELU, bias=raw["bias"][:, m, E : E + 1])
+
+        def square_s(m, h):
             v = ys[m][:, HALF * h : HALF * (h + 1)]
             nc.scalar.activation(v, v, SQUARE)
 
@@ -228,10 +237,10 @@ def tile_moe_shr_lin_relu2_kernel(tc, xT, w, b, gate, offs, pos1, pos2, out):
 
         def fetch(u, r):
             m, c0, c1 = UNITS[u]
-            if r == 0:
-                t = stage.tile([P, 2048], F32, name="raw")
-                part[u] = t[:].rearrange("p (r c) -> p r c", r=2)
-            weight = raw[("gate", m)][:, T * r + c0 : T * r + c1]
+            if u not in part:
+                t = group.tile([P, 2048], U32, name="big", bufs=4)
+                part[u] = t[:].bitcast(F32).rearrange("p (r c) -> p r c", r=2)
+            weight = raw["gate"][:, T * r + c0 : T * r + c1]
             nc.vector.tensor_tensor(
                 part[u][:, r, 0 : c1 - c0], y[m][:].indirect(pos[r][:, c0 // 16 : c1 // 16]), weight, MULT
             )
@@ -241,81 +250,112 @@ def tile_moe_shr_lin_relu2_kernel(tc, xT, w, b, gate, offs, pos1, pos2, out):
             v = part[u][:, :, 0 : c1 - c0]
             nc.vector.tensor_tensor(v[:, 0], v[:, 0], v[:, 1], ADD)
 
-        def finish(u):
+        def add_shared(u):
             m, c0, c1 = UNITS[u]
             v = part[u][:, 0, 0 : c1 - c0]
             nc.vector.tensor_tensor(v, v, ys[m][:, c0:c1], ADD)
-            nc.sync.dma_start(out[m * P : (m + 1) * P, c0:c1], v)
 
-        cast_plane(0)
-        cast_plane(1)
-        group_s(0, 0)
-        gather(0)
-        cast_plane(2)
-        cast_plane(3)
-        group_s(0, 1)
-        cast_w(0)
-        gather(1)
-        cast_w(1)
-        gather(2)
-        cast_w(2)
-        gather(3)
+        def store(u):
+            m, c0, c1 = UNITS[u]
+            nc.sync.dma_start(out[m * P : (m + 1) * P, c0:c1], part[u][:, 0, 0 : c1 - c0])
+
+        load_half(3, 0)
+        load_half(3, 1)
+        nc.sync.dma_start(offs_t[:], offs)
+        load_half(2, 0)
+        load_half(2, 1)
+        load_w(0)
+        load_plane(1)
+        load_w(1)
+        load_plane(0)
+        load_w(2)
+        load_pos()
         for e in range(3, E):
-            cast_w(e)
-        group_x(0, 0)
-        group_x(0, 1)
-        quant_s(0, 0)
-        quant_x(0)
-        group_x(1, 0)
-        quant_s(0, 1)
-        group_x(1, 1)
-        quant_w(0)
-        cast_w(E)
-        load_ahead(ring[-1])
-        quant_x(1)
-        multiply(0)
+            load_w(e)
+        load_bias()
+        load_w(E)
+        load_gate()
+
+        cast_half(3, 0, "v")
+        cast_half(3, 1, "v")
+        cast_half(2, 0, "s")
+        cast_half(2, 1, "s")
+        cast_plane(1, "s")
+        cast_plane(0, "s")
+        for e in range(E):
+            cast_w(e, 0)
+            if e % 2 == 1:
+                quant_w(e // 2, 0)
+        for c0 in range(0, S, 512):
+            gather(3, c0, 512)
+        for c0 in range(0, S, 1024):
+            gather(2, c0, 1024)
+        for c0 in range(0, S, 1024):
+            regroup(1, c0, 1024)
+        for c0 in range(0, S, 1024):
+            quant_x(1, c0, 1024)
+        for c0 in range(0, S, 1024):
+            gather(1, c0, 1024)
+        gather(0, 0, 1024)
+        gather(0, 1024, 512)
+        regroup(0, 0, 1024)
+        gather(0, 1536, 512)
+        quant_x(0, 0, 1024)
+        regroup(0, 1024, 512)
+        quant_x(0, 1024, 512)
+        regroup(0, 1536, 512)
+        quant_x(0, 1536, 512)
+        for k in range(4):
+            multiply(k, 0)
+        for e in range(E):
+            cast_w(e, 1)
+            if e % 2 == 1:
+                quant_w(e // 2, 1)
+        regroup_s(1)
+        quant_s(1)
+        for k in range(4):
+            multiply(k, 1)
+
         relu(0, 0)
-        quant_w(1)
-        multiply(1)
         relu(1, 0)
-        square(0, 0)
-        quant_w(2)
-        multiply(2)
+        square(0, 0, 2)
+        cast_w(E, 0)
+        cast_w(E, 1)
+        quant_w(4, 0)
         relu(2, 0)
-        square(1, 0)
         square(2, 0)
-        group_x(2, 0)
-        group_x(2, 1)
-        quant_w(3)
-        quant_x(2)
-        multiply(3)
         relu(3, 0)
         square(3, 0)
-        relu(0, 1)
-        relu(1, 1)
-        square(0, 1)
-        relu(2, 1)
-        square(1, 1)
-        relu(3, 1)
-        square(2, 1)
-        square(3, 1)
-        group_s(1)
-        quant_w(4)
+        regroup_s(0)
+        quant_s(0)
+        for k in range(4):
+            relu(k, 1)
+        square(0, 1, 2)
+        square(2, 1, 2)
+        multiply_s(0, 0)
+        multiply_s(0, 1)
+        multiply_s(1, 0)
+        multiply_s(1, 1)
+        relu_s(0, 0)
+        relu_s(0, 1)
+        square_s(0, 0)
+        square_s(0, 1)
+        relu_s(1, 0)
+        relu_s(1, 1)
+        square_s(1, 0)
+        square_s(1, 1)
         fetch(0, 0)
-        quant_s(1)
         fetch(0, 1)
-        for m in range(2):
-            shared(m, 0)
-            shared(m, 1)
-            square_shared(m, 0)
-            square_shared(m, 1)
         add_parts(0)
         fetch(1, 0)
+        add_shared(0)
+        store(0)
         fetch(1, 1)
-        finish(0)
         fetch(2, 0)
         add_parts(1)
         fetch(2, 1)
-        finish(1)
+        add_shared(1)
+        store(1)
         add_parts(2)
-        finish(2)
+        add_shared(2)
+        store(2)

@@ -1,6 +1,7 @@
 from contextlib import ExitStack
 
 import concourse.mybir as mybir
+from concourse.masks import make_identity
 
 K, T, E, C, N = 1024, 1024, 8, 256, 256
 S = E * C
@@ -21,7 +22,7 @@ MULT, ADD = mybir.AluOpType.mult, mybir.AluOpType.add
 HALF = 512
 CHUNKS = ((0, 1024), (1024, 512), (1536, 512))
 RAW_BUFS = 7
-UNITS = ((0, 0, 1024), (1, 0, 640), (1, 640, 1024))
+UNITS = ((0, 0, 1024),)
 
 
 def tile_moe_shr_lin_relu2_kernel(tc, xT, w, b, gate, offs, pos1, pos2, out):
@@ -50,6 +51,8 @@ def tile_moe_shr_lin_relu2_kernel(tc, xT, w, b, gate, offs, pos1, pos2, out):
         scodes = {}
         sscales = [keep.tile([P, T], U8, name=f"sscales{g}", align_bytes=64) for g in range(2)]
 
+        ident = keep.tile([P, P], F32, name="ident")
+        make_identity(nc, ident[:])
         raw = {}
 
         def rows(s):
@@ -255,6 +258,47 @@ def tile_moe_shr_lin_relu2_kernel(tc, xT, w, b, gate, offs, pos1, pos2, out):
             v = part[u][:, 0, 0 : c1 - c0]
             nc.vector.tensor_tensor(v, v, ys[m][:, c0:c1], ADD)
 
+        turned = {}
+
+        def sum_turned(u, c0):
+            m, u0, u1 = UNITS[u]
+            ps = psum.tile([P, HALF], F32, name="ps")
+            turned[u, c0] = ps
+            n = min(HALF, u1 - c0)
+            for j in range(0, n, P):
+                a = c0 - u0 + j
+                terms = (part[u][:, 0, a : a + P], part[u][:, 1, a : a + P], ys[m][:, c0 + j : c0 + j + P])
+                for i, term in enumerate(terms):
+                    nc.tensor.matmul(ps[:, j : j + P], term, ident[:], start=(i == 0), stop=(i == 2), is_transpose=True)
+
+        def copy_turned(u, c0):
+            m, u0, u1 = UNITS[u]
+            n = min(HALF, u1 - c0)
+            nc.scalar.copy(part[u][:, 1, c0 - u0 : c0 - u0 + n], turned[u, c0][:, 0:n])
+
+        def turn_back(u, c0):
+            m, u0, u1 = UNITS[u]
+            n = min(HALF, u1 - c0)
+            ps = psum.tile([P, HALF], F32, name="ps")
+            turned[u, c0] = ps
+            for j in range(0, n, P):
+                a = c0 - u0 + j
+                nc.tensor.transpose(ps[:, j : j + P], part[u][:, 1, a : a + P], ident[:])
+
+        def store_turned(u, c0):
+            m, u0, u1 = UNITS[u]
+            n = min(HALF, u1 - c0)
+            v = part[u][:, 0, c0 - u0 : c0 - u0 + n]
+            nc.scalar.copy(v, turned[u, c0][:, 0:n])
+            nc.sync.dma_start(out[m * P : (m + 1) * P, c0 : c0 + n], v)
+
+        def fetch_into(dst, m, r, c0, c1):
+            weight = raw["gate"][:, T * r + c0 : T * r + c1]
+            nc.vector.tensor_tensor(dst, y[m][:].indirect(pos[r][:, c0 // 16 : c1 // 16]), weight, MULT)
+
+        def add_into(dst, other):
+            nc.vector.tensor_tensor(dst, dst, other, ADD)
+
         def store(u):
             m, c0, c1 = UNITS[u]
             nc.sync.dma_start(out[m * P : (m + 1) * P, c0:c1], part[u][:, 0, 0 : c1 - c0])
@@ -332,30 +376,37 @@ def tile_moe_shr_lin_relu2_kernel(tc, xT, w, b, gate, offs, pos1, pos2, out):
             relu(k, 1)
         square(0, 1, 2)
         square(2, 1, 2)
-        multiply_s(0, 0)
-        multiply_s(0, 1)
-        multiply_s(1, 0)
-        multiply_s(1, 1)
-        relu_s(0, 0)
-        relu_s(0, 1)
-        square_s(0, 0)
-        square_s(0, 1)
+        for m, h in ((1, 0), (0, 0), (0, 1), (1, 1)):
+            multiply_s(m, h)
         relu_s(1, 0)
-        relu_s(1, 1)
+        relu_s(0, 0)
         square_s(1, 0)
-        square_s(1, 1)
+        square_s(0, 0)
+        relu_s(0, 1)
+        square_s(0, 1)
+
         fetch(0, 0)
         fetch(0, 1)
-        add_parts(0)
-        fetch(1, 0)
-        add_shared(0)
-        store(0)
-        fetch(1, 1)
-        fetch(2, 0)
-        add_parts(1)
-        fetch(2, 1)
-        add_shared(1)
-        store(1)
-        add_parts(2)
-        add_shared(2)
-        store(2)
+        sum_turned(0, 0)
+        sum_turned(0, 512)
+        copy_turned(0, 0)
+        relu_s(1, 1)
+        square_s(1, 1)
+        copy_turned(0, 512)
+        turn_back(0, 0)
+        turn_back(0, 512)
+        last = group.tile([P, 2048], U32, name="big", bufs=4)
+        a1, b1, b2 = (last[:, HALF * i : HALF * (i + 1)].bitcast(F32) for i in range(3))
+        a2 = ys[1][:, 0:HALF]
+        fetch_into(a1, 1, 0, 0, HALF)
+        fetch_into(b1, 1, 1, 0, HALF)
+        add_into(a1, ys[1][:, 0:HALF])
+        fetch_into(a2, 1, 0, HALF, T)
+        add_into(a1, b1)
+        nc.sync.dma_start(out[P : 2 * P, 0:HALF], a1)
+        add_into(a2, ys[1][:, HALF:T])
+        fetch_into(b2, 1, 1, HALF, T)
+        store_turned(0, 0)
+        store_turned(0, 512)
+        add_into(a2, b2)
+        nc.sync.dma_start(out[P : 2 * P, HALF:T], a2)

@@ -21,8 +21,8 @@ MULT, ADD = mybir.AluOpType.mult, mybir.AluOpType.add
 
 HALF = 512
 CHUNKS = ((0, 1024), (1024, 512), (1536, 512))
-RAW_BUFS = 7
-UNITS = ((0, 0, 1024),)
+RAW_BUFS = 6
+UNITS = ((0, 0, 512), (0, 512, 1024))
 
 
 def tile_moe_shr_lin_relu2_kernel(tc, xT, w, b, gate, offs, pos1, pos2, out):
@@ -44,7 +44,8 @@ def tile_moe_shr_lin_relu2_kernel(tc, xT, w, b, gate, offs, pos1, pos2, out):
         wcodes, wscales = {}, {}
         for k in range(E // 2 + 1):
             for m in range(2 if k < E // 2 else 1):
-                wcodes[k, m] = keep.tile([P, 4 * P], U32, name=f"wcodes{k}{m}", align_bytes=64)
+                if m == 0 or k < 2:
+                    wcodes[k, m] = keep.tile([P, 4 * P], U32, name=f"wcodes{k}{m}", align_bytes=64)
                 wscales[k, m] = keep.tile([P, 4 * P], U8, name=f"wscales{k}{m}", align_bytes=64)
         xcodes = [keep.tile([P, S], U32, name=f"xcodes{g}", align_bytes=64) for g in range(2)]
         xscales = [keep.tile([P, S], U8, name=f"xscales{g}", align_bytes=64) for g in range(2)]
@@ -65,7 +66,7 @@ def tile_moe_shr_lin_relu2_kernel(tc, xT, w, b, gate, offs, pos1, pos2, out):
             nc.sync.dma_start(t[:], rows(s)[:, :, h * HALF : (h + 1) * HALF])
 
         def load_plane(s):
-            t = stage.tile([P, 2048], F32, name="raw")
+            t = group.tile([P, 2048], F32, name=f"plane{s}", align_bytes=64)
             raw[s] = t
             nc.sync.dma_start(t[:].rearrange("p (j t) -> p j t", j=2), rows(s))
 
@@ -116,16 +117,24 @@ def tile_moe_shr_lin_relu2_kernel(tc, xT, w, b, gate, offs, pos1, pos2, out):
             elif key not in wbf:
                 wbf[key] = group.tile([P, 16 * P], BF16, name="quarter", align_bytes=64, bufs=7)
             c0 = 8 * P * (e % 2 if e < E else m)
-            src = raw["w", e][:].rearrange("p (g j m c i) -> p m g c j i", g=2, j=4, m=2, i=4)[:, m]
-            dst = wbf[key][:, c0 : c0 + 8 * P].rearrange("p (g c i j) -> p g c j i", g=2, i=4, j=4)
+            src = raw["w", e][:].rearrange("p (g j m c i) -> p m g c j i", g=2, j=4, m=2, i=2)[:, m]
+            dst = wbf[key][:, c0 : c0 + 8 * P].rearrange("p (g c i j) -> p g c j i", g=2, i=2, j=4)
             if eng == "s":
                 copy_on(eng, dst, src)
             else:
-                for g in range(2):
-                    copy_on(eng, dst[:, g], src[:, g])
+                rows4 = raw["w", e][:].rearrange("p (g j m c) -> p m g c j", g=2, j=4, m=2)[:, m]
+                copy_on(eng, wbf[key][:, c0 : c0 + 8 * P].rearrange("p (g c j) -> p g c j", g=2, j=4), rows4)
+
+        def late_codes():
+            t = group.tile([P, 2 * T + 8 * P], U32, name="late3", align_bytes=64)
+            scodes[0], scodes[1] = t[:, 0:T], t[:, T : 2 * T]
+            for k in range(2):
+                wcodes[2 + k, 1] = t[:, 2 * T + 4 * P * k : 2 * T + 4 * P * (k + 1)]
 
         def quant_w(k, m):
-            nc.vector.quantize_mx(out=wcodes[k, m][:].bitcast(FP8X4), scales=wscales[k, m][:], in_=wbf[k, m][:])
+            if (k, m) not in wcodes:
+                late_codes()
+            nc.vector.quantize_mx(out=wcodes[k, m][:, 0 : 4 * P].bitcast(FP8X4), scales=wscales[k, m][:], in_=wbf[k, m][:])
 
         picked = {}
 
@@ -143,8 +152,10 @@ def tile_moe_shr_lin_relu2_kernel(tc, xT, w, b, gate, offs, pos1, pos2, out):
         def regroup(g, c0, n, eng="v"):
             if n == 512:
                 t = group.tile([P, 4 * n], BF16, name=f"late{c0 // 512}", align_bytes=64)
+            elif g == 1:
+                t = group.tile([P, 4 * n], BF16, name=f"plane{1 - c0 // 1024}", align_bytes=64)
             else:
-                t = group.tile([P, 4 * n], BF16, name="xbf", align_bytes=64, bufs=2)
+                t = group.tile([P, 4 * n], BF16, name="xbf", align_bytes=64)
             xbf[g, c0] = t
             i = c0 // 1024
             both = picked[g, i][:].rearrange("p (h c) -> p h c", h=2)[:, :, c0 - 1024 * i : c0 - 1024 * i + n]
@@ -193,7 +204,7 @@ def tile_moe_shr_lin_relu2_kernel(tc, xT, w, b, gate, offs, pos1, pos2, out):
         sbf = {}
 
         def regroup_s(g, eng="s"):
-            t = group.tile([P, 4 * T], BF16, name=("ys", "y1")[g], align_bytes=64)
+            t = group.tile([P, 4 * T], BF16, name=("ys", "sbf1")[g], align_bytes=64)
             sbf[g] = t
             both = planes[:, 2 * g * T : 2 * (g + 1) * T].rearrange("p (h c) -> p h c", h=2)
             if eng == "v":
@@ -203,9 +214,6 @@ def tile_moe_shr_lin_relu2_kernel(tc, xT, w, b, gate, offs, pos1, pos2, out):
                 nc.scalar.copy(t[:].bitcast(U32).rearrange("p (c h) -> p c h", h=2), both.rearrange("p h c -> p c h"))
 
         def quant_s(g):
-            if g not in scodes:
-                t = group.tile([P, 2 * T], U32, name="late3", align_bytes=64)
-                scodes[0], scodes[1] = t[:, 0:T], t[:, T : 2 * T]
             nc.vector.quantize_mx(out=scodes[g].bitcast(FP8X4), scales=sscales[g][:], in_=sbf[g][:])
 
         sbanks = {}
@@ -313,12 +321,12 @@ def tile_moe_shr_lin_relu2_kernel(tc, xT, w, b, gate, offs, pos1, pos2, out):
         load_w(1)
         load_plane(0)
         load_w(2)
-        load_pos()
         for e in range(3, E):
             load_w(e)
-        load_bias()
         load_w(E)
+        load_bias()
         load_gate()
+        load_pos()
 
         cast_half(3, 0, "v")
         cast_half(3, 1, "v")
@@ -334,16 +342,16 @@ def tile_moe_shr_lin_relu2_kernel(tc, xT, w, b, gate, offs, pos1, pos2, out):
             gather(3, c0, 512)
         for c0 in range(0, S, 1024):
             gather(2, c0, 1024)
-        for c0 in range(0, S, 1024):
-            regroup(1, c0, 1024)
-        for c0 in range(0, S, 1024):
-            quant_x(1, c0, 1024)
+        regroup(1, 0, 1024)
+        regroup(1, 1024, 1024)
         for c0 in range(0, S, 1024):
             gather(1, c0, 1024)
         gather(0, 0, 1024)
         gather(0, 1024, 512)
         regroup(0, 0, 1024)
         gather(0, 1536, 512)
+        quant_x(1, 0, 1024)
+        quant_x(1, 1024, 1024)
         quant_x(0, 0, 1024)
         regroup(0, 1024, 512)
         quant_x(0, 1024, 512)
@@ -360,41 +368,42 @@ def tile_moe_shr_lin_relu2_kernel(tc, xT, w, b, gate, offs, pos1, pos2, out):
         for k in range(4):
             multiply(k, 1)
 
-        relu(0, 0)
-        relu(1, 0)
-        square(0, 0, 2)
+        regroup_s(0, "v")
         cast_w(E, 0)
         cast_w(E, 1)
         quant_w(4, 0)
-        relu(2, 0)
-        square(2, 0)
-        relu(3, 0)
-        square(3, 0)
-        regroup_s(0)
         quant_s(0)
+        relu(0, 0)
+        relu(1, 0)
+        relu(2, 0)
+        square(0, 0, 2)
+        relu(3, 0)
+        square(2, 0)
+        square(3, 0)
         for k in range(4):
             relu(k, 1)
         square(0, 1, 2)
         square(2, 1, 2)
-        for m, h in ((1, 0), (0, 0), (0, 1), (1, 1)):
+        for m, h in ((0, 0), (0, 1), (1, 0), (1, 1)):
             multiply_s(m, h)
-        relu_s(1, 0)
         relu_s(0, 0)
-        square_s(1, 0)
-        square_s(0, 0)
         relu_s(0, 1)
+        square_s(0, 0)
+        relu_s(1, 0)
         square_s(0, 1)
+        square_s(1, 0)
 
-        fetch(0, 0)
-        fetch(0, 1)
+        for u in range(2):
+            fetch(u, 0)
+            fetch(u, 1)
         sum_turned(0, 0)
-        sum_turned(0, 512)
+        sum_turned(1, 512)
         copy_turned(0, 0)
-        relu_s(1, 1)
-        square_s(1, 1)
-        copy_turned(0, 512)
         turn_back(0, 0)
-        turn_back(0, 512)
+        relu_s(1, 1)
+        copy_turned(1, 512)
+        turn_back(1, 512)
+        square_s(1, 1)
         last = group.tile([P, 2048], U32, name="big", bufs=4)
         a1, b1, b2 = (last[:, HALF * i : HALF * (i + 1)].bitcast(F32) for i in range(3))
         a2 = ys[1][:, 0:HALF]
@@ -407,6 +416,6 @@ def tile_moe_shr_lin_relu2_kernel(tc, xT, w, b, gate, offs, pos1, pos2, out):
         add_into(a2, ys[1][:, HALF:T])
         fetch_into(b2, 1, 1, HALF, T)
         store_turned(0, 0)
-        store_turned(0, 512)
+        store_turned(1, 512)
         add_into(a2, b2)
         nc.sync.dma_start(out[P : 2 * P, HALF:T], a2)

@@ -44,10 +44,10 @@ def tile_moe_shr_lin_relu2_kernel(tc, xT, w, b, gate, offs, pos1, pos2, out):
         wcodes, wscales = {}, {}
         for k in range(E // 2 + 1):
             for m in range(2 if k < E // 2 else 1):
-                if m == 0 or k < 2:
+                if k > 0 and (m == 0 or k < 2):
                     wcodes[k, m] = keep.tile([P, 4 * P], U32, name=f"wcodes{k}{m}", align_bytes=64)
                 wscales[k, m] = keep.tile([P, 4 * P], U8, name=f"wscales{k}{m}", align_bytes=64)
-        xcodes = [keep.tile([P, S], U32, name=f"xcodes{g}", align_bytes=64) for g in range(2)]
+        xcodes = {0: keep.tile([P, S], U32, name="xcodes0", align_bytes=64)}
         xscales = [keep.tile([P, S], U8, name=f"xscales{g}", align_bytes=64) for g in range(2)]
         scodes = {}
         sscales = [keep.tile([P, T], U8, name=f"sscales{g}", align_bytes=64) for g in range(2)]
@@ -64,6 +64,15 @@ def tile_moe_shr_lin_relu2_kernel(tc, xT, w, b, gate, offs, pos1, pos2, out):
             t = group.tile([P, 2, HALF], F32, name="quarter", align_bytes=64, bufs=7)
             raw[s, h] = t
             nc.sync.dma_start(t[:], rows(s)[:, :, h * HALF : (h + 1) * HALF])
+
+        def load_piece(s, c0, c1):
+            t = group.tile([P, 2, c1 - c0], F32, name=f"piece{c0}", align_bytes=64)
+            raw[s, c0] = t
+            nc.sync.dma_start(t[:], rows(s)[:, :, c0:c1])
+
+        def cast_piece(s, c0, c1, eng):
+            dst = planes[:, s * T + c0 : s * T + c1].bitcast(BF16).rearrange("p (t e) -> p t e", e=2)
+            copy_on(eng, dst, raw[s, c0][:].rearrange("p e t -> p t e"))
 
         def load_plane(s):
             t = group.tile([P, 2048], F32, name=f"plane{s}", align_bytes=64)
@@ -125,6 +134,12 @@ def tile_moe_shr_lin_relu2_kernel(tc, xT, w, b, gate, offs, pos1, pos2, out):
                 rows4 = raw["w", e][:].rearrange("p (g j m c) -> p m g c j", g=2, j=4, m=2)[:, m]
                 copy_on(eng, wbf[key][:, c0 : c0 + 8 * P].rearrange("p (g c j) -> p g c j", g=2, j=4), rows4)
 
+        def held_codes():
+            t = group.tile([P, S + 8 * P], U32, name="piece768", align_bytes=64)
+            xcodes[1] = t[:, 0:S]
+            for m in range(2):
+                wcodes[0, m] = t[:, S + 4 * P * m : S + 4 * P * (m + 1)]
+
         def late_codes():
             t = group.tile([P, 2 * T + 8 * P], U32, name="late3", align_bytes=64)
             scodes[0], scodes[1] = t[:, 0:T], t[:, T : 2 * T]
@@ -153,7 +168,7 @@ def tile_moe_shr_lin_relu2_kernel(tc, xT, w, b, gate, offs, pos1, pos2, out):
             if n == 512:
                 t = group.tile([P, 4 * n], BF16, name=f"late{c0 // 512}", align_bytes=64)
             elif g == 1:
-                t = group.tile([P, 4 * n], BF16, name=f"plane{1 - c0 // 1024}", align_bytes=64)
+                t = group.tile([P, 4 * n], BF16, name="plane1" if c0 == 0 else "piece0", align_bytes=64)
             else:
                 t = group.tile([P, 4 * n], BF16, name="xbf", align_bytes=64)
             xbf[g, c0] = t
@@ -163,11 +178,14 @@ def tile_moe_shr_lin_relu2_kernel(tc, xT, w, b, gate, offs, pos1, pos2, out):
                 src = both.bitcast(BF16).rearrange("p h (c e) -> p c h e", e=2)
                 nc.vector.tensor_copy(t[:].rearrange("p (c h e) -> p c h e", h=2, e=2), src)
             else:
-                nc.scalar.copy(t[:].bitcast(U32).rearrange("p (c h) -> p c h", h=2), both.rearrange("p h c -> p c h"))
+                nc.scalar.copy(
+                    t[:, :].bitcast(U32).rearrange("p (c i h) -> p c h i", i=2, h=2),
+                    both.rearrange("p h (c i) -> p c h i", i=2),
+                )
 
         def quant_x(g, c0, n):
             cols = slice(c0, c0 + n)
-            nc.vector.quantize_mx(out=xcodes[g][:, cols].bitcast(FP8X4), scales=xscales[g][:, cols], in_=xbf[g, c0][:])
+            nc.vector.quantize_mx(out=xcodes[g][:, cols].bitcast(FP8X4), scales=xscales[g][:, cols], in_=xbf[g, c0][:, :])
 
         banks = {}
 
@@ -211,7 +229,10 @@ def tile_moe_shr_lin_relu2_kernel(tc, xT, w, b, gate, offs, pos1, pos2, out):
                 src = both.bitcast(BF16).rearrange("p h (c e) -> p c h e", e=2)
                 nc.vector.tensor_copy(t[:].rearrange("p (c h e) -> p c h e", h=2, e=2), src)
             else:
-                nc.scalar.copy(t[:].bitcast(U32).rearrange("p (c h) -> p c h", h=2), both.rearrange("p h c -> p c h"))
+                nc.scalar.copy(
+                    t[:, :].bitcast(U32).rearrange("p (c i h) -> p c h i", i=2, h=2),
+                    both.rearrange("p h (c i) -> p c h i", i=2),
+                )
 
         def quant_s(g):
             nc.vector.quantize_mx(out=scodes[g].bitcast(FP8X4), scales=sscales[g][:], in_=sbf[g][:])
@@ -319,7 +340,8 @@ def tile_moe_shr_lin_relu2_kernel(tc, xT, w, b, gate, offs, pos1, pos2, out):
         load_w(0)
         load_plane(1)
         load_w(1)
-        load_plane(0)
+        load_piece(0, 0, 768)
+        load_piece(0, 768, 1024)
         load_w(2)
         for e in range(3, E):
             load_w(e)
@@ -333,23 +355,27 @@ def tile_moe_shr_lin_relu2_kernel(tc, xT, w, b, gate, offs, pos1, pos2, out):
         cast_half(2, 0, "s")
         cast_half(2, 1, "s")
         cast_plane(1, "s")
-        cast_plane(0, "s")
+        cast_piece(0, 0, 768, "s")
+        cast_piece(0, 768, 1024, "s")
+        held_codes()
         for e in range(E):
-            cast_w(e, 0)
+            cast_w(e, 0, "g" if e < 4 else "s")
+            if e < 4:
+                cast_w(e, 1, "g")
             if e % 2 == 1:
                 quant_w(e // 2, 0)
         for c0 in range(0, S, 512):
             gather(3, c0, 512)
         for c0 in range(0, S, 1024):
             gather(2, c0, 1024)
-        regroup(1, 0, 1024)
-        regroup(1, 1024, 1024)
+        regroup(1, 0, 1024, "s")
+        regroup(1, 1024, 1024, "s")
         for c0 in range(0, S, 1024):
             gather(1, c0, 1024)
         gather(0, 0, 1024)
         gather(0, 1024, 512)
-        regroup(0, 0, 1024)
         gather(0, 1536, 512)
+        regroup(0, 0, 1024)
         quant_x(1, 0, 1024)
         quant_x(1, 1024, 1024)
         quant_x(0, 0, 1024)
@@ -360,7 +386,8 @@ def tile_moe_shr_lin_relu2_kernel(tc, xT, w, b, gate, offs, pos1, pos2, out):
         for k in range(4):
             multiply(k, 0)
         for e in range(E):
-            cast_w(e, 1)
+            if e >= 4:
+                cast_w(e, 1)
             if e % 2 == 1:
                 quant_w(e // 2, 1)
         regroup_s(1)
@@ -368,7 +395,7 @@ def tile_moe_shr_lin_relu2_kernel(tc, xT, w, b, gate, offs, pos1, pos2, out):
         for k in range(4):
             multiply(k, 1)
 
-        regroup_s(0, "v")
+        regroup_s(0)
         cast_w(E, 0)
         cast_w(E, 1)
         quant_w(4, 0)

@@ -19,10 +19,16 @@ RELU = mybir.ActivationFunctionType.Relu
 SQUARE = mybir.ActivationFunctionType.Square
 MULT, ADD = mybir.AluOpType.mult, mybir.AluOpType.add
 
-HALF = 512
-CHUNKS = ((0, 1024), (1024, 512), (1536, 512))
-RAW_BUFS = 6
-UNITS = ((0, 0, 512), (0, 512, 1024))
+K_PASS = 512
+BANK = 512
+PAIRS = E // 2
+SHARED = PAIRS
+CHUNK = 1024
+WEIGHT_BUFS = 6
+SMALL_BUFS = 7
+CHUNK_BUFS = 4
+GPSIMD_WEIGHTS = 3
+LAST_CUT = 768
 
 
 def tile_moe_shr_lin_relu2_kernel(tc, xT, w, b, gate, offs, pos1, pos2, out):
@@ -30,7 +36,7 @@ def tile_moe_shr_lin_relu2_kernel(tc, xT, w, b, gate, offs, pos1, pos2, out):
     with ExitStack() as ctx:
         lists = ctx.enter_context(tc.tile_pool(name="lists", bufs=1))
         keep = ctx.enter_context(tc.tile_pool(name="keep", bufs=1))
-        stage = ctx.enter_context(tc.tile_pool(name="stage", bufs=RAW_BUFS))
+        stage = ctx.enter_context(tc.tile_pool(name="stage", bufs=WEIGHT_BUFS))
         group = ctx.enter_context(tc.tile_pool(name="group", bufs=1))
         psum = ctx.enter_context(tc.psum_pool(name="psum", bufs=8))
 
@@ -40,164 +46,130 @@ def tile_moe_shr_lin_relu2_kernel(tc, xT, w, b, gate, offs, pos1, pos2, out):
         pos = (pos1_t, pos2_t)
 
         planes = keep.tile([P, 4 * T], U32, name="planes")
-        y, ys = {}, {}
-        wcodes, wscales = {}, {}
-        for k in range(E // 2 + 1):
-            for m in range(2 if k < E // 2 else 1):
-                if k > 0 and (m == 0 or k < 2):
-                    wcodes[k, m] = keep.tile([P, 4 * P], U32, name=f"wcodes{k}{m}", align_bytes=64)
-                wscales[k, m] = keep.tile([P, 4 * P], U8, name=f"wscales{k}{m}", align_bytes=64)
+
+        wcodes, wscales, scodes = {}, {}, {}
+        for k, m in [(k, m) for k in range(PAIRS) for m in range(2)] + [(SHARED, 0)]:
+            if k > 0 and (m == 0 or k == 1):
+                wcodes[k, m] = keep.tile([P, 4 * P], U32, name=f"wcodes{k}{m}", align_bytes=64)[:]
+            wscales[k, m] = keep.tile([P, 4 * P], U8, name=f"wscales{k}{m}", align_bytes=64)
         xcodes = {0: keep.tile([P, S], U32, name="xcodes0", align_bytes=64)}
         xscales = [keep.tile([P, S], U8, name=f"xscales{g}", align_bytes=64) for g in range(2)]
-        scodes = {}
         sscales = [keep.tile([P, T], U8, name=f"sscales{g}", align_bytes=64) for g in range(2)]
 
         ident = keep.tile([P, P], F32, name="ident")
         make_identity(nc, ident[:])
-        raw = {}
 
-        def rows(s):
+        x_raw, w_raw = {}, {}
+
+        def load_x(s, c0, c1, tag, bufs=1):
             g, h = divmod(s, 2)
-            return xT[HALF * g : HALF * (g + 1), :].rearrange("(p j) t -> p j t", j=4)[:, 2 * h : 2 * h + 2, :]
-
-        def load_half(s, h):
-            t = group.tile([P, 2, HALF], F32, name="quarter", align_bytes=64, bufs=7)
-            raw[s, h] = t
-            nc.sync.dma_start(t[:], rows(s)[:, :, h * HALF : (h + 1) * HALF])
-
-        def load_piece(s, c0, c1):
-            t = group.tile([P, 2, c1 - c0], F32, name=f"piece{c0}", align_bytes=64)
-            raw[s, c0] = t
-            nc.sync.dma_start(t[:], rows(s)[:, :, c0:c1])
-
-        def cast_piece(s, c0, c1, eng):
-            dst = planes[:, s * T + c0 : s * T + c1].bitcast(BF16).rearrange("p (t e) -> p t e", e=2)
-            copy_on(eng, dst, raw[s, c0][:].rearrange("p e t -> p t e"))
-
-        def load_plane(s):
-            t = group.tile([P, 2048], F32, name=f"plane{s}", align_bytes=64)
-            raw[s] = t
-            nc.sync.dma_start(t[:].rearrange("p (j t) -> p j t", j=2), rows(s))
+            rows = xT[K_PASS * g : K_PASS * (g + 1), :].rearrange("(p j) t -> p j t", j=4)
+            x_raw[s, c0] = group.tile([P, 2, c1 - c0], F32, name=tag, align_bytes=64, bufs=bufs)
+            nc.sync.dma_start(x_raw[s, c0][:], rows[:, 2 * h : 2 * h + 2, c0:c1])
 
         def load_w(e):
-            t = stage.tile([P, 2048], F32, name="raw")
-            raw["w", e] = t
+            w_raw[e] = stage.tile([P, 8 * N], F32, name="raw")
             nc.sync.dma_start(
-                t[:].rearrange("p (g j n) -> p g j n", g=2, j=4),
+                w_raw[e][:].rearrange("p (g j n) -> p g j n", g=2, j=4),
                 w[e].rearrange("(g p j) n -> p g j n", p=P, j=4),
             )
 
-        def load_gate():
-            t = stage.tile([P, 2048], F32, name="raw")
-            raw["gate"] = t
-            nc.sync.dma_start(t[:].rearrange("p (r t) -> p r t", r=2), gate[:, 0:P, :].rearrange("r p t -> p r t"))
+        load_x(3, 0, T // 2, "small", SMALL_BUFS)
+        load_x(3, T // 2, T, "small", SMALL_BUFS)
+        nc.sync.dma_start(offs_t[:], offs)
+        load_x(2, 0, T // 2, "small", SMALL_BUFS)
+        load_x(2, T // 2, T, "small", SMALL_BUFS)
+        load_w(0)
+        load_x(1, 0, T, "plane1")
+        load_w(1)
+        load_x(0, 0, LAST_CUT, "plane0_first")
+        load_x(0, LAST_CUT, T, "plane0_last")
+        for e in range(2, E + 1):
+            load_w(e)
+        bias = stage.tile([P, 2, E + 1], F32, name="raw")
+        nc.sync.dma_start(bias[:], b.rearrange("(m p) e -> p m e", p=P))
+        gates = stage.tile([P, 2 * T], F32, name="raw")
+        nc.sync.dma_start(gates[:].rearrange("p (r t) -> p r t", r=2), gate[:, 0:P, :].rearrange("r p t -> p r t"))
+        nc.sync.dma_start(pos1_t[:], pos1)
+        nc.sync.dma_start(pos2_t[:], pos2)
 
-        def load_bias():
-            t = stage.tile([P, 2, E + 1], F32, name="raw")
-            raw["bias"] = t
-            nc.sync.dma_start(t[:], b.rearrange("(m p) e -> p m e", p=P))
+        def cast_x(copy, s, c0, c1):
+            words = planes[:, s * T + c0 : s * T + c1]
+            copy(words.bitcast(BF16).rearrange("p (t e) -> p t e", e=2), x_raw[s, c0][:].rearrange("p e t -> p t e"))
 
-        def load_pos():
-            nc.sync.dma_start(pos1_t[:], pos1)
-            nc.sync.dma_start(pos2_t[:], pos2)
+        w_bf = {}
 
-        def copy_on(eng, dst, src):
-            if eng == "v":
-                nc.vector.tensor_copy(dst, src)
-            elif eng == "s":
-                nc.scalar.copy(dst, src)
+        def cast_w(e, m):
+            key, place = ((e // 2, m), e % 2) if e < E else ((SHARED, 0), m)
+            if key not in w_bf and key in ((2, 0), (3, 0)):
+                w_bf[key] = group.tile([P, 16 * P], BF16, name=f"pair{key[0]}", align_bytes=64)
+            elif key not in w_bf:
+                w_bf[key] = group.tile([P, 16 * P], BF16, name="small", align_bytes=64, bufs=SMALL_BUFS)
+            dst = w_bf[key][:, 8 * P * place : 8 * P * (place + 1)]
+            if e < GPSIMD_WEIGHTS:
+                src = w_raw[e][:].rearrange("p (g j m c) -> p m g c j", g=2, j=4, m=2)[:, m]
+                nc.gpsimd.tensor_scalar(dst.rearrange("p (g c j) -> p g c j", g=2, j=4), src, 1.0, 0.0, MULT, ADD)
             else:
-                nc.gpsimd.tensor_scalar(dst, src, 1.0, 0.0, MULT, ADD)
+                src = w_raw[e][:].rearrange("p (g j m c i) -> p m g c j i", g=2, j=4, m=2, i=2)[:, m]
+                nc.scalar.copy(dst.rearrange("p (g c i j) -> p g c j i", g=2, i=2, j=4), src)
 
-        def cast_half(s, h, eng):
-            dst = planes[:, s * T + h * HALF : s * T + (h + 1) * HALF].bitcast(BF16).rearrange("p (t e) -> p t e", e=2)
-            copy_on(eng, dst, raw[s, h][:].rearrange("p e t -> p t e"))
-
-        def cast_plane(s, eng):
-            dst = planes[:, s * T : (s + 1) * T].bitcast(BF16).rearrange("p (t e) -> p t e", e=2)
-            copy_on(eng, dst, raw[s][:].rearrange("p (e t) -> p t e", e=2))
-
-        wbf = {}
-
-        def cast_w(e, m, eng="s"):
-            key = (e // 2, m) if e < E else (E // 2, 0)
-            if key not in wbf and key in ((2, 0), (3, 0)):
-                wbf[key] = group.tile([P, 16 * P], BF16, name=f"late{key[0]}", align_bytes=64)
-            elif key not in wbf:
-                wbf[key] = group.tile([P, 16 * P], BF16, name="quarter", align_bytes=64, bufs=7)
-            c0 = 8 * P * (e % 2 if e < E else m)
-            src = raw["w", e][:].rearrange("p (g j m c i) -> p m g c j i", g=2, j=4, m=2, i=2)[:, m]
-            dst = wbf[key][:, c0 : c0 + 8 * P].rearrange("p (g c i j) -> p g c j i", g=2, i=2, j=4)
-            if eng == "s":
-                copy_on(eng, dst, src)
-            else:
-                rows4 = raw["w", e][:].rearrange("p (g j m c) -> p m g c j", g=2, j=4, m=2)[:, m]
-                copy_on(eng, wbf[key][:, c0 : c0 + 8 * P].rearrange("p (g c j) -> p g c j", g=2, j=4), rows4)
-
-        def held_codes():
-            t = group.tile([P, S + 8 * P], U32, name="piece768", align_bytes=64)
+        def after_gathers():
+            t = group.tile([P, S + 8 * P], U32, name="plane0_last", align_bytes=64)
             xcodes[1] = t[:, 0:S]
             for m in range(2):
                 wcodes[0, m] = t[:, S + 4 * P * m : S + 4 * P * (m + 1)]
 
-        def late_codes():
-            t = group.tile([P, 2 * T + 8 * P], U32, name="late3", align_bytes=64)
+        def after_routed():
+            t = group.tile([P, 2 * T + 8 * P], U32, name="pair3", align_bytes=64)
             scodes[0], scodes[1] = t[:, 0:T], t[:, T : 2 * T]
-            for k in range(2):
-                wcodes[2 + k, 1] = t[:, 2 * T + 4 * P * k : 2 * T + 4 * P * (k + 1)]
+            for i in range(2):
+                wcodes[2 + i, 1] = t[:, 2 * T + 4 * P * i : 2 * T + 4 * P * (i + 1)]
 
         def quant_w(k, m):
-            if (k, m) not in wcodes:
-                late_codes()
-            nc.vector.quantize_mx(out=wcodes[k, m][:, 0 : 4 * P].bitcast(FP8X4), scales=wscales[k, m][:], in_=wbf[k, m][:])
+            nc.vector.quantize_mx(out=wcodes[k, m].bitcast(FP8X4), scales=wscales[k, m][:], in_=w_bf[k, m][:])
 
         picked = {}
 
         def gather(s, c0, n):
             g, h = divmod(s, 2)
-            i = c0 // 1024
+            i, c = divmod(c0, CHUNK)
             if (g, i) not in picked:
-                picked[g, i] = group.tile([P, 2048], U32, name="big", bufs=4)
+                picked[g, i] = group.tile([P, 2 * CHUNK], U32, name="chunk", bufs=CHUNK_BUFS)
             window = planes[:, s * T : min(s + 2, 4) * T]
-            d0 = 1024 * h + c0 - 1024 * i
-            nc.vector.tensor_copy(picked[g, i][:, d0 : d0 + n], window.indirect(offs_t[:, c0 // 16 : (c0 + n) // 16]))
+            dst = picked[g, i][:, CHUNK * h + c : CHUNK * h + c + n]
+            nc.vector.tensor_copy(dst, window.indirect(offs_t[:, c0 // 16 : (c0 + n) // 16]))
 
-        xbf = {}
+        def side_by_side_on_vector(dst, both):
+            src = both.bitcast(BF16).rearrange("p h (c e) -> p c h e", e=2)
+            nc.vector.tensor_copy(dst[:].rearrange("p (c h e) -> p c h e", h=2, e=2), src)
 
-        def regroup(g, c0, n, eng="v"):
-            if n == 512:
-                t = group.tile([P, 4 * n], BF16, name=f"late{c0 // 512}", align_bytes=64)
-            elif g == 1:
-                t = group.tile([P, 4 * n], BF16, name="plane1" if c0 == 0 else "piece0", align_bytes=64)
-            else:
-                t = group.tile([P, 4 * n], BF16, name="xbf", align_bytes=64)
-            xbf[g, c0] = t
-            i = c0 // 1024
-            both = picked[g, i][:].rearrange("p (h c) -> p h c", h=2)[:, :, c0 - 1024 * i : c0 - 1024 * i + n]
-            if eng == "v":
-                src = both.bitcast(BF16).rearrange("p h (c e) -> p c h e", e=2)
-                nc.vector.tensor_copy(t[:].rearrange("p (c h e) -> p c h e", h=2, e=2), src)
-            else:
-                nc.scalar.copy(
-                    t[:, :].bitcast(U32).rearrange("p (c i h) -> p c h i", i=2, h=2),
-                    both.rearrange("p h (c i) -> p c h i", i=2),
-                )
+        def side_by_side_on_scalar(dst, both):
+            nc.scalar.copy(
+                dst[:].bitcast(U32).rearrange("p (c i h) -> p c h i", i=2, h=2),
+                both.rearrange("p h (c i) -> p c h i", i=2),
+            )
+
+        x_bf = {}
+
+        def regroup(side_by_side, g, c0, n, tag):
+            i, c = divmod(c0, CHUNK)
+            x_bf[g, c0] = group.tile([P, 4 * n], BF16, name=tag, align_bytes=64)
+            side_by_side(x_bf[g, c0], picked[g, i][:].rearrange("p (h c) -> p h c", h=2)[:, :, c : c + n])
 
         def quant_x(g, c0, n):
             cols = slice(c0, c0 + n)
-            nc.vector.quantize_mx(out=xcodes[g][:, cols].bitcast(FP8X4), scales=xscales[g][:, cols], in_=xbf[g, c0][:, :])
+            nc.vector.quantize_mx(out=xcodes[g][:, cols].bitcast(FP8X4), scales=xscales[g][:, cols], in_=x_bf[g, c0][:])
 
         banks = {}
 
         def multiply(k, m):
-            ps = psum.tile([P, 2 * C], F32, name="ps")
-            banks[k, m] = ps
-            for e in range(2):
+            banks[k, m] = psum.tile([P, BANK], F32, name="ps")
+            for i in range(2):
                 for g in (1, 0):
-                    w0 = 2 * P * e + P * g
-                    x0 = C * (2 * k + e)
+                    w0 = 2 * P * i + P * g
+                    x0 = C * (2 * k + i)
                     nc.tensor.matmul_mx(
-                        out=ps[:, C * e : C * (e + 1)],
+                        out=banks[k, m][:, C * i : C * (i + 1)],
                         lhsT=wcodes[k, m][:, w0 : w0 + P].bitcast(FP8X4),
                         lhsT_scale=wscales[k, m][:, w0 : w0 + P],
                         rhs=xcodes[g][:, x0 : x0 + C].bitcast(FP8X4),
@@ -206,243 +178,182 @@ def tile_moe_shr_lin_relu2_kernel(tc, xT, w, b, gate, offs, pos1, pos2, out):
                         stop=(g == 0),
                     )
 
+        y = {}
+
         def relu(k, m):
             if m not in y:
                 y[m] = group.tile([P, S], F32, name=f"y{m}", align_bytes=64)
-            for e in range(2):
-                v = y[m][:, C * (2 * k + e) : C * (2 * k + e + 1)]
+            for i in range(2):
+                e = 2 * k + i
                 nc.scalar.activation(
-                    v, banks[k, m][:, C * e : C * (e + 1)], RELU, bias=raw["bias"][:, m, 2 * k + e : 2 * k + e + 1]
+                    y[m][:, C * e : C * (e + 1)], banks[k, m][:, C * i : C * (i + 1)], RELU, bias=bias[:, m, e : e + 1]
                 )
 
-        def square(k, m, n=1):
-            v = y[m][:, 2 * C * k : 2 * C * (k + n)]
+        def square(v):
             nc.scalar.activation(v, v, SQUARE)
 
-        sbf = {}
+        def y_pairs(m, k0, k1):
+            return y[m][:, BANK * k0 : BANK * k1]
 
-        def regroup_s(g, eng="s"):
-            t = group.tile([P, 4 * T], BF16, name=("ys", "sbf1")[g], align_bytes=64)
-            sbf[g] = t
-            both = planes[:, 2 * g * T : 2 * (g + 1) * T].rearrange("p (h c) -> p h c", h=2)
-            if eng == "v":
-                src = both.bitcast(BF16).rearrange("p h (c e) -> p c h e", e=2)
-                nc.vector.tensor_copy(t[:].rearrange("p (c h e) -> p c h e", h=2, e=2), src)
-            else:
-                nc.scalar.copy(
-                    t[:, :].bitcast(U32).rearrange("p (c i h) -> p c h i", i=2, h=2),
-                    both.rearrange("p h (c i) -> p c h i", i=2),
-                )
+        s_bf = {}
 
-        def quant_s(g):
-            nc.vector.quantize_mx(out=scodes[g].bitcast(FP8X4), scales=sscales[g][:], in_=sbf[g][:])
+        def regroup_shared(side_by_side, g, tag):
+            s_bf[g] = group.tile([P, 4 * T], BF16, name=tag, align_bytes=64)
+            side_by_side(s_bf[g], planes[:, 2 * g * T : 2 * (g + 1) * T].rearrange("p (h c) -> p h c", h=2))
 
-        sbanks = {}
+        def quant_shared(g):
+            nc.vector.quantize_mx(out=scodes[g].bitcast(FP8X4), scales=sscales[g][:], in_=s_bf[g][:])
 
-        def multiply_s(m, h):
-            ps = psum.tile([P, HALF], F32, name="ps")
-            sbanks[m, h] = ps
+        def multiply_shared(m, half):
+            banks[SHARED, m, half] = psum.tile([P, BANK], F32, name="ps")
+            cols = slice(BANK * half, BANK * (half + 1))
             for g in (1, 0):
                 w0 = 2 * P * m + P * g
                 nc.tensor.matmul_mx(
-                    out=ps[:],
-                    lhsT=wcodes[E // 2, 0][:, w0 : w0 + P].bitcast(FP8X4),
-                    lhsT_scale=wscales[E // 2, 0][:, w0 : w0 + P],
-                    rhs=scodes[g][:, HALF * h : HALF * (h + 1)].bitcast(FP8X4),
-                    rhs_scale=sscales[g][:, HALF * h : HALF * (h + 1)],
+                    out=banks[SHARED, m, half][:],
+                    lhsT=wcodes[SHARED, 0][:, w0 : w0 + P].bitcast(FP8X4),
+                    lhsT_scale=wscales[SHARED, 0][:, w0 : w0 + P],
+                    rhs=scodes[g][:, cols].bitcast(FP8X4),
+                    rhs_scale=sscales[g][:, cols],
                     start=(g == 1),
                     stop=(g == 0),
                 )
 
-        def relu_s(m, h):
-            if m not in ys:
-                t = group.tile([P, 2 * T], F32, name="ys", align_bytes=64)
-                ys[0], ys[1] = t[:, 0:T], t[:, T : 2 * T]
-            v = ys[m][:, HALF * h : HALF * (h + 1)]
-            nc.scalar.activation(v, sbanks[m, h][:], RELU, bias=raw["bias"][:, m, E : E + 1])
+        cast_x(nc.vector.tensor_copy, 3, 0, T // 2)
+        cast_x(nc.vector.tensor_copy, 3, T // 2, T)
+        cast_x(nc.scalar.copy, 2, 0, T // 2)
+        cast_x(nc.scalar.copy, 2, T // 2, T)
+        cast_x(nc.scalar.copy, 1, 0, T)
+        cast_x(nc.scalar.copy, 0, 0, LAST_CUT)
+        cast_x(nc.scalar.copy, 0, LAST_CUT, T)
+        after_gathers()
+        for e in range(E):
+            cast_w(e, 0)
+            if e < GPSIMD_WEIGHTS:
+                cast_w(e, 1)
+        for c0 in range(0, S, T // 2):
+            gather(3, c0, T // 2)
+        for c0 in range(0, S, CHUNK):
+            gather(2, c0, CHUNK)
+        regroup(side_by_side_on_scalar, 1, 0, CHUNK, "plane1")
+        regroup(side_by_side_on_scalar, 1, CHUNK, CHUNK, "plane0_first")
+        for c0 in range(0, S, CHUNK):
+            gather(1, c0, CHUNK)
+        gather(0, 0, CHUNK)
+        gather(0, 2 * BANK, BANK)
+        gather(0, 3 * BANK, BANK)
+        for k in range(PAIRS):
+            quant_w(k, 0)
+        regroup(side_by_side_on_vector, 0, 0, CHUNK, "x_bf")
+        quant_x(1, 0, CHUNK)
+        quant_x(1, CHUNK, CHUNK)
+        quant_x(0, 0, CHUNK)
+        for k in (2, 3):
+            regroup(side_by_side_on_vector, 0, BANK * k, BANK, f"pair{k}")
+            quant_x(0, BANK * k, BANK)
+        for k in range(PAIRS):
+            multiply(k, 0)
+        after_routed()
+        for e in range(E):
+            if e >= GPSIMD_WEIGHTS:
+                cast_w(e, 1)
+            if e % 2 == 1:
+                quant_w(e // 2, 1)
+        regroup_shared(side_by_side_on_scalar, 1, "s_bf1")
+        quant_shared(1)
+        for k in range(PAIRS):
+            multiply(k, 1)
+        regroup_shared(side_by_side_on_vector, 0, "ys")
+        cast_w(E, 0)
+        cast_w(E, 1)
+        quant_w(SHARED, 0)
+        quant_shared(0)
 
-        def square_s(m, h):
-            v = ys[m][:, HALF * h : HALF * (h + 1)]
-            nc.scalar.activation(v, v, SQUARE)
+        relu(0, 0)
+        relu(1, 0)
+        relu(2, 0)
+        square(y_pairs(0, 0, 2))
+        relu(3, 0)
+        square(y_pairs(0, 2, 3))
+        square(y_pairs(0, 3, 4))
+        for k in range(PAIRS):
+            relu(k, 1)
+        square(y_pairs(1, 0, 2))
+        square(y_pairs(1, 2, 4))
+        for m in range(2):
+            for half in range(2):
+                multiply_shared(m, half)
+        ys_all = group.tile([P, 2 * T], F32, name="ys", align_bytes=64)
 
-        part = {}
+        def ys(m, half):
+            return ys_all[:, T * m + BANK * half : T * m + BANK * (half + 1)]
 
-        def fetch(u, r):
-            m, c0, c1 = UNITS[u]
-            if u not in part:
-                t = group.tile([P, 2048], U32, name="big", bufs=4)
-                part[u] = t[:].bitcast(F32).rearrange("p (r c) -> p r c", r=2)
-            weight = raw["gate"][:, T * r + c0 : T * r + c1]
-            nc.vector.tensor_tensor(
-                part[u][:, r, 0 : c1 - c0], y[m][:].indirect(pos[r][:, c0 // 16 : c1 // 16]), weight, MULT
-            )
+        def relu_shared(m, half):
+            nc.scalar.activation(ys(m, half), banks[SHARED, m, half][:], RELU, bias=bias[:, m, E : E + 1])
 
-        def add_parts(u):
-            m, c0, c1 = UNITS[u]
-            v = part[u][:, :, 0 : c1 - c0]
-            nc.vector.tensor_tensor(v[:, 0], v[:, 0], v[:, 1], ADD)
+        relu_shared(0, 0)
+        relu_shared(0, 1)
+        square(ys(0, 0))
+        relu_shared(1, 0)
+        square(ys(0, 1))
+        square(ys(1, 0))
 
-        def add_shared(u):
-            m, c0, c1 = UNITS[u]
-            v = part[u][:, 0, 0 : c1 - c0]
-            nc.vector.tensor_tensor(v, v, ys[m][:, c0:c1], ADD)
-
-        turned = {}
-
-        def sum_turned(u, c0):
-            m, u0, u1 = UNITS[u]
-            ps = psum.tile([P, HALF], F32, name="ps")
-            turned[u, c0] = ps
-            n = min(HALF, u1 - c0)
-            for j in range(0, n, P):
-                a = c0 - u0 + j
-                terms = (part[u][:, 0, a : a + P], part[u][:, 1, a : a + P], ys[m][:, c0 + j : c0 + j + P])
-                for i, term in enumerate(terms):
-                    nc.tensor.matmul(ps[:, j : j + P], term, ident[:], start=(i == 0), stop=(i == 2), is_transpose=True)
-
-        def copy_turned(u, c0):
-            m, u0, u1 = UNITS[u]
-            n = min(HALF, u1 - c0)
-            nc.scalar.copy(part[u][:, 1, c0 - u0 : c0 - u0 + n], turned[u, c0][:, 0:n])
-
-        def turn_back(u, c0):
-            m, u0, u1 = UNITS[u]
-            n = min(HALF, u1 - c0)
-            ps = psum.tile([P, HALF], F32, name="ps")
-            turned[u, c0] = ps
-            for j in range(0, n, P):
-                a = c0 - u0 + j
-                nc.tensor.transpose(ps[:, j : j + P], part[u][:, 1, a : a + P], ident[:])
-
-        def store_turned(u, c0):
-            m, u0, u1 = UNITS[u]
-            n = min(HALF, u1 - c0)
-            v = part[u][:, 0, c0 - u0 : c0 - u0 + n]
-            nc.scalar.copy(v, turned[u, c0][:, 0:n])
-            nc.sync.dma_start(out[m * P : (m + 1) * P, c0 : c0 + n], v)
-
-        def fetch_into(dst, m, r, c0, c1):
-            weight = raw["gate"][:, T * r + c0 : T * r + c1]
+        def fetch(dst, m, half, r):
+            c0, c1 = BANK * half, BANK * (half + 1)
+            weight = gates[:, T * r + c0 : T * r + c1]
             nc.vector.tensor_tensor(dst, y[m][:].indirect(pos[r][:, c0 // 16 : c1 // 16]), weight, MULT)
 
         def add_into(dst, other):
             nc.vector.tensor_tensor(dst, dst, other, ADD)
 
-        def store(u):
-            m, c0, c1 = UNITS[u]
-            nc.sync.dma_start(out[m * P : (m + 1) * P, c0:c1], part[u][:, 0, 0 : c1 - c0])
+        def store(m, half, src):
+            nc.sync.dma_start(out[m * P : (m + 1) * P, BANK * half : BANK * (half + 1)], src)
 
-        load_half(3, 0)
-        load_half(3, 1)
-        nc.sync.dma_start(offs_t[:], offs)
-        load_half(2, 0)
-        load_half(2, 1)
-        load_w(0)
-        load_plane(1)
-        load_w(1)
-        load_piece(0, 0, 768)
-        load_piece(0, 768, 1024)
-        load_w(2)
-        for e in range(3, E):
-            load_w(e)
-        load_w(E)
-        load_bias()
-        load_gate()
-        load_pos()
+        terms, turned = {}, {}
+        for half in range(2):
+            t = group.tile([P, 2 * CHUNK], U32, name="chunk", bufs=CHUNK_BUFS)
+            terms[half] = (t[:, 0:BANK].bitcast(F32), t[:, CHUNK : CHUNK + BANK].bitcast(F32))
+            for r in range(2):
+                fetch(terms[half][r], 0, half, r)
 
-        cast_half(3, 0, "v")
-        cast_half(3, 1, "v")
-        cast_half(2, 0, "s")
-        cast_half(2, 1, "s")
-        cast_plane(1, "s")
-        cast_piece(0, 0, 768, "s")
-        cast_piece(0, 768, 1024, "s")
-        held_codes()
-        for e in range(E):
-            cast_w(e, 0, "g" if e < 4 else "s")
-            if e < 4:
-                cast_w(e, 1, "g")
-            if e % 2 == 1:
-                quant_w(e // 2, 0)
-        for c0 in range(0, S, 512):
-            gather(3, c0, 512)
-        for c0 in range(0, S, 1024):
-            gather(2, c0, 1024)
-        regroup(1, 0, 1024, "s")
-        regroup(1, 1024, 1024, "s")
-        for c0 in range(0, S, 1024):
-            gather(1, c0, 1024)
-        gather(0, 0, 1024)
-        gather(0, 1024, 512)
-        gather(0, 1536, 512)
-        regroup(0, 0, 1024)
-        quant_x(1, 0, 1024)
-        quant_x(1, 1024, 1024)
-        quant_x(0, 0, 1024)
-        regroup(0, 1024, 512)
-        quant_x(0, 1024, 512)
-        regroup(0, 1536, 512)
-        quant_x(0, 1536, 512)
-        for k in range(4):
-            multiply(k, 0)
-        for e in range(E):
-            if e >= 4:
-                cast_w(e, 1)
-            if e % 2 == 1:
-                quant_w(e // 2, 1)
-        regroup_s(1)
-        quant_s(1)
-        for k in range(4):
-            multiply(k, 1)
+        def sum_turned(half):
+            turned[half] = psum.tile([P, BANK], F32, name="ps")
+            for j in range(0, BANK, P):
+                for i, term in enumerate((*terms[half], ys(0, half))):
+                    nc.tensor.matmul(
+                        turned[half][:, j : j + P], term[:, j : j + P], ident[:],
+                        start=(i == 0), stop=(i == 2), is_transpose=True,
+                    )
 
-        regroup_s(0)
-        cast_w(E, 0)
-        cast_w(E, 1)
-        quant_w(4, 0)
-        quant_s(0)
-        relu(0, 0)
-        relu(1, 0)
-        relu(2, 0)
-        square(0, 0, 2)
-        relu(3, 0)
-        square(2, 0)
-        square(3, 0)
-        for k in range(4):
-            relu(k, 1)
-        square(0, 1, 2)
-        square(2, 1, 2)
-        for m, h in ((0, 0), (0, 1), (1, 0), (1, 1)):
-            multiply_s(m, h)
-        relu_s(0, 0)
-        relu_s(0, 1)
-        square_s(0, 0)
-        relu_s(1, 0)
-        square_s(0, 1)
-        square_s(1, 0)
+        def turn_back(half):
+            nc.scalar.copy(terms[half][1], turned[half][:])
+            turned[half] = psum.tile([P, BANK], F32, name="ps")
+            for j in range(0, BANK, P):
+                nc.tensor.transpose(turned[half][:, j : j + P], terms[half][1][:, j : j + P], ident[:])
 
-        for u in range(2):
-            fetch(u, 0)
-            fetch(u, 1)
-        sum_turned(0, 0)
-        sum_turned(1, 512)
-        copy_turned(0, 0)
-        turn_back(0, 0)
-        relu_s(1, 1)
-        copy_turned(1, 512)
-        turn_back(1, 512)
-        square_s(1, 1)
-        last = group.tile([P, 2048], U32, name="big", bufs=4)
-        a1, b1, b2 = (last[:, HALF * i : HALF * (i + 1)].bitcast(F32) for i in range(3))
-        a2 = ys[1][:, 0:HALF]
-        fetch_into(a1, 1, 0, 0, HALF)
-        fetch_into(b1, 1, 1, 0, HALF)
-        add_into(a1, ys[1][:, 0:HALF])
-        fetch_into(a2, 1, 0, HALF, T)
-        add_into(a1, b1)
-        nc.sync.dma_start(out[P : 2 * P, 0:HALF], a1)
-        add_into(a2, ys[1][:, HALF:T])
-        fetch_into(b2, 1, 1, HALF, T)
-        store_turned(0, 0)
-        store_turned(1, 512)
-        add_into(a2, b2)
-        nc.sync.dma_start(out[P : 2 * P, HALF:T], a2)
+        def store_turned(half):
+            nc.scalar.copy(terms[half][0], turned[half][:])
+            store(0, half, terms[half][0])
+
+        sum_turned(0)
+        sum_turned(1)
+        turn_back(0)
+        relu_shared(1, 1)
+        turn_back(1)
+        square(ys(1, 1))
+
+        t = group.tile([P, 2 * CHUNK], U32, name="chunk", bufs=CHUNK_BUFS)
+        first0, second0, second1 = (t[:, BANK * i : BANK * (i + 1)].bitcast(F32) for i in range(3))
+        first1 = ys(1, 0)
+        fetch(first0, 1, 0, 0)
+        fetch(second0, 1, 0, 1)
+        add_into(first0, ys(1, 0))
+        fetch(first1, 1, 1, 0)
+        add_into(first0, second0)
+        store(1, 0, first0)
+        add_into(first1, ys(1, 1))
+        fetch(second1, 1, 1, 1)
+        store_turned(0)
+        store_turned(1)
+        add_into(first1, second1)
+        store(1, 1, first1)

@@ -24,11 +24,11 @@ BANK = 512
 PAIRS = E // 2
 SHARED = PAIRS
 CHUNK = 1024
-WEIGHT_BUFS = 6
-SMALL_BUFS = 7
-CHUNK_BUFS = 4
-GPSIMD_WEIGHTS = 3
-LAST_CUT = 768
+HALF = T // 2
+WEIGHT_BUFS = 8
+GPSIMD_WEIGHTS = 4
+KIB = 1024
+LINK = 64
 
 
 def tile_moe_shr_lin_relu2_kernel(tc, xT, w, b, gate, offs, pos1, pos2, out):
@@ -37,8 +37,11 @@ def tile_moe_shr_lin_relu2_kernel(tc, xT, w, b, gate, offs, pos1, pos2, out):
         lists = ctx.enter_context(tc.tile_pool(name="lists", bufs=1))
         keep = ctx.enter_context(tc.tile_pool(name="keep", bufs=1))
         stage = ctx.enter_context(tc.tile_pool(name="stage", bufs=WEIGHT_BUFS))
-        group = ctx.enter_context(tc.tile_pool(name="group", bufs=1))
+        placed = ctx.enter_context(tc.tile_pool(name="placed", bufs=1))
         psum = ctx.enter_context(tc.psum_pool(name="psum", bufs=8))
+
+        def place(name, offset, shape, dtype):
+            return placed.tile(shape, dtype, name=name, offset=offset, align_bytes=64)
 
         offs_t = lists.tile([P, S // 16], U16, name="offs_t")
         pos1_t = lists.tile([P, T // 16], U16, name="pos1_t")
@@ -60,12 +63,15 @@ def tile_moe_shr_lin_relu2_kernel(tc, xT, w, b, gate, offs, pos1, pos2, out):
         make_identity(nc, ident[:])
 
         x_raw, w_raw = {}, {}
+        X_AT = {(3, 0): 0, (3, 1): 4 * KIB, (2, 0): 8 * KIB, (2, 1): 12 * KIB, (1, 0): 16 * KIB, (1, 1): 20 * KIB,
+                (0, 0): 24 * KIB, (0, 1): 40 * KIB - LINK}
 
-        def load_x(s, c0, c1, tag, bufs=1):
+        def load_x(s):
             g, h = divmod(s, 2)
             rows = xT[K_PASS * g : K_PASS * (g + 1), :].rearrange("(p j) t -> p j t", j=4)
-            x_raw[s, c0] = group.tile([P, 2, c1 - c0], F32, name=tag, align_bytes=64, bufs=bufs)
-            nc.sync.dma_start(x_raw[s, c0][:], rows[:, 2 * h : 2 * h + 2, c0:c1])
+            for i in range(2):
+                x_raw[s, i] = place(f"x_raw{s}{i}", X_AT[s, i], [P, 2, HALF], F32)
+                nc.sync.dma_start(x_raw[s, i][:], rows[:, 2 * h : 2 * h + 2, HALF * i : HALF * (i + 1)])
 
         def load_w(e):
             w_raw[e] = stage.tile([P, 8 * N], F32, name="raw")
@@ -74,17 +80,13 @@ def tile_moe_shr_lin_relu2_kernel(tc, xT, w, b, gate, offs, pos1, pos2, out):
                 w[e].rearrange("(g p j) n -> p g j n", p=P, j=4),
             )
 
-        load_x(3, 0, T // 2, "small", SMALL_BUFS)
-        load_x(3, T // 2, T, "small", SMALL_BUFS)
+        load_x(3)
         nc.sync.dma_start(offs_t[:], offs)
-        load_x(2, 0, T // 2, "small", SMALL_BUFS)
-        load_x(2, T // 2, T, "small", SMALL_BUFS)
+        load_x(2)
         load_w(0)
-        load_x(1, 0, T, "plane1")
-        load_w(1)
-        load_x(0, 0, LAST_CUT, "plane0_first")
-        load_x(0, LAST_CUT, T, "plane0_last")
-        for e in range(2, E + 1):
+        load_x(1)
+        load_x(0)
+        for e in range(1, E + 1):
             load_w(e)
         bias = stage.tile([P, 2, E + 1], F32, name="raw")
         nc.sync.dma_start(bias[:], b.rearrange("(m p) e -> p m e", p=P))
@@ -93,34 +95,36 @@ def tile_moe_shr_lin_relu2_kernel(tc, xT, w, b, gate, offs, pos1, pos2, out):
         nc.sync.dma_start(pos1_t[:], pos1)
         nc.sync.dma_start(pos2_t[:], pos2)
 
-        def cast_x(copy, s, c0, c1):
-            words = planes[:, s * T + c0 : s * T + c1]
-            copy(words.bitcast(BF16).rearrange("p (t e) -> p t e", e=2), x_raw[s, c0][:].rearrange("p e t -> p t e"))
+        def gpsimd_copy(dst, src):
+            nc.gpsimd.tensor_scalar(dst, src, 1.0, 0.0, MULT, ADD)
+
+        def cast_x(copy, s, i):
+            words = planes[:, s * T + HALF * i : s * T + HALF * (i + 1)]
+            copy(words.bitcast(BF16).rearrange("p (t e) -> p t e", e=2), x_raw[s, i][:].rearrange("p e t -> p t e"))
 
         w_bf = {}
+        W_AT = {(0, 0): 80, (0, 1): 84, (1, 0): 88, (1, 1): 92, (2, 0): 96, (3, 0): 100, (2, 1): 64, (3, 1): 68, (SHARED, 0): 72}
 
         def cast_w(e, m):
-            key, place = ((e // 2, m), e % 2) if e < E else ((SHARED, 0), m)
-            if key not in w_bf and key in ((2, 0), (3, 0)):
-                w_bf[key] = group.tile([P, 16 * P], BF16, name=f"pair{key[0]}", align_bytes=64)
-            elif key not in w_bf:
-                w_bf[key] = group.tile([P, 16 * P], BF16, name="small", align_bytes=64, bufs=SMALL_BUFS)
-            dst = w_bf[key][:, 8 * P * place : 8 * P * (place + 1)]
+            key, at = ((e // 2, m), e % 2) if e < E else ((SHARED, 0), m)
+            if key not in w_bf:
+                w_bf[key] = place(f"w_bf{key[0]}{key[1]}", W_AT[key] * KIB, [P, 16 * P], BF16)
+            dst = w_bf[key][:, 8 * P * at : 8 * P * (at + 1)]
             if e < GPSIMD_WEIGHTS:
                 src = w_raw[e][:].rearrange("p (g j m c) -> p m g c j", g=2, j=4, m=2)[:, m]
-                nc.gpsimd.tensor_scalar(dst.rearrange("p (g c j) -> p g c j", g=2, j=4), src, 1.0, 0.0, MULT, ADD)
+                gpsimd_copy(dst.rearrange("p (g c j) -> p g c j", g=2, j=4), src)
             else:
                 src = w_raw[e][:].rearrange("p (g j m c i) -> p m g c j i", g=2, j=4, m=2, i=2)[:, m]
                 nc.scalar.copy(dst.rearrange("p (g c i j) -> p g c j i", g=2, i=2, j=4), src)
 
         def after_gathers():
-            t = group.tile([P, S + 8 * P], U32, name="plane0_last", align_bytes=64)
+            t = place("codes_after_gathers", 44 * KIB - 2 * LINK, [P, S + 8 * P], U32)
             xcodes[1] = t[:, 0:S]
             for m in range(2):
                 wcodes[0, m] = t[:, S + 4 * P * m : S + 4 * P * (m + 1)]
 
         def after_routed():
-            t = group.tile([P, 2 * T + 8 * P], U32, name="pair3", align_bytes=64)
+            t = place("codes_after_routed", 100 * KIB, [P, 2 * T + 8 * P], U32)
             scodes[0], scodes[1] = t[:, 0:T], t[:, T : 2 * T]
             for i in range(2):
                 wcodes[2 + i, 1] = t[:, 2 * T + 4 * P * i : 2 * T + 4 * P * (i + 1)]
@@ -129,12 +133,13 @@ def tile_moe_shr_lin_relu2_kernel(tc, xT, w, b, gate, offs, pos1, pos2, out):
             nc.vector.quantize_mx(out=wcodes[k, m].bitcast(FP8X4), scales=wscales[k, m][:], in_=w_bf[k, m][:])
 
         picked = {}
+        PICKED_AT = {(1, 0): 56, (1, 1): 64, (0, 0): 72, (0, 1): 32}
 
         def gather(s, c0, n):
             g, h = divmod(s, 2)
             i, c = divmod(c0, CHUNK)
             if (g, i) not in picked:
-                picked[g, i] = group.tile([P, 2 * CHUNK], U32, name="chunk", bufs=CHUNK_BUFS)
+                picked[g, i] = place(f"picked{g}{i}", PICKED_AT[g, i] * KIB, [P, 2 * CHUNK], U32)
             window = planes[:, s * T : min(s + 2, 4) * T]
             dst = picked[g, i][:, CHUNK * h + c : CHUNK * h + c + n]
             nc.vector.tensor_copy(dst, window.indirect(offs_t[:, c0 // 16 : (c0 + n) // 16]))
@@ -151,9 +156,9 @@ def tile_moe_shr_lin_relu2_kernel(tc, xT, w, b, gate, offs, pos1, pos2, out):
 
         x_bf = {}
 
-        def regroup(side_by_side, g, c0, n, tag):
+        def regroup(side_by_side, g, c0, n, kib):
             i, c = divmod(c0, CHUNK)
-            x_bf[g, c0] = group.tile([P, 4 * n], BF16, name=tag, align_bytes=64)
+            x_bf[g, c0] = place(f"x_bf{g}_{c0}", kib * KIB, [P, 4 * n], BF16)
             side_by_side(x_bf[g, c0], picked[g, i][:].rearrange("p (h c) -> p h c", h=2)[:, :, c : c + n])
 
         def quant_x(g, c0, n):
@@ -182,7 +187,7 @@ def tile_moe_shr_lin_relu2_kernel(tc, xT, w, b, gate, offs, pos1, pos2, out):
 
         def relu(k, m):
             if m not in y:
-                y[m] = group.tile([P, S], F32, name=f"y{m}", align_bytes=64)
+                y[m] = place(f"y{m}", (16 + 8 * m) * KIB, [P, S], F32)
             for i in range(2):
                 e = 2 * k + i
                 nc.scalar.activation(
@@ -197,8 +202,8 @@ def tile_moe_shr_lin_relu2_kernel(tc, xT, w, b, gate, offs, pos1, pos2, out):
 
         s_bf = {}
 
-        def regroup_shared(side_by_side, g, tag):
-            s_bf[g] = group.tile([P, 4 * T], BF16, name=tag, align_bytes=64)
+        def regroup_shared(side_by_side, g):
+            s_bf[g] = place(f"s_bf{g}", 8 * (1 - g) * KIB, [P, 4 * T], BF16)
             side_by_side(s_bf[g], planes[:, 2 * g * T : 2 * (g + 1) * T].rearrange("p (h c) -> p h c", h=2))
 
         def quant_shared(g):
@@ -219,37 +224,44 @@ def tile_moe_shr_lin_relu2_kernel(tc, xT, w, b, gate, offs, pos1, pos2, out):
                     stop=(g == 0),
                 )
 
-        cast_x(nc.vector.tensor_copy, 3, 0, T // 2)
-        cast_x(nc.vector.tensor_copy, 3, T // 2, T)
-        cast_x(nc.scalar.copy, 2, 0, T // 2)
-        cast_x(nc.scalar.copy, 2, T // 2, T)
-        cast_x(nc.scalar.copy, 1, 0, T)
-        cast_x(nc.scalar.copy, 0, 0, LAST_CUT)
-        cast_x(nc.scalar.copy, 0, LAST_CUT, T)
+        cast_x(nc.vector.tensor_copy, 3, 0)
+        cast_x(nc.vector.tensor_copy, 3, 1)
+        cast_x(nc.scalar.copy, 2, 0)
+        cast_x(nc.scalar.copy, 2, 1)
+        cast_w(0, 0)
+        cast_w(0, 1)
+        cast_x(nc.scalar.copy, 1, 0)
+        cast_x(nc.scalar.copy, 1, 1)
+        cast_x(nc.scalar.copy, 0, 0)
+        cast_x(gpsimd_copy, 0, 1)
         after_gathers()
-        for e in range(E):
+        for e in range(1, GPSIMD_WEIGHTS):
             cast_w(e, 0)
-            if e < GPSIMD_WEIGHTS:
-                cast_w(e, 1)
-        for c0 in range(0, S, T // 2):
-            gather(3, c0, T // 2)
+            cast_w(e, 1)
+        for c0 in range(0, S, HALF):
+            gather(3, c0, HALF)
         for c0 in range(0, S, CHUNK):
             gather(2, c0, CHUNK)
-        regroup(side_by_side_on_scalar, 1, 0, CHUNK, "plane1")
-        regroup(side_by_side_on_scalar, 1, CHUNK, CHUNK, "plane0_first")
-        for c0 in range(0, S, CHUNK):
-            gather(1, c0, CHUNK)
+        regroup_shared(side_by_side_on_scalar, 1)
+        regroup(side_by_side_on_scalar, 1, 0, CHUNK, 16)
+        regroup(side_by_side_on_scalar, 1, CHUNK, CHUNK, 24)
+        gather(1, 0, CHUNK)
         gather(0, 0, CHUNK)
+        gather(1, CHUNK, CHUNK)
         gather(0, 2 * BANK, BANK)
         gather(0, 3 * BANK, BANK)
-        for k in range(PAIRS):
-            quant_w(k, 0)
-        regroup(side_by_side_on_vector, 0, 0, CHUNK, "x_bf")
+        regroup_shared(side_by_side_on_scalar, 0)
+        regroup(side_by_side_on_scalar, 0, 0, CHUNK, 56)
+        for e in range(GPSIMD_WEIGHTS, E):
+            cast_w(e, 0)
+        quant_w(0, 0)
+        quant_w(1, 0)
         quant_x(1, 0, CHUNK)
-        quant_x(1, CHUNK, CHUNK)
         quant_x(0, 0, CHUNK)
+        quant_x(1, CHUNK, CHUNK)
         for k in (2, 3):
-            regroup(side_by_side_on_vector, 0, BANK * k, BANK, f"pair{k}")
+            quant_w(k, 0)
+            regroup(side_by_side_on_vector, 0, BANK * k, BANK, W_AT[k, 0])
             quant_x(0, BANK * k, BANK)
         for k in range(PAIRS):
             multiply(k, 0)
@@ -259,11 +271,9 @@ def tile_moe_shr_lin_relu2_kernel(tc, xT, w, b, gate, offs, pos1, pos2, out):
                 cast_w(e, 1)
             if e % 2 == 1:
                 quant_w(e // 2, 1)
-        regroup_shared(side_by_side_on_scalar, 1, "s_bf1")
         quant_shared(1)
         for k in range(PAIRS):
             multiply(k, 1)
-        regroup_shared(side_by_side_on_vector, 0, "ys")
         cast_w(E, 0)
         cast_w(E, 1)
         quant_w(SHARED, 0)
@@ -283,7 +293,7 @@ def tile_moe_shr_lin_relu2_kernel(tc, xT, w, b, gate, offs, pos1, pos2, out):
         for m in range(2):
             for half in range(2):
                 multiply_shared(m, half)
-        ys_all = group.tile([P, 2 * T], F32, name="ys", align_bytes=64)
+        ys_all = place("ys", 32 * KIB, [P, 2 * T], F32)
 
         def ys(m, half):
             return ys_all[:, T * m + BANK * half : T * m + BANK * (half + 1)]
@@ -311,8 +321,8 @@ def tile_moe_shr_lin_relu2_kernel(tc, xT, w, b, gate, offs, pos1, pos2, out):
 
         terms, turned = {}, {}
         for half in range(2):
-            t = group.tile([P, 2 * CHUNK], U32, name="chunk", bufs=CHUNK_BUFS)
-            terms[half] = (t[:, 0:BANK].bitcast(F32), t[:, CHUNK : CHUNK + BANK].bitcast(F32))
+            t = place(f"terms{half}", 4 * half * KIB, [P, 2 * BANK], F32)
+            terms[half] = (t[:, 0:BANK], t[:, BANK : 2 * BANK])
             for r in range(2):
                 fetch(terms[half][r], 0, half, r)
 
@@ -342,8 +352,8 @@ def tile_moe_shr_lin_relu2_kernel(tc, xT, w, b, gate, offs, pos1, pos2, out):
         turn_back(1)
         square(ys(1, 1))
 
-        t = group.tile([P, 2 * CHUNK], U32, name="chunk", bufs=CHUNK_BUFS)
-        first0, second0, second1 = (t[:, BANK * i : BANK * (i + 1)].bitcast(F32) for i in range(3))
+        t = place("terms_last", 8 * KIB, [P, 3 * BANK], F32)
+        first0, second0, second1 = (t[:, BANK * i : BANK * (i + 1)] for i in range(3))
         first1 = ys(1, 0)
         fetch(first0, 1, 0, 0)
         fetch(second0, 1, 0, 1)

@@ -22,13 +22,16 @@ MULT, ADD = mybir.AluOpType.mult, mybir.AluOpType.add
 K_PASS = 512
 BANK = 512
 PAIRS = E // 2
-SHARED = PAIRS
 CHUNK = 1024
 HALF = T // 2
-WEIGHT_BUFS = 8
-GPSIMD_WEIGHTS = 4
 KIB = 1024
 LINK = 64
+
+RAW_X = 0
+PICKED = 32
+RAW_W = 64
+CAST_W = 136
+GATES = 152
 
 
 def tile_moe_shr_lin_relu2_kernel(tc, xT, w, b, gate, offs, pos1, pos2, out):
@@ -36,12 +39,11 @@ def tile_moe_shr_lin_relu2_kernel(tc, xT, w, b, gate, offs, pos1, pos2, out):
     with ExitStack() as ctx:
         lists = ctx.enter_context(tc.tile_pool(name="lists", bufs=1))
         keep = ctx.enter_context(tc.tile_pool(name="keep", bufs=1))
-        stage = ctx.enter_context(tc.tile_pool(name="stage", bufs=WEIGHT_BUFS))
         placed = ctx.enter_context(tc.tile_pool(name="placed", bufs=1))
         psum = ctx.enter_context(tc.psum_pool(name="psum", bufs=8))
 
-        def place(name, offset, shape, dtype):
-            return placed.tile(shape, dtype, name=name, offset=offset, align_bytes=64)
+        def place(name, kib, shape, dtype, shift=0):
+            return placed.tile(shape, dtype, name=name, offset=kib * KIB + shift, align_bytes=64)
 
         offs_t = lists.tile([P, S // 16], U16, name="offs_t")
         pos1_t = lists.tile([P, T // 16], U16, name="pos1_t")
@@ -49,32 +51,28 @@ def tile_moe_shr_lin_relu2_kernel(tc, xT, w, b, gate, offs, pos1, pos2, out):
         pos = (pos1_t, pos2_t)
 
         planes = keep.tile([P, 4 * T], U32, name="planes")
-
-        wcodes, wscales, scodes = {}, {}, {}
-        for k, m in [(k, m) for k in range(PAIRS) for m in range(2)] + [(SHARED, 0)]:
-            if k > 0 and (m == 0 or k == 1):
-                wcodes[k, m] = keep.tile([P, 4 * P], U32, name=f"wcodes{k}{m}", align_bytes=64)[:]
-            wscales[k, m] = keep.tile([P, 4 * P], U8, name=f"wscales{k}{m}", align_bytes=64)
-        xcodes = {0: keep.tile([P, S], U32, name="xcodes0", align_bytes=64)}
+        wcodes = [keep.tile([P, 2 * N], U32, name=f"wcodes{e}", align_bytes=64) for e in range(E + 1)]
+        wscales = [keep.tile([P, 2 * N], U8, name=f"wscales{e}", align_bytes=64) for e in range(E + 1)]
+        xcodes = [keep.tile([P, S], U32, name=f"xcodes{g}", align_bytes=64) for g in range(2)]
         xscales = [keep.tile([P, S], U8, name=f"xscales{g}", align_bytes=64) for g in range(2)]
         sscales = [keep.tile([P, T], U8, name=f"sscales{g}", align_bytes=64) for g in range(2)]
+        bias = keep.tile([P, 2, E + 1], F32, name="bias")
 
         ident = keep.tile([P, P], F32, name="ident")
         make_identity(nc, ident[:])
 
         x_raw, w_raw = {}, {}
-        X_AT = {(3, 0): 0, (3, 1): 4 * KIB, (2, 0): 8 * KIB, (2, 1): 12 * KIB, (1, 0): 16 * KIB, (1, 1): 20 * KIB,
-                (0, 0): 24 * KIB, (0, 1): 40 * KIB - LINK}
 
         def load_x(s):
             g, h = divmod(s, 2)
             rows = xT[K_PASS * g : K_PASS * (g + 1), :].rearrange("(p j) t -> p j t", j=4)
-            for i in range(2):
-                x_raw[s, i] = place(f"x_raw{s}{i}", X_AT[s, i], [P, 2, HALF], F32)
+            for i in (1, 0):
+                last = s == 0 and i == 0
+                x_raw[s, i] = place(f"x_raw{s}{i}", RAW_X + 8 * (3 - s) + 4 * (1 - i), [P, 2, HALF], F32, LINK if last else 0)
                 nc.sync.dma_start(x_raw[s, i][:], rows[:, 2 * h : 2 * h + 2, HALF * i : HALF * (i + 1)])
 
         def load_w(e):
-            w_raw[e] = stage.tile([P, 8 * N], F32, name="raw")
+            w_raw[e] = place(f"w_raw{e}", RAW_W + 8 * e, [P, 8 * N], F32)
             nc.sync.dma_start(
                 w_raw[e][:].rearrange("p (g j n) -> p g j n", g=2, j=4),
                 w[e].rearrange("(g p j) n -> p g j n", p=P, j=4),
@@ -82,15 +80,13 @@ def tile_moe_shr_lin_relu2_kernel(tc, xT, w, b, gate, offs, pos1, pos2, out):
 
         load_x(3)
         nc.sync.dma_start(offs_t[:], offs)
-        load_x(2)
-        load_w(0)
-        load_x(1)
-        load_x(0)
-        for e in range(1, E + 1):
+        for s in (2, 1, 0):
+            load_x(s)
+        for e in range(E):
             load_w(e)
-        bias = stage.tile([P, 2, E + 1], F32, name="raw")
         nc.sync.dma_start(bias[:], b.rearrange("(m p) e -> p m e", p=P))
-        gates = stage.tile([P, 2 * T], F32, name="raw")
+        load_w(E)
+        gates = place("gates", GATES, [P, 2 * T], F32)
         nc.sync.dma_start(gates[:].rearrange("p (r t) -> p r t", r=2), gate[:, 0:P, :].rearrange("r p t -> p r t"))
         nc.sync.dma_start(pos1_t[:], pos1)
         nc.sync.dma_start(pos2_t[:], pos2)
@@ -103,54 +99,40 @@ def tile_moe_shr_lin_relu2_kernel(tc, xT, w, b, gate, offs, pos1, pos2, out):
             copy(words.bitcast(BF16).rearrange("p (t e) -> p t e", e=2), x_raw[s, i][:].rearrange("p e t -> p t e"))
 
         w_bf = {}
-        W_AT = {(0, 0): 80, (0, 1): 84, (1, 0): 88, (1, 1): 92, (2, 0): 96, (3, 0): 100, (2, 1): 64, (3, 1): 68, (SHARED, 0): 72}
+        W_AT = [CAST_W, CAST_W + 4, CAST_W + 8, CAST_W + 12, PICKED + 8, PICKED + 12, PICKED + 16, PICKED + 20, RAW_W + 8 * 7 + 4]
 
-        def cast_w(e, m):
-            key, at = ((e // 2, m), e % 2) if e < E else ((SHARED, 0), m)
-            if key not in w_bf:
-                w_bf[key] = place(f"w_bf{key[0]}{key[1]}", W_AT[key] * KIB, [P, 16 * P], BF16)
-            dst = w_bf[key][:, 8 * P * at : 8 * P * (at + 1)]
-            if e < GPSIMD_WEIGHTS:
-                src = w_raw[e][:].rearrange("p (g j m c) -> p m g c j", g=2, j=4, m=2)[:, m]
-                gpsimd_copy(dst.rearrange("p (g c j) -> p g c j", g=2, j=4), src)
-            else:
-                src = w_raw[e][:].rearrange("p (g j m c i) -> p m g c j i", g=2, j=4, m=2, i=2)[:, m]
-                nc.scalar.copy(dst.rearrange("p (g c i j) -> p g c j i", g=2, i=2, j=4), src)
+        def cast_w(copy, e):
+            w_bf[e] = place(f"w_bf{e}", W_AT[e], [P, 8 * N], BF16)
+            src = w_raw[e][:].rearrange("p (g j c i) -> p g c j i", g=2, j=4, i=4)
+            copy(w_bf[e][:].rearrange("p (g c i j) -> p g c j i", g=2, i=4, j=4), src)
 
-        def after_gathers():
-            t = place("codes_after_gathers", 44 * KIB - 2 * LINK, [P, S + 8 * P], U32)
-            xcodes[1] = t[:, 0:S]
-            for m in range(2):
-                wcodes[0, m] = t[:, S + 4 * P * m : S + 4 * P * (m + 1)]
+        def cast_w_on_gpsimd(e):
+            w_bf[e] = place(f"w_bf{e}", W_AT[e], [P, 8 * N], BF16)
+            src = w_raw[e][:].rearrange("p (g j n) -> p g n j", g=2, j=4)
+            gpsimd_copy(w_bf[e][:].rearrange("p (g n j) -> p g n j", g=2, j=4), src)
 
-        def after_routed():
-            t = place("codes_after_routed", 100 * KIB, [P, 2 * T + 8 * P], U32)
-            scodes[0], scodes[1] = t[:, 0:T], t[:, T : 2 * T]
-            for i in range(2):
-                wcodes[2 + i, 1] = t[:, 2 * T + 4 * P * i : 2 * T + 4 * P * (i + 1)]
-
-        def quant_w(k, m):
-            nc.vector.quantize_mx(out=wcodes[k, m].bitcast(FP8X4), scales=wscales[k, m][:], in_=w_bf[k, m][:])
+        def quant_w(e):
+            nc.vector.quantize_mx(out=wcodes[e][:].bitcast(FP8X4), scales=wscales[e][:], in_=w_bf[e][:])
 
         picked = {}
-        PICKED_AT = {(1, 0): 56, (1, 1): 64, (0, 0): 72, (0, 1): 32}
+        PICKED_AT = {(0, 1): PICKED, (1, 0): PICKED + 8, (1, 1): PICKED + 16, (0, 0): PICKED + 24}
 
         def gather(s, c0, n):
             g, h = divmod(s, 2)
             i, c = divmod(c0, CHUNK)
             if (g, i) not in picked:
-                picked[g, i] = place(f"picked{g}{i}", PICKED_AT[g, i] * KIB, [P, 2 * CHUNK], U32)
+                picked[g, i] = place(f"picked{g}{i}", PICKED_AT[g, i], [P, 2 * CHUNK], U32)
             window = planes[:, s * T : min(s + 2, 4) * T]
             dst = picked[g, i][:, CHUNK * h + c : CHUNK * h + c + n]
             nc.vector.tensor_copy(dst, window.indirect(offs_t[:, c0 // 16 : (c0 + n) // 16]))
 
         def side_by_side_on_vector(dst, both):
             src = both.bitcast(BF16).rearrange("p h (c e) -> p c h e", e=2)
-            nc.vector.tensor_copy(dst[:].rearrange("p (c h e) -> p c h e", h=2, e=2), src)
+            nc.vector.tensor_copy(dst.rearrange("p (c h e) -> p c h e", h=2, e=2), src)
 
         def side_by_side_on_scalar(dst, both):
             nc.scalar.copy(
-                dst[:].bitcast(U32).rearrange("p (c i h) -> p c h i", i=2, h=2),
+                dst.bitcast(U32).rearrange("p (c i h) -> p c h i", i=2, h=2),
                 both.rearrange("p h (c i) -> p c h i", i=2),
             )
 
@@ -158,8 +140,8 @@ def tile_moe_shr_lin_relu2_kernel(tc, xT, w, b, gate, offs, pos1, pos2, out):
 
         def regroup(side_by_side, g, c0, n, kib):
             i, c = divmod(c0, CHUNK)
-            x_bf[g, c0] = place(f"x_bf{g}_{c0}", kib * KIB, [P, 4 * n], BF16)
-            side_by_side(x_bf[g, c0], picked[g, i][:].rearrange("p (h c) -> p h c", h=2)[:, :, c : c + n])
+            x_bf[g, c0] = place(f"x_bf{g}_{c0}", kib, [P, 4 * n], BF16)
+            side_by_side(x_bf[g, c0][:], picked[g, i][:].rearrange("p (h c) -> p h c", h=2)[:, :, c : c + n])
 
         def quant_x(g, c0, n):
             cols = slice(c0, c0 + n)
@@ -167,27 +149,27 @@ def tile_moe_shr_lin_relu2_kernel(tc, xT, w, b, gate, offs, pos1, pos2, out):
 
         banks = {}
 
-        def multiply(k, m):
-            banks[k, m] = psum.tile([P, BANK], F32, name="ps")
-            for i in range(2):
-                for g in (1, 0):
-                    w0 = 2 * P * i + P * g
-                    x0 = C * (2 * k + i)
-                    nc.tensor.matmul_mx(
-                        out=banks[k, m][:, C * i : C * (i + 1)],
-                        lhsT=wcodes[k, m][:, w0 : w0 + P].bitcast(FP8X4),
-                        lhsT_scale=wscales[k, m][:, w0 : w0 + P],
-                        rhs=xcodes[g][:, x0 : x0 + C].bitcast(FP8X4),
-                        rhs_scale=xscales[g][:, x0 : x0 + C],
-                        start=(g == 1),
-                        stop=(g == 0),
-                    )
+        def multiply(e, m):
+            k, i = divmod(e, 2)
+            if i == 0:
+                banks[k, m] = psum.tile([P, BANK], F32, name="ps")
+            for g in (1, 0):
+                w0 = N * g + P * m
+                nc.tensor.matmul_mx(
+                    out=banks[k, m][:, C * i : C * (i + 1)],
+                    lhsT=wcodes[e][:, w0 : w0 + P].bitcast(FP8X4),
+                    lhsT_scale=wscales[e][:, w0 : w0 + P],
+                    rhs=xcodes[g][:, C * e : C * (e + 1)].bitcast(FP8X4),
+                    rhs_scale=xscales[g][:, C * e : C * (e + 1)],
+                    start=(g == 1),
+                    stop=(g == 0),
+                )
 
         y = {}
 
         def relu(k, m):
             if m not in y:
-                y[m] = place(f"y{m}", (16 + 8 * m) * KIB, [P, S], F32)
+                y[m] = place(f"y{m}", RAW_X + 16 + 8 * m, [P, S], F32)
             for i in range(2):
                 e = 2 * k + i
                 nc.scalar.activation(
@@ -202,104 +184,102 @@ def tile_moe_shr_lin_relu2_kernel(tc, xT, w, b, gate, offs, pos1, pos2, out):
 
         s_bf = {}
 
-        def regroup_shared(side_by_side, g):
-            s_bf[g] = place(f"s_bf{g}", 8 * (1 - g) * KIB, [P, 4 * T], BF16)
-            side_by_side(s_bf[g], planes[:, 2 * g * T : 2 * (g + 1) * T].rearrange("p (h c) -> p h c", h=2))
+        def regroup_shared(g, i):
+            if g not in s_bf:
+                s_bf[g] = place(f"s_bf{g}", RAW_X + 8 * (1 - g), [P, 4 * T], BF16)
+            both = planes[:, 2 * g * T : 2 * (g + 1) * T].rearrange("p (h c) -> p h c", h=2)
+            side_by_side_on_scalar(s_bf[g][:, 4 * HALF * i : 4 * HALF * (i + 1)], both[:, :, HALF * i : HALF * (i + 1)])
 
         def quant_shared(g):
-            nc.vector.quantize_mx(out=scodes[g].bitcast(FP8X4), scales=sscales[g][:], in_=s_bf[g][:])
+            nc.vector.quantize_mx(out=scodes[:, T * g : T * (g + 1)].bitcast(FP8X4), scales=sscales[g][:], in_=s_bf[g][:])
 
         def multiply_shared(m, half):
-            banks[SHARED, m, half] = psum.tile([P, BANK], F32, name="ps")
-            cols = slice(BANK * half, BANK * (half + 1))
+            banks[PAIRS, m, half] = psum.tile([P, BANK], F32, name="ps")
             for g in (1, 0):
-                w0 = 2 * P * m + P * g
+                w0 = N * g + P * m
+                t0 = BANK * half
                 nc.tensor.matmul_mx(
-                    out=banks[SHARED, m, half][:],
-                    lhsT=wcodes[SHARED, 0][:, w0 : w0 + P].bitcast(FP8X4),
-                    lhsT_scale=wscales[SHARED, 0][:, w0 : w0 + P],
-                    rhs=scodes[g][:, cols].bitcast(FP8X4),
-                    rhs_scale=sscales[g][:, cols],
+                    out=banks[PAIRS, m, half][:],
+                    lhsT=wcodes[E][:, w0 : w0 + P].bitcast(FP8X4),
+                    lhsT_scale=wscales[E][:, w0 : w0 + P],
+                    rhs=scodes[:, T * g + t0 : T * g + t0 + BANK].bitcast(FP8X4),
+                    rhs_scale=sscales[g][:, t0 : t0 + BANK],
                     start=(g == 1),
                     stop=(g == 0),
                 )
 
-        cast_x(nc.vector.tensor_copy, 3, 0)
         cast_x(nc.vector.tensor_copy, 3, 1)
-        cast_x(nc.scalar.copy, 2, 0)
+        cast_x(nc.vector.tensor_copy, 3, 0)
         cast_x(nc.scalar.copy, 2, 1)
-        cast_w(0, 0)
-        cast_w(0, 1)
-        cast_x(nc.scalar.copy, 1, 0)
+        cast_x(gpsimd_copy, 2, 0)
+        regroup_shared(1, 1)
         cast_x(nc.scalar.copy, 1, 1)
-        cast_x(nc.scalar.copy, 0, 0)
-        cast_x(gpsimd_copy, 0, 1)
-        after_gathers()
-        for e in range(1, GPSIMD_WEIGHTS):
-            cast_w(e, 0)
-            cast_w(e, 1)
+        cast_x(gpsimd_copy, 1, 0)
+        regroup_shared(1, 0)
+        cast_x(nc.scalar.copy, 0, 1)
+        cast_x(gpsimd_copy, 0, 0)
+        regroup_shared(0, 1)
+        cast_w_on_gpsimd(0)
+        cast_w_on_gpsimd(1)
+        cast_w_on_gpsimd(3)
         for c0 in range(0, S, HALF):
             gather(3, c0, HALF)
         for c0 in range(0, S, CHUNK):
             gather(2, c0, CHUNK)
-        regroup_shared(side_by_side_on_scalar, 1)
-        regroup(side_by_side_on_scalar, 1, 0, CHUNK, 16)
-        regroup(side_by_side_on_scalar, 1, CHUNK, CHUNK, 24)
-        gather(1, 0, CHUNK)
-        gather(0, 0, CHUNK)
-        gather(1, CHUNK, CHUNK)
-        gather(0, 2 * BANK, BANK)
-        gather(0, 3 * BANK, BANK)
-        regroup_shared(side_by_side_on_scalar, 0)
-        regroup(side_by_side_on_scalar, 0, 0, CHUNK, 56)
-        for e in range(GPSIMD_WEIGHTS, E):
-            cast_w(e, 0)
-        quant_w(0, 0)
-        quant_w(1, 0)
+        for c0 in range(0, S, CHUNK):
+            gather(1, c0, CHUNK)
+            gather(0, c0, CHUNK)
+        regroup(side_by_side_on_scalar, 1, 0, CHUNK, RAW_X + 16)
+        regroup_shared(0, 0)
+        regroup(side_by_side_on_scalar, 1, CHUNK, CHUNK, RAW_X + 24)
+        cast_w(nc.scalar.copy, 2)
+        regroup(side_by_side_on_scalar, 0, 0, CHUNK, RAW_W + 8 * 2)
+        for e in range(4, E):
+            cast_w(nc.scalar.copy, e)
         quant_x(1, 0, CHUNK)
-        quant_x(0, 0, CHUNK)
+        quant_w(0)
         quant_x(1, CHUNK, CHUNK)
+        quant_w(1)
+        quant_w(2)
+        quant_x(0, 0, CHUNK)
+        quant_w(3)
         for k in (2, 3):
-            quant_w(k, 0)
-            regroup(side_by_side_on_vector, 0, BANK * k, BANK, W_AT[k, 0])
+            regroup(side_by_side_on_vector, 0, BANK * k, BANK, RAW_W + 8 * 2 * k)
+            quant_w(2 * k)
             quant_x(0, BANK * k, BANK)
-        for k in range(PAIRS):
-            multiply(k, 0)
-        after_routed()
-        for e in range(E):
-            if e >= GPSIMD_WEIGHTS:
-                cast_w(e, 1)
-            if e % 2 == 1:
-                quant_w(e // 2, 1)
+            quant_w(2 * k + 1)
+        cast_w(nc.vector.tensor_copy, E)
+        scodes = place("scodes", RAW_W + 8 * 7 - 4, [P, 2 * T], U32)
         quant_shared(1)
-        for k in range(PAIRS):
-            multiply(k, 1)
-        cast_w(E, 0)
-        cast_w(E, 1)
-        quant_w(SHARED, 0)
+        quant_w(E)
         quant_shared(0)
+        for e0 in range(0, E, 4):
+            for m in range(2):
+                for e in range(e0, e0 + 4):
+                    multiply(e, m)
 
         relu(0, 0)
         relu(1, 0)
-        relu(2, 0)
+        relu(0, 1)
         square(y_pairs(0, 0, 2))
+        relu(2, 0)
+        relu(1, 1)
         relu(3, 0)
-        square(y_pairs(0, 2, 3))
-        square(y_pairs(0, 3, 4))
-        for k in range(PAIRS):
-            relu(k, 1)
+        relu(2, 1)
+        square(y_pairs(0, 2, 4))
+        relu(3, 1)
         square(y_pairs(1, 0, 2))
         square(y_pairs(1, 2, 4))
         for m in range(2):
             for half in range(2):
                 multiply_shared(m, half)
-        ys_all = place("ys", 32 * KIB, [P, 2 * T], F32)
+        ys_all = place("ys", RAW_W, [P, 2 * T], F32)
 
         def ys(m, half):
             return ys_all[:, T * m + BANK * half : T * m + BANK * (half + 1)]
 
         def relu_shared(m, half):
-            nc.scalar.activation(ys(m, half), banks[SHARED, m, half][:], RELU, bias=bias[:, m, E : E + 1])
+            nc.scalar.activation(ys(m, half), banks[PAIRS, m, half][:], RELU, bias=bias[:, m, E : E + 1])
 
         relu_shared(0, 0)
         relu_shared(0, 1)
@@ -308,20 +288,22 @@ def tile_moe_shr_lin_relu2_kernel(tc, xT, w, b, gate, offs, pos1, pos2, out):
         square(ys(0, 1))
         square(ys(1, 0))
 
-        def fetch(dst, m, half, r):
-            c0, c1 = BANK * half, BANK * (half + 1)
+        def fetch(dst, m, half, r, first=0, count=BANK):
+            c0 = BANK * half + first
+            c1 = c0 + count
             weight = gates[:, T * r + c0 : T * r + c1]
             nc.vector.tensor_tensor(dst, y[m][:].indirect(pos[r][:, c0 // 16 : c1 // 16]), weight, MULT)
 
         def add_into(dst, other):
             nc.vector.tensor_tensor(dst, dst, other, ADD)
 
-        def store(m, half, src):
-            nc.sync.dma_start(out[m * P : (m + 1) * P, BANK * half : BANK * (half + 1)], src)
+        def store(m, half, src, first=0, count=BANK):
+            c0 = BANK * half + first
+            nc.sync.dma_start(out[m * P : (m + 1) * P, c0 : c0 + count], src)
 
         terms, turned = {}, {}
         for half in range(2):
-            t = place(f"terms{half}", 4 * half * KIB, [P, 2 * BANK], F32)
+            t = place(f"terms{half}", RAW_W + 8 + 4 * half, [P, 2 * BANK], F32)
             terms[half] = (t[:, 0:BANK], t[:, BANK : 2 * BANK])
             for r in range(2):
                 fetch(terms[half][r], 0, half, r)
@@ -352,7 +334,7 @@ def tile_moe_shr_lin_relu2_kernel(tc, xT, w, b, gate, offs, pos1, pos2, out):
         turn_back(1)
         square(ys(1, 1))
 
-        t = place("terms_last", 8 * KIB, [P, 3 * BANK], F32)
+        t = place("terms_last", RAW_W + 24, [P, 3 * BANK], F32)
         first0, second0, second1 = (t[:, BANK * i : BANK * (i + 1)] for i in range(3))
         first1 = ys(1, 0)
         fetch(first0, 1, 0, 0)
@@ -361,9 +343,11 @@ def tile_moe_shr_lin_relu2_kernel(tc, xT, w, b, gate, offs, pos1, pos2, out):
         fetch(first1, 1, 1, 0)
         add_into(first0, second0)
         store(1, 0, first0)
+        fetch(second1[:, 0:C], 1, 1, 1, 0, C)
         add_into(first1, ys(1, 1))
-        fetch(second1, 1, 1, 1)
+        fetch(second1[:, C:BANK], 1, 1, 1, C, C)
         store_turned(0)
         store_turned(1)
-        add_into(first1, second1)
-        store(1, 1, first1)
+        for c0 in (0, C):
+            add_into(first1[:, c0 : c0 + C], second1[:, c0 : c0 + C])
+            store(1, 1, first1[:, c0 : c0 + C], c0, C)

@@ -24,14 +24,16 @@ BANK = 512
 PAIRS = E // 2
 CHUNK = 1024
 HALF = T // 2
+THIRD = 384
 KIB = 1024
 LINK = 64
 
 RAW_X = 0
 PICKED = 32
-RAW_W = 64
-CAST_W = 136
-GATES = 152
+RAW_W = [64, 72, 80, 92, 100, 108, 116, 124, 132]
+CAST_W = 140
+GATES = PICKED
+LAST_PAIRS = 156
 
 
 def tile_moe_shr_lin_relu2_kernel(tc, xT, w, b, gate, offs, pos1, pos2, out):
@@ -67,12 +69,12 @@ def tile_moe_shr_lin_relu2_kernel(tc, xT, w, b, gate, offs, pos1, pos2, out):
             g, h = divmod(s, 2)
             rows = xT[K_PASS * g : K_PASS * (g + 1), :].rearrange("(p j) t -> p j t", j=4)
             for i in (1, 0):
-                last = s == 0 and i == 0
-                x_raw[s, i] = place(f"x_raw{s}{i}", RAW_X + 8 * (3 - s) + 4 * (1 - i), [P, 2, HALF], F32, LINK if last else 0)
+                kib, shift = (LAST_PAIRS + 4, -LINK) if s == 0 and i == 0 else (RAW_X + 8 * (3 - s) + 4 * (1 - i), 0)
+                x_raw[s, i] = place(f"x_raw{s}{i}", kib, [P, 2, HALF], F32, shift)
                 nc.sync.dma_start(x_raw[s, i][:], rows[:, 2 * h : 2 * h + 2, HALF * i : HALF * (i + 1)])
 
         def load_w(e):
-            w_raw[e] = place(f"w_raw{e}", RAW_W + 8 * e, [P, 8 * N], F32)
+            w_raw[e] = place(f"w_raw{e}", RAW_W[e], [P, 8 * N], F32)
             nc.sync.dma_start(
                 w_raw[e][:].rearrange("p (g j n) -> p g j n", g=2, j=4),
                 w[e].rearrange("(g p j) n -> p g j n", p=P, j=4),
@@ -99,7 +101,7 @@ def tile_moe_shr_lin_relu2_kernel(tc, xT, w, b, gate, offs, pos1, pos2, out):
             copy(words.bitcast(BF16).rearrange("p (t e) -> p t e", e=2), x_raw[s, i][:].rearrange("p e t -> p t e"))
 
         w_bf = {}
-        W_AT = [CAST_W, CAST_W + 4, CAST_W + 8, CAST_W + 12, PICKED + 8, PICKED + 12, PICKED + 16, PICKED + 20, RAW_W + 8 * 7 + 4]
+        W_AT = [CAST_W, CAST_W + 4, CAST_W + 8, CAST_W + 12, PICKED + 12, PICKED + 8, PICKED + 16, PICKED + 20, RAW_W[7] + 4]
 
         def cast_w(copy, e):
             w_bf[e] = place(f"w_bf{e}", W_AT[e], [P, 8 * N], BF16)
@@ -115,15 +117,23 @@ def tile_moe_shr_lin_relu2_kernel(tc, xT, w, b, gate, offs, pos1, pos2, out):
             nc.vector.quantize_mx(out=wcodes[e][:].bitcast(FP8X4), scales=wscales[e][:], in_=w_bf[e][:])
 
         picked = {}
-        PICKED_AT = {(0, 1): PICKED, (1, 0): PICKED + 8, (1, 1): PICKED + 16, (0, 0): PICKED + 24}
+        PICKED_AT = {
+            (1, 0): (CHUNK, PICKED + 8, 0),
+            (1, CHUNK): (CHUNK, PICKED + 16, 0),
+            (0, 0): (CHUNK, PICKED + 24, 0),
+            (0, 2 * BANK): (BANK, LAST_PAIRS, 0),
+            (0, 3 * BANK): (BANK, LAST_PAIRS + 8, -2 * LINK),
+        }
 
         def gather(s, c0, n):
             g, h = divmod(s, 2)
-            i, c = divmod(c0, CHUNK)
-            if (g, i) not in picked:
-                picked[g, i] = place(f"picked{g}{i}", PICKED_AT[g, i], [P, 2 * CHUNK], U32)
+            first = max(f for gg, f in PICKED_AT if gg == g and f <= c0)
+            width, kib, shift = PICKED_AT[g, first]
+            if (g, first) not in picked:
+                picked[g, first] = place(f"picked{g}_{first}", kib, [P, 2 * width], U32, shift)
             window = planes[:, s * T : min(s + 2, 4) * T]
-            dst = picked[g, i][:, CHUNK * h + c : CHUNK * h + c + n]
+            c = width * h + c0 - first
+            dst = picked[g, first][:, c : c + n]
             nc.vector.tensor_copy(dst, window.indirect(offs_t[:, c0 // 16 : (c0 + n) // 16]))
 
         def side_by_side_on_vector(dst, both):
@@ -138,10 +148,12 @@ def tile_moe_shr_lin_relu2_kernel(tc, xT, w, b, gate, offs, pos1, pos2, out):
 
         x_bf = {}
 
-        def regroup(side_by_side, g, c0, n, kib):
-            i, c = divmod(c0, CHUNK)
-            x_bf[g, c0] = place(f"x_bf{g}_{c0}", kib, [P, 4 * n], BF16)
-            side_by_side(x_bf[g, c0][:], picked[g, i][:].rearrange("p (h c) -> p h c", h=2)[:, :, c : c + n])
+        def side_by_side_on_gpsimd(dst, both):
+            nc.gpsimd.tensor_copy(dst.bitcast(U32).rearrange("p (c h) -> p c h", h=2), both.rearrange("p h c -> p c h"))
+
+        def regroup(side_by_side, g, c0, n, kib, shift=0):
+            x_bf[g, c0] = place(f"x_bf{g}_{c0}", kib, [P, 4 * n], BF16, shift)
+            side_by_side(x_bf[g, c0][:], picked[g, c0][:].rearrange("p (h c) -> p h c", h=2))
 
         def quant_x(g, c0, n):
             cols = slice(c0, c0 + n)
@@ -184,11 +196,11 @@ def tile_moe_shr_lin_relu2_kernel(tc, xT, w, b, gate, offs, pos1, pos2, out):
 
         s_bf = {}
 
-        def regroup_shared(g, i):
+        def regroup_shared(side_by_side, g, i):
             if g not in s_bf:
                 s_bf[g] = place(f"s_bf{g}", RAW_X + 8 * (1 - g), [P, 4 * T], BF16)
             both = planes[:, 2 * g * T : 2 * (g + 1) * T].rearrange("p (h c) -> p h c", h=2)
-            side_by_side_on_scalar(s_bf[g][:, 4 * HALF * i : 4 * HALF * (i + 1)], both[:, :, HALF * i : HALF * (i + 1)])
+            side_by_side(s_bf[g][:, 4 * HALF * i : 4 * HALF * (i + 1)], both[:, :, HALF * i : HALF * (i + 1)])
 
         def quant_shared(g):
             nc.vector.quantize_mx(out=scodes[:, T * g : T * (g + 1)].bitcast(FP8X4), scales=sscales[g][:], in_=s_bf[g][:])
@@ -212,13 +224,14 @@ def tile_moe_shr_lin_relu2_kernel(tc, xT, w, b, gate, offs, pos1, pos2, out):
         cast_x(nc.vector.tensor_copy, 3, 0)
         cast_x(nc.scalar.copy, 2, 1)
         cast_x(gpsimd_copy, 2, 0)
-        regroup_shared(1, 1)
+        regroup_shared(side_by_side_on_scalar, 1, 1)
+        regroup_shared(side_by_side_on_gpsimd, 1, 0)
         cast_x(nc.scalar.copy, 1, 1)
         cast_x(gpsimd_copy, 1, 0)
-        regroup_shared(1, 0)
         cast_x(nc.scalar.copy, 0, 1)
         cast_x(gpsimd_copy, 0, 0)
-        regroup_shared(0, 1)
+        regroup_shared(side_by_side_on_scalar, 0, 1)
+        regroup_shared(side_by_side_on_gpsimd, 0, 0)
         cast_w_on_gpsimd(0)
         cast_w_on_gpsimd(1)
         cast_w_on_gpsimd(3)
@@ -226,14 +239,14 @@ def tile_moe_shr_lin_relu2_kernel(tc, xT, w, b, gate, offs, pos1, pos2, out):
             gather(3, c0, HALF)
         for c0 in range(0, S, CHUNK):
             gather(2, c0, CHUNK)
-        for c0 in range(0, S, CHUNK):
-            gather(1, c0, CHUNK)
-            gather(0, c0, CHUNK)
+        for c0, n in ((0, CHUNK), (2 * BANK, BANK), (3 * BANK, BANK)):
+            gather(1, c0, n)
+            gather(0, c0, n)
         regroup(side_by_side_on_scalar, 1, 0, CHUNK, RAW_X + 16)
-        regroup_shared(0, 0)
         regroup(side_by_side_on_scalar, 1, CHUNK, CHUNK, RAW_X + 24)
         cast_w(nc.scalar.copy, 2)
-        regroup(side_by_side_on_scalar, 0, 0, CHUNK, RAW_W + 8 * 2)
+        regroup(side_by_side_on_scalar, 0, 0, CHUNK, RAW_W[2], -LINK)
+        regroup(side_by_side_on_scalar, 0, 2 * BANK, BANK, RAW_W[2] + 8, -LINK)
         for e in range(4, E):
             cast_w(nc.scalar.copy, e)
         quant_x(1, 0, CHUNK)
@@ -243,13 +256,15 @@ def tile_moe_shr_lin_relu2_kernel(tc, xT, w, b, gate, offs, pos1, pos2, out):
         quant_w(2)
         quant_x(0, 0, CHUNK)
         quant_w(3)
-        for k in (2, 3):
-            regroup(side_by_side_on_vector, 0, BANK * k, BANK, RAW_W + 8 * 2 * k)
-            quant_w(2 * k)
-            quant_x(0, BANK * k, BANK)
-            quant_w(2 * k + 1)
+        quant_x(0, 2 * BANK, BANK)
+        quant_w(4)
+        quant_w(5)
+        regroup(side_by_side_on_vector, 0, 3 * BANK, BANK, RAW_W[6])
+        quant_w(6)
+        quant_x(0, 3 * BANK, BANK)
+        quant_w(7)
         cast_w(nc.vector.tensor_copy, E)
-        scodes = place("scodes", RAW_W + 8 * 7 - 4, [P, 2 * T], U32)
+        scodes = place("scodes", RAW_W[7] - 4, [P, 2 * T], U32)
         quant_shared(1)
         quant_w(E)
         quant_shared(0)
@@ -260,20 +275,19 @@ def tile_moe_shr_lin_relu2_kernel(tc, xT, w, b, gate, offs, pos1, pos2, out):
 
         relu(0, 0)
         relu(1, 0)
-        relu(0, 1)
-        square(y_pairs(0, 0, 2))
         relu(2, 0)
-        relu(1, 1)
+        square(y_pairs(0, 0, 2))
         relu(3, 0)
-        relu(2, 1)
+        relu(0, 1)
         square(y_pairs(0, 2, 4))
-        relu(3, 1)
+        for k in range(1, PAIRS):
+            relu(k, 1)
         square(y_pairs(1, 0, 2))
         square(y_pairs(1, 2, 4))
         for m in range(2):
             for half in range(2):
                 multiply_shared(m, half)
-        ys_all = place("ys", RAW_W, [P, 2 * T], F32)
+        ys_all = place("ys", RAW_W[0], [P, 2 * T], F32)
 
         def ys(m, half):
             return ys_all[:, T * m + BANK * half : T * m + BANK * (half + 1)]
@@ -288,66 +302,71 @@ def tile_moe_shr_lin_relu2_kernel(tc, xT, w, b, gate, offs, pos1, pos2, out):
         square(ys(0, 1))
         square(ys(1, 0))
 
-        def fetch(dst, m, half, r, first=0, count=BANK):
-            c0 = BANK * half + first
-            c1 = c0 + count
-            weight = gates[:, T * r + c0 : T * r + c1]
-            nc.vector.tensor_tensor(dst, y[m][:].indirect(pos[r][:, c0 // 16 : c1 // 16]), weight, MULT)
+        def fetch(dst, r, m, c0, n):
+            weight = gates[:, T * r + c0 : T * r + c0 + n]
+            nc.vector.tensor_tensor(dst, y[m][:].indirect(pos[r][:, c0 // 16 : (c0 + n) // 16]), weight, MULT)
+
+        def shared_term(m, c0, n):
+            return ys_all[:, T * m + c0 : T * m + c0 + n]
 
         def add_into(dst, other):
             nc.vector.tensor_tensor(dst, dst, other, ADD)
 
-        def store(m, half, src, first=0, count=BANK):
-            c0 = BANK * half + first
-            nc.sync.dma_start(out[m * P : (m + 1) * P, c0 : c0 + count], src)
+        def store(src, m, c0, n):
+            nc.sync.dma_start(out[m * P : (m + 1) * P, c0 : c0 + n], src)
 
         terms, turned = {}, {}
-        for half in range(2):
-            t = place(f"terms{half}", RAW_W + 8 + 4 * half, [P, 2 * BANK], F32)
-            terms[half] = (t[:, 0:BANK], t[:, BANK : 2 * BANK])
+        units = [(0, 0, BANK), (0, BANK, BANK), (1, 0, THIRD)]
+        for i, u in enumerate(units):
+            t = place(f"terms{i}", RAW_W[1] + 4 * i, [P, 2 * u[2]], F32)
+            terms[u] = (t[:, 0 : u[2]], t[:, u[2] : 2 * u[2]])
             for r in range(2):
-                fetch(terms[half][r], 0, half, r)
+                fetch(terms[u][r], r, *u)
 
-        def sum_turned(half):
-            turned[half] = psum.tile([P, BANK], F32, name="ps")
-            for j in range(0, BANK, P):
-                for i, term in enumerate((*terms[half], ys(0, half))):
+        def sum_turned(u):
+            turned[u] = psum.tile([P, BANK], F32, name="ps")
+            for j in range(0, u[2], P):
+                for i, term in enumerate((*terms[u], shared_term(*u))):
                     nc.tensor.matmul(
-                        turned[half][:, j : j + P], term[:, j : j + P], ident[:],
+                        turned[u][:, j : j + P], term[:, j : j + P], ident[:],
                         start=(i == 0), stop=(i == 2), is_transpose=True,
                     )
 
-        def turn_back(half):
-            nc.scalar.copy(terms[half][1], turned[half][:])
-            turned[half] = psum.tile([P, BANK], F32, name="ps")
-            for j in range(0, BANK, P):
-                nc.tensor.transpose(turned[half][:, j : j + P], terms[half][1][:, j : j + P], ident[:])
+        def empty_turned(u):
+            nc.scalar.copy(terms[u][1], turned[u][:, 0 : u[2]])
 
-        def store_turned(half):
-            nc.scalar.copy(terms[half][0], turned[half][:])
-            store(0, half, terms[half][0])
+        def turn_back(u):
+            turned[u] = psum.tile([P, BANK], F32, name="ps")
+            for j in range(0, u[2], P):
+                nc.tensor.transpose(turned[u][:, j : j + P], terms[u][1][:, j : j + P], ident[:])
 
-        sum_turned(0)
-        sum_turned(1)
-        turn_back(0)
+        def store_turned(u):
+            nc.scalar.copy(terms[u][0], turned[u][:, 0 : u[2]])
+            store(terms[u][0], *u)
+
+        sum_turned(units[0])
+        sum_turned(units[1])
+        empty_turned(units[0])
+        turn_back(units[0])
         relu_shared(1, 1)
-        turn_back(1)
+        sum_turned(units[2])
+        empty_turned(units[1])
+        turn_back(units[1])
         square(ys(1, 1))
+        store_turned(units[0])
+        empty_turned(units[2])
+        turn_back(units[2])
+        store_turned(units[1])
+        store_turned(units[2])
 
-        t = place("terms_last", RAW_W + 24, [P, 3 * BANK], F32)
-        first0, second0, second1 = (t[:, BANK * i : BANK * (i + 1)] for i in range(3))
-        first1 = ys(1, 0)
-        fetch(first0, 1, 0, 0)
-        fetch(second0, 1, 0, 1)
-        add_into(first0, ys(1, 0))
-        fetch(first1, 1, 1, 0)
-        add_into(first0, second0)
-        store(1, 0, first0)
-        fetch(second1[:, 0:C], 1, 1, 1, 0, C)
-        add_into(first1, ys(1, 1))
-        fetch(second1[:, C:BANK], 1, 1, 1, C, C)
-        store_turned(0)
-        store_turned(1)
-        for c0 in (0, C):
-            add_into(first1[:, c0 : c0 + C], second1[:, c0 : c0 + C])
-            store(1, 1, first1[:, c0 : c0 + C], c0, C)
+        rest = T - THIRD
+        t = place("terms_last", RAW_W[3], [P, 2 * rest], F32)
+        first, second = t[:, 0:rest], t[:, rest : 2 * rest]
+        pieces = ((0, rest - C), (rest - C, C))
+        fetch(first, 0, 1, THIRD, rest)
+        fetch(second[:, 0 : rest - C], 1, 1, THIRD, rest - C)
+        add_into(first, shared_term(1, THIRD, rest))
+        fetch(second[:, rest - C : rest], 1, 1, T - C, C)
+        for c0, n in pieces:
+            add_into(first[:, c0 : c0 + n], second[:, c0 : c0 + n])
+            store(first[:, c0 : c0 + n], 1, THIRD + c0, n)

@@ -24,7 +24,8 @@ BANK = 512
 PAIRS = E // 2
 CHUNK = 1024
 HALF = T // 2
-THIRD = 384
+THIRD = 256
+FIRST_CUT = 384
 KIB = 1024
 LINK = 64
 
@@ -55,7 +56,9 @@ def tile_moe_shr_lin_relu2_kernel(tc, xT, w, b, gate, offs, pos1, pos2, out):
         planes = keep.tile([P, 4 * T], U32, name="planes")
         wcodes = [keep.tile([P, 2 * N], U32, name=f"wcodes{e}", align_bytes=64) for e in range(E + 1)]
         wscales = [keep.tile([P, 2 * N], U8, name=f"wscales{e}", align_bytes=64) for e in range(E + 1)]
-        xcodes = [keep.tile([P, S], U32, name=f"xcodes{g}", align_bytes=64) for g in range(2)]
+        xcodes = {
+            (g, i): keep.tile([P, CHUNK], U32, name=f"xcodes{g}{i}", align_bytes=64) for g, i in ((0, 0), (0, 1), (1, 0))
+        }
         xscales = [keep.tile([P, S], U8, name=f"xscales{g}", align_bytes=64) for g in range(2)]
         sscales = [keep.tile([P, T], U8, name=f"sscales{g}", align_bytes=64) for g in range(2)]
         bias = keep.tile([P, 2, E + 1], F32, name="bias")
@@ -65,13 +68,18 @@ def tile_moe_shr_lin_relu2_kernel(tc, xT, w, b, gate, offs, pos1, pos2, out):
 
         x_raw, w_raw = {}, {}
 
+        def piece(s, i):
+            cut = FIRST_CUT if s == 3 else HALF
+            return (cut, T) if i else (0, cut)
+
         def load_x(s):
             g, h = divmod(s, 2)
             rows = xT[K_PASS * g : K_PASS * (g + 1), :].rearrange("(p j) t -> p j t", j=4)
             for i in (1, 0):
-                kib, shift = (LAST_PAIRS + 4, -LINK) if s == 0 and i == 0 else (RAW_X + 8 * (3 - s) + 4 * (1 - i), 0)
-                x_raw[s, i] = place(f"x_raw{s}{i}", kib, [P, 2, HALF], F32, shift)
-                nc.sync.dma_start(x_raw[s, i][:], rows[:, 2 * h : 2 * h + 2, HALF * i : HALF * (i + 1)])
+                c0, c1 = piece(s, i)
+                kib, shift = (LAST_PAIRS + 4, -LINK) if s == 0 and i == 0 else (RAW_X + 8 * (3 - s), 8 * (T - c1))
+                x_raw[s, i] = place(f"x_raw{s}{i}", kib, [P, 2, c1 - c0], F32, shift)
+                nc.sync.dma_start(x_raw[s, i][:], rows[:, 2 * h : 2 * h + 2, c0:c1])
 
         def load_w(e):
             w_raw[e] = place(f"w_raw{e}", RAW_W[e], [P, 8 * N], F32)
@@ -97,11 +105,12 @@ def tile_moe_shr_lin_relu2_kernel(tc, xT, w, b, gate, offs, pos1, pos2, out):
             nc.gpsimd.tensor_scalar(dst, src, 1.0, 0.0, MULT, ADD)
 
         def cast_x(copy, s, i):
-            words = planes[:, s * T + HALF * i : s * T + HALF * (i + 1)]
+            c0, c1 = piece(s, i)
+            words = planes[:, s * T + c0 : s * T + c1]
             copy(words.bitcast(BF16).rearrange("p (t e) -> p t e", e=2), x_raw[s, i][:].rearrange("p e t -> p t e"))
 
         w_bf = {}
-        W_AT = [CAST_W, CAST_W + 4, CAST_W + 8, CAST_W + 12, PICKED + 12, PICKED + 8, PICKED + 16, PICKED + 20, RAW_W[7] + 4]
+        W_AT = [CAST_W, CAST_W + 4, CAST_W + 8, CAST_W + 12, PICKED + 12, PICKED + 8, PICKED + 16, PICKED + 20]
 
         def cast_w(copy, e):
             w_bf[e] = place(f"w_bf{e}", W_AT[e], [P, 8 * N], BF16)
@@ -112,6 +121,15 @@ def tile_moe_shr_lin_relu2_kernel(tc, xT, w, b, gate, offs, pos1, pos2, out):
             w_bf[e] = place(f"w_bf{e}", W_AT[e], [P, 8 * N], BF16)
             src = w_raw[e][:].rearrange("p (g j n) -> p g n j", g=2, j=4)
             gpsimd_copy(w_bf[e][:].rearrange("p (g n j) -> p g n j", g=2, j=4), src)
+
+        def cast_shared_w(copy, g, kib):
+            w_bf[E, g] = place(f"w_bf{E}{g}", kib, [P, 4 * N], BF16)
+            src = w_raw[E][:, 4 * N * g : 4 * N * (g + 1)].rearrange("p (j c i) -> p c j i", j=4, i=4)
+            copy(w_bf[E, g][:].rearrange("p (c i j) -> p c j i", i=4, j=4), src)
+
+        def quant_shared_w(g):
+            cols = slice(N * g, N * (g + 1))
+            nc.vector.quantize_mx(out=wcodes[E][:, cols].bitcast(FP8X4), scales=wscales[E][:, cols], in_=w_bf[E, g][:])
 
         def quant_w(e):
             nc.vector.quantize_mx(out=wcodes[e][:].bitcast(FP8X4), scales=wscales[e][:], in_=w_bf[e][:])
@@ -155,9 +173,13 @@ def tile_moe_shr_lin_relu2_kernel(tc, xT, w, b, gate, offs, pos1, pos2, out):
             x_bf[g, c0] = place(f"x_bf{g}_{c0}", kib, [P, 4 * n], BF16, shift)
             side_by_side(x_bf[g, c0][:], picked[g, c0][:].rearrange("p (h c) -> p h c", h=2))
 
+        def slot_codes(g, c0, n):
+            i, c = divmod(c0, CHUNK)
+            return xcodes[g, i][:, c : c + n]
+
         def quant_x(g, c0, n):
             cols = slice(c0, c0 + n)
-            nc.vector.quantize_mx(out=xcodes[g][:, cols].bitcast(FP8X4), scales=xscales[g][:, cols], in_=x_bf[g, c0][:])
+            nc.vector.quantize_mx(out=slot_codes(g, c0, n).bitcast(FP8X4), scales=xscales[g][:, cols], in_=x_bf[g, c0][:])
 
         banks = {}
 
@@ -171,7 +193,7 @@ def tile_moe_shr_lin_relu2_kernel(tc, xT, w, b, gate, offs, pos1, pos2, out):
                     out=banks[k, m][:, C * i : C * (i + 1)],
                     lhsT=wcodes[e][:, w0 : w0 + P].bitcast(FP8X4),
                     lhsT_scale=wscales[e][:, w0 : w0 + P],
-                    rhs=xcodes[g][:, C * e : C * (e + 1)].bitcast(FP8X4),
+                    rhs=slot_codes(g, C * e, C).bitcast(FP8X4),
                     rhs_scale=xscales[g][:, C * e : C * (e + 1)],
                     start=(g == 1),
                     stop=(g == 0),
@@ -234,7 +256,6 @@ def tile_moe_shr_lin_relu2_kernel(tc, xT, w, b, gate, offs, pos1, pos2, out):
         regroup_shared(side_by_side_on_gpsimd, 0, 0)
         cast_w_on_gpsimd(0)
         cast_w_on_gpsimd(1)
-        cast_w_on_gpsimd(3)
         for c0 in range(0, S, HALF):
             gather(3, c0, HALF)
         for c0 in range(0, S, CHUNK):
@@ -245,17 +266,19 @@ def tile_moe_shr_lin_relu2_kernel(tc, xT, w, b, gate, offs, pos1, pos2, out):
         regroup(side_by_side_on_scalar, 1, 0, CHUNK, RAW_X + 16)
         regroup(side_by_side_on_scalar, 1, CHUNK, CHUNK, RAW_X + 24)
         cast_w(nc.scalar.copy, 2)
-        regroup(side_by_side_on_scalar, 0, 0, CHUNK, RAW_W[2], -LINK)
-        regroup(side_by_side_on_scalar, 0, 2 * BANK, BANK, RAW_W[2] + 8, -LINK)
-        for e in range(4, E):
+        regroup(side_by_side_on_gpsimd, 0, 0, CHUNK, RAW_W[0], LINK)
+        regroup(side_by_side_on_gpsimd, 0, 2 * BANK, BANK, RAW_W[1], LINK)
+        for e in range(3, E):
             cast_w(nc.scalar.copy, e)
+        cast_shared_w(nc.scalar.copy, 1, RAW_W[2])
         quant_x(1, 0, CHUNK)
         quant_w(0)
-        quant_x(1, CHUNK, CHUNK)
         quant_w(1)
         quant_w(2)
         quant_x(0, 0, CHUNK)
         quant_w(3)
+        xcodes[1, 1] = place("xcodes11", RAW_W[3], [P, CHUNK], U32)
+        quant_x(1, CHUNK, CHUNK)
         quant_x(0, 2 * BANK, BANK)
         quant_w(4)
         quant_w(5)
@@ -263,10 +286,11 @@ def tile_moe_shr_lin_relu2_kernel(tc, xT, w, b, gate, offs, pos1, pos2, out):
         quant_w(6)
         quant_x(0, 3 * BANK, BANK)
         quant_w(7)
-        cast_w(nc.vector.tensor_copy, E)
+        cast_shared_w(nc.vector.tensor_copy, 0, RAW_W[7] + 4)
         scodes = place("scodes", RAW_W[7] - 4, [P, 2 * T], U32)
         quant_shared(1)
-        quant_w(E)
+        quant_shared_w(1)
+        quant_shared_w(0)
         quant_shared(0)
         for e0 in range(0, E, 4):
             for m in range(2):
@@ -275,13 +299,15 @@ def tile_moe_shr_lin_relu2_kernel(tc, xT, w, b, gate, offs, pos1, pos2, out):
 
         relu(0, 0)
         relu(1, 0)
-        relu(2, 0)
-        square(y_pairs(0, 0, 2))
-        relu(3, 0)
         relu(0, 1)
-        square(y_pairs(0, 2, 4))
-        for k in range(1, PAIRS):
-            relu(k, 1)
+        square(y_pairs(0, 0, 2))
+        relu(2, 0)
+        relu(1, 1)
+        relu(3, 0)
+        square(y_pairs(0, 2, 3))
+        square(y_pairs(0, 3, 4))
+        relu(2, 1)
+        relu(3, 1)
         square(y_pairs(1, 0, 2))
         square(y_pairs(1, 2, 4))
         for m in range(2):
@@ -312,8 +338,8 @@ def tile_moe_shr_lin_relu2_kernel(tc, xT, w, b, gate, offs, pos1, pos2, out):
         def add_into(dst, other):
             nc.vector.tensor_tensor(dst, dst, other, ADD)
 
-        def store(src, m, c0, n):
-            nc.sync.dma_start(out[m * P : (m + 1) * P, c0 : c0 + n], src)
+        def store(queue, src, m, c0, n):
+            queue.dma_start(out[m * P : (m + 1) * P, c0 : c0 + n], src)
 
         terms, turned = {}, {}
         units = [(0, 0, BANK), (0, BANK, BANK), (1, 0, THIRD)]
@@ -342,7 +368,7 @@ def tile_moe_shr_lin_relu2_kernel(tc, xT, w, b, gate, offs, pos1, pos2, out):
 
         def store_turned(u):
             nc.scalar.copy(terms[u][0], turned[u][:, 0 : u[2]])
-            store(terms[u][0], *u)
+            store(nc.scalar, terms[u][0], *u)
 
         sum_turned(units[0])
         sum_turned(units[1])
@@ -369,4 +395,4 @@ def tile_moe_shr_lin_relu2_kernel(tc, xT, w, b, gate, offs, pos1, pos2, out):
         fetch(second[:, rest - C : rest], 1, 1, T - C, C)
         for c0, n in pieces:
             add_into(first[:, c0 : c0 + n], second[:, c0 : c0 + n])
-            store(first[:, c0 : c0 + n], 1, THIRD + c0, n)
+            store(nc.sync, first[:, c0 : c0 + n], 1, THIRD + c0, n)

@@ -24,7 +24,7 @@ BANK = 512
 PAIRS = E // 2
 CHUNK = 1024
 HALF = T // 2
-THIRD = 256
+THIRD = 384
 FIRST_CUT = 384
 KIB = 1024
 LINK = 64
@@ -75,11 +75,17 @@ def tile_moe_shr_lin_relu2_kernel(tc, xT, w, b, gate, offs, pos1, pos2, out):
         def load_x(s):
             g, h = divmod(s, 2)
             rows = xT[K_PASS * g : K_PASS * (g + 1), :].rearrange("(p j) t -> p j t", j=4)
+            if s in (2, 1):
+                whole = place(f"x_raw{s}", RAW_X + 8 * (3 - s), [P, 2, T], F32)
+                nc.sync.dma_start(whole[:], rows[:, 2 * h : 2 * h + 2, :])
+                for i in range(2):
+                    x_raw[s, i] = whole[:, :, HALF * i : HALF * (i + 1)]
+                return
             for i in (1, 0):
                 c0, c1 = piece(s, i)
                 kib, shift = (LAST_PAIRS + 4, -LINK) if s == 0 and i == 0 else (RAW_X + 8 * (3 - s), 8 * (T - c1))
-                x_raw[s, i] = place(f"x_raw{s}{i}", kib, [P, 2, c1 - c0], F32, shift)
-                nc.sync.dma_start(x_raw[s, i][:], rows[:, 2 * h : 2 * h + 2, c0:c1])
+                x_raw[s, i] = place(f"x_raw{s}{i}", kib, [P, 2, c1 - c0], F32, shift)[:]
+                nc.sync.dma_start(x_raw[s, i], rows[:, 2 * h : 2 * h + 2, c0:c1])
 
         def load_w(e):
             w_raw[e] = place(f"w_raw{e}", RAW_W[e], [P, 8 * N], F32)
@@ -107,10 +113,10 @@ def tile_moe_shr_lin_relu2_kernel(tc, xT, w, b, gate, offs, pos1, pos2, out):
         def cast_x(copy, s, i):
             c0, c1 = piece(s, i)
             words = planes[:, s * T + c0 : s * T + c1]
-            copy(words.bitcast(BF16).rearrange("p (t e) -> p t e", e=2), x_raw[s, i][:].rearrange("p e t -> p t e"))
+            copy(words.bitcast(BF16).rearrange("p (t e) -> p t e", e=2), x_raw[s, i].rearrange("p e t -> p t e"))
 
         w_bf = {}
-        W_AT = [CAST_W, CAST_W + 4, CAST_W + 8, CAST_W + 12, PICKED + 12, PICKED + 8, PICKED + 16, PICKED + 20]
+        W_AT = [CAST_W, CAST_W + 4, CAST_W + 8, CAST_W + 12, PICKED + 12, PICKED + 8, PICKED + 16, PICKED + 20, RAW_W[7] + 4]
 
         def cast_w(copy, e):
             w_bf[e] = place(f"w_bf{e}", W_AT[e], [P, 8 * N], BF16)
@@ -121,15 +127,6 @@ def tile_moe_shr_lin_relu2_kernel(tc, xT, w, b, gate, offs, pos1, pos2, out):
             w_bf[e] = place(f"w_bf{e}", W_AT[e], [P, 8 * N], BF16)
             src = w_raw[e][:].rearrange("p (g j n) -> p g n j", g=2, j=4)
             gpsimd_copy(w_bf[e][:].rearrange("p (g n j) -> p g n j", g=2, j=4), src)
-
-        def cast_shared_w(copy, g, kib):
-            w_bf[E, g] = place(f"w_bf{E}{g}", kib, [P, 4 * N], BF16)
-            src = w_raw[E][:, 4 * N * g : 4 * N * (g + 1)].rearrange("p (j c i) -> p c j i", j=4, i=4)
-            copy(w_bf[E, g][:].rearrange("p (c i j) -> p c j i", i=4, j=4), src)
-
-        def quant_shared_w(g):
-            cols = slice(N * g, N * (g + 1))
-            nc.vector.quantize_mx(out=wcodes[E][:, cols].bitcast(FP8X4), scales=wscales[E][:, cols], in_=w_bf[E, g][:])
 
         def quant_w(e):
             nc.vector.quantize_mx(out=wcodes[e][:].bitcast(FP8X4), scales=wscales[e][:], in_=w_bf[e][:])
@@ -256,6 +253,7 @@ def tile_moe_shr_lin_relu2_kernel(tc, xT, w, b, gate, offs, pos1, pos2, out):
         regroup_shared(side_by_side_on_gpsimd, 0, 0)
         cast_w_on_gpsimd(0)
         cast_w_on_gpsimd(1)
+        cast_w_on_gpsimd(3)
         for c0 in range(0, S, HALF):
             gather(3, c0, HALF)
         for c0 in range(0, S, CHUNK):
@@ -266,18 +264,17 @@ def tile_moe_shr_lin_relu2_kernel(tc, xT, w, b, gate, offs, pos1, pos2, out):
         regroup(side_by_side_on_scalar, 1, 0, CHUNK, RAW_X + 16)
         regroup(side_by_side_on_scalar, 1, CHUNK, CHUNK, RAW_X + 24)
         cast_w(nc.scalar.copy, 2)
-        regroup(side_by_side_on_gpsimd, 0, 0, CHUNK, RAW_W[0], LINK)
-        regroup(side_by_side_on_gpsimd, 0, 2 * BANK, BANK, RAW_W[1], LINK)
-        for e in range(3, E):
+        regroup(side_by_side_on_scalar, 0, 0, CHUNK, RAW_W[2], -LINK)
+        regroup(side_by_side_on_scalar, 0, 2 * BANK, BANK, RAW_W[2] + 8, -LINK)
+        for e in range(4, E):
             cast_w(nc.scalar.copy, e)
-        cast_shared_w(nc.scalar.copy, 1, RAW_W[2])
         quant_x(1, 0, CHUNK)
         quant_w(0)
         quant_w(1)
         quant_w(2)
         quant_x(0, 0, CHUNK)
         quant_w(3)
-        xcodes[1, 1] = place("xcodes11", RAW_W[3], [P, CHUNK], U32)
+        xcodes[1, 1] = place("xcodes11", LAST_PAIRS, [P, CHUNK], U32)
         quant_x(1, CHUNK, CHUNK)
         quant_x(0, 2 * BANK, BANK)
         quant_w(4)
@@ -286,11 +283,10 @@ def tile_moe_shr_lin_relu2_kernel(tc, xT, w, b, gate, offs, pos1, pos2, out):
         quant_w(6)
         quant_x(0, 3 * BANK, BANK)
         quant_w(7)
-        cast_shared_w(nc.vector.tensor_copy, 0, RAW_W[7] + 4)
+        cast_w(nc.vector.tensor_copy, E)
         scodes = place("scodes", RAW_W[7] - 4, [P, 2 * T], U32)
         quant_shared(1)
-        quant_shared_w(1)
-        quant_shared_w(0)
+        quant_w(E)
         quant_shared(0)
         for e0 in range(0, E, 4):
             for m in range(2):
@@ -338,14 +334,13 @@ def tile_moe_shr_lin_relu2_kernel(tc, xT, w, b, gate, offs, pos1, pos2, out):
         def add_into(dst, other):
             nc.vector.tensor_tensor(dst, dst, other, ADD)
 
-        def store(queue, src, m, c0, n):
-            queue.dma_start(out[m * P : (m + 1) * P, c0 : c0 + n], src)
+        def store(src, m, c0, n):
+            nc.sync.dma_start(out[m * P : (m + 1) * P, c0 : c0 + n], src)
 
         terms, turned = {}, {}
         units = [(0, 0, BANK), (0, BANK, BANK), (1, 0, THIRD)]
         for i, u in enumerate(units):
-            t = place(f"terms{i}", RAW_W[1] + 4 * i, [P, 2 * u[2]], F32)
-            terms[u] = (t[:, 0 : u[2]], t[:, u[2] : 2 * u[2]])
+            terms[u] = [place(f"terms{i}{r}", RAW_W[1] + 4 * i + 2 * r, [P, u[2]], F32)[:] for r in range(2)]
             for r in range(2):
                 fetch(terms[u][r], r, *u)
 
@@ -368,7 +363,7 @@ def tile_moe_shr_lin_relu2_kernel(tc, xT, w, b, gate, offs, pos1, pos2, out):
 
         def store_turned(u):
             nc.scalar.copy(terms[u][0], turned[u][:, 0 : u[2]])
-            store(nc.scalar, terms[u][0], *u)
+            store(terms[u][0], *u)
 
         sum_turned(units[0])
         sum_turned(units[1])
@@ -393,6 +388,8 @@ def tile_moe_shr_lin_relu2_kernel(tc, xT, w, b, gate, offs, pos1, pos2, out):
         fetch(second[:, 0 : rest - C], 1, 1, THIRD, rest - C)
         add_into(first, shared_term(1, THIRD, rest))
         fetch(second[:, rest - C : rest], 1, 1, T - C, C)
+        total = place("total", RAW_W[1] + 4 * 2 + 2, [P, rest], F32)
         for c0, n in pieces:
-            add_into(first[:, c0 : c0 + n], second[:, c0 : c0 + n])
-            store(nc.sync, first[:, c0 : c0 + n], 1, THIRD + c0, n)
+            cols = slice(c0, c0 + n)
+            nc.vector.tensor_tensor(total[:, cols], first[:, cols], second[:, cols], ADD)
+            store(total[:, cols], 1, THIRD + c0, n)

@@ -120,8 +120,8 @@ def tile_moe_shr_lin_relu2_kernel(tc, xT, w, b, gate, offs, pos1, pos2, out):
 
         def cast_w(copy, e):
             w_bf[e] = place(f"w_bf{e}", W_AT[e], [P, 8 * N], BF16)
-            src = w_raw[e][:].rearrange("p (g j c i) -> p g c j i", g=2, j=4, i=4)
-            copy(w_bf[e][:].rearrange("p (g c i j) -> p g c j i", g=2, i=4, j=4), src)
+            src = w_raw[e][:].rearrange("p (g j c i) -> p g c j i", g=2, j=4, i=2)
+            copy(w_bf[e][:].rearrange("p (g c i j) -> p g c j i", g=2, i=2, j=4), src)
 
         def cast_w_on_gpsimd(e):
             w_bf[e] = place(f"w_bf{e}", W_AT[e], [P, 8 * N], BF16)

@@ -25,16 +25,23 @@ PAIRS = E // 2
 CHUNK = 1024
 HALF = T // 2
 THIRD = 384
-FIRST_CUT = 384
+LOADS = {3: ((384, T), (0, 384)), 2: ((0, T),), 0: ((0, T),), 1: ((0, 640), (640, T))}
+ON_SCALAR = {2: (HALF, T), 0: (0, HALF), 1: (0, 640)}
+ON_GPSIMD = {2: (0, HALF), 0: (HALF, T), 1: (640, T)}
 KIB = 1024
-LINK = 64
 
-RAW_X = 0
-PICKED = 32
-RAW_W = [64, 72, 80, 92, 100, 108, 116, 124, 132]
-CAST_W = 140
-GATES = PICKED
-LAST_PAIRS = 156
+RAW_X = {2: 0, 1: 8, 0: 16, 3: 24}
+SHARED_BF = {1: 160, 0: 32}
+PICKED = {(1, 0): 40, (1, 1024): 48, (0, 0): 56, (0, 512): 60, (0, 1024): 64, (0, 1536): 68}
+RAW_W = [72 + 8 * e for e in range(E + 1)]
+CAST_W = [144, 148, 152, 156, 40, 44, 48, 52, RAW_W[1] + 4]
+SLOT_BF = {(1, 0): 6, (1, 1024): 14, (0, 0): RAW_W[0], (0, 512): RAW_W[0] + 4, (0, 1024): RAW_W[1], (0, 1536): RAW_W[4]}
+SHARED_CODES = RAW_W[7]
+GATES = RAW_W[2]
+Y = [RAW_W[3], 56]
+YS = 64
+TERMS = RAW_W[5]
+TERMS_LAST = 144
 
 
 def tile_moe_shr_lin_relu2_kernel(tc, xT, w, b, gate, offs, pos1, pos2, out):
@@ -56,9 +63,7 @@ def tile_moe_shr_lin_relu2_kernel(tc, xT, w, b, gate, offs, pos1, pos2, out):
         planes = keep.tile([P, 4 * T], U32, name="planes")
         wcodes = [keep.tile([P, 2 * N], U32, name=f"wcodes{e}", align_bytes=64) for e in range(E + 1)]
         wscales = [keep.tile([P, 2 * N], U8, name=f"wscales{e}", align_bytes=64) for e in range(E + 1)]
-        xcodes = {
-            (g, i): keep.tile([P, CHUNK], U32, name=f"xcodes{g}{i}", align_bytes=64) for g, i in ((0, 0), (0, 1), (1, 0))
-        }
+        xcodes = [keep.tile([P, S], U32, name=f"xcodes{g}", align_bytes=64) for g in range(2)]
         xscales = [keep.tile([P, S], U8, name=f"xscales{g}", align_bytes=64) for g in range(2)]
         sscales = [keep.tile([P, T], U8, name=f"sscales{g}", align_bytes=64) for g in range(2)]
         bias = keep.tile([P, 2, E + 1], F32, name="bias")
@@ -68,24 +73,14 @@ def tile_moe_shr_lin_relu2_kernel(tc, xT, w, b, gate, offs, pos1, pos2, out):
 
         x_raw, w_raw = {}, {}
 
-        def piece(s, i):
-            cut = FIRST_CUT if s == 3 else HALF
-            return (cut, T) if i else (0, cut)
-
         def load_x(s):
             g, h = divmod(s, 2)
             rows = xT[K_PASS * g : K_PASS * (g + 1), :].rearrange("(p j) t -> p j t", j=4)
-            if s in (2, 1):
-                whole = place(f"x_raw{s}", RAW_X + 8 * (3 - s), [P, 2, T], F32)
-                nc.sync.dma_start(whole[:], rows[:, 2 * h : 2 * h + 2, :])
-                for i in range(2):
-                    x_raw[s, i] = whole[:, :, HALF * i : HALF * (i + 1)]
-                return
-            for i in (1, 0):
-                c0, c1 = piece(s, i)
-                kib, shift = (LAST_PAIRS + 4, -LINK) if s == 0 and i == 0 else (RAW_X + 8 * (3 - s), 8 * (T - c1))
-                x_raw[s, i] = place(f"x_raw{s}{i}", kib, [P, 2, c1 - c0], F32, shift)[:]
-                nc.sync.dma_start(x_raw[s, i], rows[:, 2 * h : 2 * h + 2, c0:c1])
+            shift = 0
+            for c0, c1 in LOADS[s]:
+                x_raw[s, c0, c1] = place(f"x_raw{s}_{c0}", RAW_X[s], [P, 2, c1 - c0], F32, shift)
+                nc.sync.dma_start(x_raw[s, c0, c1][:], rows[:, 2 * h : 2 * h + 2, c0:c1])
+                shift += 8 * (c1 - c0)
 
         def load_w(e):
             w_raw[e] = place(f"w_raw{e}", RAW_W[e], [P, 8 * N], F32)
@@ -96,7 +91,7 @@ def tile_moe_shr_lin_relu2_kernel(tc, xT, w, b, gate, offs, pos1, pos2, out):
 
         load_x(3)
         nc.sync.dma_start(offs_t[:], offs)
-        for s in (2, 1, 0):
+        for s in (2, 0, 1):
             load_x(s)
         for e in range(E):
             load_w(e)
@@ -110,50 +105,36 @@ def tile_moe_shr_lin_relu2_kernel(tc, xT, w, b, gate, offs, pos1, pos2, out):
         def gpsimd_copy(dst, src):
             nc.gpsimd.tensor_scalar(dst, src, 1.0, 0.0, MULT, ADD)
 
-        def cast_x(copy, s, i):
-            c0, c1 = piece(s, i)
+        def cast_x(copy, s, c0, c1):
+            l0, l1 = [(a, z) for a, z in LOADS[s] if a <= c0 < z][0]
             words = planes[:, s * T + c0 : s * T + c1]
-            copy(words.bitcast(BF16).rearrange("p (t e) -> p t e", e=2), x_raw[s, i].rearrange("p e t -> p t e"))
+            rows = x_raw[s, l0, l1][:, :, c0 - l0 : c1 - l0]
+            copy(words.bitcast(BF16).rearrange("p (t e) -> p t e", e=2), rows.rearrange("p e t -> p t e"))
 
         w_bf = {}
-        W_AT = [CAST_W, CAST_W + 4, CAST_W + 8, CAST_W + 12, PICKED + 12, PICKED + 8, PICKED + 16, PICKED + 20, RAW_W[7] + 4]
 
         def cast_w(copy, e):
-            w_bf[e] = place(f"w_bf{e}", W_AT[e], [P, 8 * N], BF16)
+            w_bf[e] = place(f"w_bf{e}", CAST_W[e], [P, 8 * N], BF16)
             src = w_raw[e][:].rearrange("p (g j c i) -> p g c j i", g=2, j=4, i=2)
             copy(w_bf[e][:].rearrange("p (g c i j) -> p g c j i", g=2, i=2, j=4), src)
-
-        def cast_w_on_gpsimd(e):
-            w_bf[e] = place(f"w_bf{e}", W_AT[e], [P, 8 * N], BF16)
-            src = w_raw[e][:].rearrange("p (g j n) -> p g n j", g=2, j=4)
-            gpsimd_copy(w_bf[e][:].rearrange("p (g n j) -> p g n j", g=2, j=4), src)
 
         def quant_w(e):
             nc.vector.quantize_mx(out=wcodes[e][:].bitcast(FP8X4), scales=wscales[e][:], in_=w_bf[e][:])
 
         picked = {}
-        PICKED_AT = {
-            (1, 0): (CHUNK, PICKED + 8, 0),
-            (1, CHUNK): (CHUNK, PICKED + 16, 0),
-            (0, 0): (CHUNK, PICKED + 24, 0),
-            (0, 2 * BANK): (BANK, LAST_PAIRS, 0),
-            (0, 3 * BANK): (BANK, LAST_PAIRS + 8, -2 * LINK),
-        }
+
+        def width(g):
+            return CHUNK if g else BANK
 
         def gather(s, c0, n):
             g, h = divmod(s, 2)
-            first = max(f for gg, f in PICKED_AT if gg == g and f <= c0)
-            width, kib, shift = PICKED_AT[g, first]
+            first = c0 - c0 % width(g)
             if (g, first) not in picked:
-                picked[g, first] = place(f"picked{g}_{first}", kib, [P, 2 * width], U32, shift)
+                picked[g, first] = place(f"picked{g}_{first}", PICKED[g, first], [P, 2 * width(g)], U32)
             window = planes[:, s * T : min(s + 2, 4) * T]
-            c = width * h + c0 - first
+            c = width(g) * h + c0 - first
             dst = picked[g, first][:, c : c + n]
             nc.vector.tensor_copy(dst, window.indirect(offs_t[:, c0 // 16 : (c0 + n) // 16]))
-
-        def side_by_side_on_vector(dst, both):
-            src = both.bitcast(BF16).rearrange("p h (c e) -> p c h e", e=2)
-            nc.vector.tensor_copy(dst.rearrange("p (c h e) -> p c h e", h=2, e=2), src)
 
         def side_by_side_on_scalar(dst, both):
             nc.scalar.copy(
@@ -166,17 +147,13 @@ def tile_moe_shr_lin_relu2_kernel(tc, xT, w, b, gate, offs, pos1, pos2, out):
         def side_by_side_on_gpsimd(dst, both):
             nc.gpsimd.tensor_copy(dst.bitcast(U32).rearrange("p (c h) -> p c h", h=2), both.rearrange("p h c -> p c h"))
 
-        def regroup(side_by_side, g, c0, n, kib, shift=0):
-            x_bf[g, c0] = place(f"x_bf{g}_{c0}", kib, [P, 4 * n], BF16, shift)
+        def regroup(side_by_side, g, c0):
+            x_bf[g, c0] = place(f"x_bf{g}_{c0}", SLOT_BF[g, c0], [P, 4 * width(g)], BF16)
             side_by_side(x_bf[g, c0][:], picked[g, c0][:].rearrange("p (h c) -> p h c", h=2))
 
-        def slot_codes(g, c0, n):
-            i, c = divmod(c0, CHUNK)
-            return xcodes[g, i][:, c : c + n]
-
-        def quant_x(g, c0, n):
-            cols = slice(c0, c0 + n)
-            nc.vector.quantize_mx(out=slot_codes(g, c0, n).bitcast(FP8X4), scales=xscales[g][:, cols], in_=x_bf[g, c0][:])
+        def quant_x(g, c0):
+            cols = slice(c0, c0 + width(g))
+            nc.vector.quantize_mx(out=xcodes[g][:, cols].bitcast(FP8X4), scales=xscales[g][:, cols], in_=x_bf[g, c0][:])
 
         banks = {}
 
@@ -190,7 +167,7 @@ def tile_moe_shr_lin_relu2_kernel(tc, xT, w, b, gate, offs, pos1, pos2, out):
                     out=banks[k, m][:, C * i : C * (i + 1)],
                     lhsT=wcodes[e][:, w0 : w0 + P].bitcast(FP8X4),
                     lhsT_scale=wscales[e][:, w0 : w0 + P],
-                    rhs=slot_codes(g, C * e, C).bitcast(FP8X4),
+                    rhs=xcodes[g][:, C * e : C * (e + 1)].bitcast(FP8X4),
                     rhs_scale=xscales[g][:, C * e : C * (e + 1)],
                     start=(g == 1),
                     stop=(g == 0),
@@ -200,7 +177,7 @@ def tile_moe_shr_lin_relu2_kernel(tc, xT, w, b, gate, offs, pos1, pos2, out):
 
         def relu(k, m):
             if m not in y:
-                y[m] = place(f"y{m}", RAW_X + 16 + 8 * m, [P, S], F32)
+                y[m] = place(f"y{m}", Y[m], [P, S], F32)
             for i in range(2):
                 e = 2 * k + i
                 nc.scalar.activation(
@@ -215,11 +192,11 @@ def tile_moe_shr_lin_relu2_kernel(tc, xT, w, b, gate, offs, pos1, pos2, out):
 
         s_bf = {}
 
-        def regroup_shared(side_by_side, g, i):
+        def regroup_shared(side_by_side, g, c0, c1):
             if g not in s_bf:
-                s_bf[g] = place(f"s_bf{g}", RAW_X + 8 * (1 - g), [P, 4 * T], BF16)
+                s_bf[g] = place(f"s_bf{g}", SHARED_BF[g], [P, 4 * T], BF16)
             both = planes[:, 2 * g * T : 2 * (g + 1) * T].rearrange("p (h c) -> p h c", h=2)
-            side_by_side(s_bf[g][:, 4 * HALF * i : 4 * HALF * (i + 1)], both[:, :, HALF * i : HALF * (i + 1)])
+            side_by_side(s_bf[g][:, 4 * c0 : 4 * c1], both[:, :, c0:c1])
 
         def quant_shared(g):
             nc.vector.quantize_mx(out=scodes[:, T * g : T * (g + 1)].bitcast(FP8X4), scales=sscales[g][:], in_=s_bf[g][:])
@@ -239,52 +216,45 @@ def tile_moe_shr_lin_relu2_kernel(tc, xT, w, b, gate, offs, pos1, pos2, out):
                     stop=(g == 0),
                 )
 
-        cast_x(nc.vector.tensor_copy, 3, 1)
-        cast_x(nc.vector.tensor_copy, 3, 0)
-        cast_x(nc.scalar.copy, 2, 1)
-        cast_x(gpsimd_copy, 2, 0)
-        regroup_shared(side_by_side_on_scalar, 1, 1)
-        regroup_shared(side_by_side_on_gpsimd, 1, 0)
-        cast_x(nc.scalar.copy, 1, 1)
-        cast_x(gpsimd_copy, 1, 0)
-        cast_x(nc.scalar.copy, 0, 1)
-        cast_x(gpsimd_copy, 0, 0)
-        regroup_shared(side_by_side_on_scalar, 0, 1)
-        regroup_shared(side_by_side_on_gpsimd, 0, 0)
-        cast_w_on_gpsimd(0)
-        cast_w_on_gpsimd(1)
-        cast_w_on_gpsimd(3)
+        cast_x(nc.vector.tensor_copy, 3, 384, T)
+        cast_x(nc.vector.tensor_copy, 3, 128, 384)
+        cast_x(nc.scalar.copy, 3, 0, 128)
+        for g in (1, 0):
+            for s in (2,) if g else (0, 1):
+                cast_x(nc.scalar.copy, s, *ON_SCALAR[s])
+                cast_x(gpsimd_copy, s, *ON_GPSIMD[s])
+            regroup_shared(side_by_side_on_scalar, g, *ON_SCALAR[g + 1])
+            regroup_shared(side_by_side_on_gpsimd, g, *ON_GPSIMD[g + 1])
         for c0 in range(0, S, HALF):
             gather(3, c0, HALF)
         for c0 in range(0, S, CHUNK):
             gather(2, c0, CHUNK)
-        for c0, n in ((0, CHUNK), (2 * BANK, BANK), (3 * BANK, BANK)):
-            gather(1, c0, n)
-            gather(0, c0, n)
-        regroup(side_by_side_on_scalar, 1, 0, CHUNK, RAW_X + 16)
-        regroup(side_by_side_on_scalar, 1, CHUNK, CHUNK, RAW_X + 24)
-        cast_w(nc.scalar.copy, 2)
-        regroup(side_by_side_on_scalar, 0, 0, CHUNK, RAW_W[2], -LINK)
-        regroup(side_by_side_on_scalar, 0, 2 * BANK, BANK, RAW_W[2] + 8, -LINK)
-        for e in range(4, E):
+        for c0 in range(0, S, BANK):
+            gather(0, c0, BANK)
+            gather(1, c0, BANK)
+        for g, c0 in ((1, 0), (1, 1024), (0, 0), (0, 512), (0, 1024)):
+            regroup(side_by_side_on_gpsimd, g, c0)
+        for e in range(5):
             cast_w(nc.scalar.copy, e)
-        quant_x(1, 0, CHUNK)
+        regroup(side_by_side_on_scalar, 0, 1536)
+        for e in range(5, E):
+            cast_w(nc.scalar.copy, e)
+        quant_x(1, 0)
         quant_w(0)
         quant_w(1)
+        quant_x(0, 0)
+        quant_x(1, 1024)
         quant_w(2)
-        quant_x(0, 0, CHUNK)
         quant_w(3)
-        xcodes[1, 1] = place("xcodes11", LAST_PAIRS, [P, CHUNK], U32)
-        quant_x(1, CHUNK, CHUNK)
-        quant_x(0, 2 * BANK, BANK)
+        quant_x(0, 512)
+        quant_x(0, 1024)
         quant_w(4)
         quant_w(5)
-        regroup(side_by_side_on_vector, 0, 3 * BANK, BANK, RAW_W[6])
+        quant_x(0, 1536)
         quant_w(6)
-        quant_x(0, 3 * BANK, BANK)
         quant_w(7)
         cast_w(nc.vector.tensor_copy, E)
-        scodes = place("scodes", RAW_W[7] - 4, [P, 2 * T], U32)
+        scodes = place("scodes", SHARED_CODES, [P, 2 * T], U32)
         quant_shared(1)
         quant_w(E)
         quant_shared(0)
@@ -309,7 +279,7 @@ def tile_moe_shr_lin_relu2_kernel(tc, xT, w, b, gate, offs, pos1, pos2, out):
         for m in range(2):
             for half in range(2):
                 multiply_shared(m, half)
-        ys_all = place("ys", RAW_W[0], [P, 2 * T], F32)
+        ys_all = place("ys", YS, [P, 2 * T], F32)
 
         def ys(m, half):
             return ys_all[:, T * m + BANK * half : T * m + BANK * (half + 1)]
@@ -340,7 +310,7 @@ def tile_moe_shr_lin_relu2_kernel(tc, xT, w, b, gate, offs, pos1, pos2, out):
         terms, turned = {}, {}
         units = [(0, 0, BANK), (0, BANK, BANK), (1, 0, THIRD)]
         for i, u in enumerate(units):
-            terms[u] = [place(f"terms{i}{r}", RAW_W[1] + 4 * i + 2 * r, [P, u[2]], F32)[:] for r in range(2)]
+            terms[u] = [place(f"terms{i}{r}", TERMS + 4 * i + 2 * r, [P, u[2]], F32)[:] for r in range(2)]
             for r in range(2):
                 fetch(terms[u][r], r, *u)
 
@@ -381,14 +351,14 @@ def tile_moe_shr_lin_relu2_kernel(tc, xT, w, b, gate, offs, pos1, pos2, out):
         store_turned(units[2])
 
         rest = T - THIRD
-        t = place("terms_last", RAW_W[3], [P, 2 * rest], F32)
+        t = place("terms_last", TERMS_LAST, [P, 2 * rest], F32)
         first, second = t[:, 0:rest], t[:, rest : 2 * rest]
         pieces = ((0, rest - C), (rest - C, C))
         fetch(first, 0, 1, THIRD, rest)
         fetch(second[:, 0 : rest - C], 1, 1, THIRD, rest - C)
         add_into(first, shared_term(1, THIRD, rest))
         fetch(second[:, rest - C : rest], 1, 1, T - C, C)
-        total = place("total", RAW_W[1] + 4 * 2 + 2, [P, rest], F32)
+        total = place("total", TERMS + 4 * 2 + 2, [P, rest], F32)
         for c0, n in pieces:
             cols = slice(c0, c0 + n)
             nc.vector.tensor_tensor(total[:, cols], first[:, cols], second[:, cols], ADD)

@@ -32,13 +32,13 @@ KIB = 1024
 
 RAW_X = {2: 0, 1: 8, 0: 16, 3: 24}
 SHARED_BF = {1: 160, 0: 32}
-PICKED = {(1, 0): 40, (1, 1024): 48, (0, 0): 56, (0, 512): 60, (0, 1024): 64, (0, 1536): 68}
+PICKED = {(1, 0): 40, (1, CHUNK): 48, (0, 0): 56, (0, CHUNK): 64}
 RAW_W = [72 + 8 * e for e in range(E + 1)]
-CAST_W = [144, 148, 152, 156, 40, 44, 48, 52, RAW_W[1] + 4]
-SLOT_BF = {(1, 0): 6, (1, 1024): 14, (0, 0): RAW_W[0], (0, 512): RAW_W[0] + 4, (0, 1024): RAW_W[1], (0, 1536): RAW_W[4]}
+CAST_W = [144, 148, 152, 156, 56, 60, 40, 44, RAW_W[4]]
+SLOT_BF = {(1, 0): 6, (1, CHUNK): 14, (0, 0): RAW_W[2], (0, CHUNK): RAW_W[3]}
 SHARED_CODES = RAW_W[7]
-GATES = RAW_W[2]
-Y = [RAW_W[3], 56]
+GATES = RAW_W[0]
+Y = [RAW_W[1], 48]
 YS = 64
 TERMS = RAW_W[5]
 TERMS_LAST = 144
@@ -118,23 +118,29 @@ def tile_moe_shr_lin_relu2_kernel(tc, xT, w, b, gate, offs, pos1, pos2, out):
             src = w_raw[e][:].rearrange("p (g j c i) -> p g c j i", g=2, j=4, i=2)
             copy(w_bf[e][:].rearrange("p (g c i j) -> p g c j i", g=2, i=2, j=4), src)
 
+        def cast_w_on_gpsimd(e):
+            w_bf[e] = place(f"w_bf{e}", CAST_W[e], [P, 8 * N], BF16)
+            src = w_raw[e][:].rearrange("p (g j n) -> p g n j", g=2, j=4)
+            gpsimd_copy(w_bf[e][:].rearrange("p (g n j) -> p g n j", g=2, j=4), src)
+
         def quant_w(e):
             nc.vector.quantize_mx(out=wcodes[e][:].bitcast(FP8X4), scales=wscales[e][:], in_=w_bf[e][:])
 
         picked = {}
 
-        def width(g):
-            return CHUNK if g else BANK
-
         def gather(s, c0, n):
             g, h = divmod(s, 2)
-            first = c0 - c0 % width(g)
+            first = c0 - c0 % CHUNK
             if (g, first) not in picked:
-                picked[g, first] = place(f"picked{g}_{first}", PICKED[g, first], [P, 2 * width(g)], U32)
+                picked[g, first] = place(f"picked{g}_{first}", PICKED[g, first], [P, 2 * CHUNK], U32)
             window = planes[:, s * T : min(s + 2, 4) * T]
-            c = width(g) * h + c0 - first
+            c = CHUNK * h + c0 - first
             dst = picked[g, first][:, c : c + n]
             nc.vector.tensor_copy(dst, window.indirect(offs_t[:, c0 // 16 : (c0 + n) // 16]))
+
+        def side_by_side_on_vector(dst, both):
+            src = both.bitcast(BF16).rearrange("p h (c e) -> p c h e", e=2)
+            nc.vector.tensor_copy(dst.rearrange("p (c h e) -> p c h e", h=2, e=2), src)
 
         def side_by_side_on_scalar(dst, both):
             nc.scalar.copy(
@@ -148,11 +154,11 @@ def tile_moe_shr_lin_relu2_kernel(tc, xT, w, b, gate, offs, pos1, pos2, out):
             nc.gpsimd.tensor_copy(dst.bitcast(U32).rearrange("p (c h) -> p c h", h=2), both.rearrange("p h c -> p c h"))
 
         def regroup(side_by_side, g, c0):
-            x_bf[g, c0] = place(f"x_bf{g}_{c0}", SLOT_BF[g, c0], [P, 4 * width(g)], BF16)
+            x_bf[g, c0] = place(f"x_bf{g}_{c0}", SLOT_BF[g, c0], [P, 4 * CHUNK], BF16)
             side_by_side(x_bf[g, c0][:], picked[g, c0][:].rearrange("p (h c) -> p h c", h=2))
 
         def quant_x(g, c0):
-            cols = slice(c0, c0 + width(g))
+            cols = slice(c0, c0 + CHUNK)
             nc.vector.quantize_mx(out=xcodes[g][:, cols].bitcast(FP8X4), scales=xscales[g][:, cols], in_=x_bf[g, c0][:])
 
         banks = {}
@@ -229,28 +235,28 @@ def tile_moe_shr_lin_relu2_kernel(tc, xT, w, b, gate, offs, pos1, pos2, out):
             gather(3, c0, HALF)
         for c0 in range(0, S, CHUNK):
             gather(2, c0, CHUNK)
-        for c0 in range(0, S, BANK):
-            gather(0, c0, BANK)
-            gather(1, c0, BANK)
-        for g, c0 in ((1, 0), (1, 1024), (0, 0), (0, 512), (0, 1024)):
-            regroup(side_by_side_on_gpsimd, g, c0)
-        for e in range(5):
-            cast_w(nc.scalar.copy, e)
-        regroup(side_by_side_on_scalar, 0, 1536)
-        for e in range(5, E):
+        for c0 in range(0, S, CHUNK):
+            gather(0, c0, CHUNK)
+            gather(1, c0, CHUNK)
+        for e in (0, 1, 3):
+            cast_w_on_gpsimd(e)
+        regroup(side_by_side_on_scalar, 1, 0)
+        regroup(side_by_side_on_scalar, 1, CHUNK)
+        cast_w(nc.scalar.copy, 2)
+        regroup(side_by_side_on_scalar, 0, 0)
+        for e in range(4, E):
             cast_w(nc.scalar.copy, e)
         quant_x(1, 0)
         quant_w(0)
         quant_w(1)
-        quant_x(0, 0)
-        quant_x(1, 1024)
         quant_w(2)
+        quant_x(0, 0)
         quant_w(3)
-        quant_x(0, 512)
-        quant_x(0, 1024)
+        regroup(side_by_side_on_vector, 0, CHUNK)
+        quant_x(1, CHUNK)
         quant_w(4)
+        quant_x(0, CHUNK)
         quant_w(5)
-        quant_x(0, 1536)
         quant_w(6)
         quant_w(7)
         cast_w(nc.vector.tensor_copy, E)
@@ -263,19 +269,19 @@ def tile_moe_shr_lin_relu2_kernel(tc, xT, w, b, gate, offs, pos1, pos2, out):
                 for e in range(e0, e0 + 4):
                     multiply(e, m)
 
-        relu(0, 0)
-        relu(1, 0)
-        relu(0, 1)
-        square(y_pairs(0, 0, 2))
+        for m in range(2):
+            relu(0, m)
+            relu(1, m)
+        for m in range(2):
+            square(y_pairs(m, 0, 2))
         relu(2, 0)
-        relu(1, 1)
         relu(3, 0)
         square(y_pairs(0, 2, 3))
-        square(y_pairs(0, 3, 4))
         relu(2, 1)
+        square(y_pairs(0, 3, 4))
         relu(3, 1)
-        square(y_pairs(1, 0, 2))
-        square(y_pairs(1, 2, 4))
+        square(y_pairs(1, 2, 3))
+        square(y_pairs(1, 3, 4))
         for m in range(2):
             for half in range(2):
                 multiply_shared(m, half)
@@ -316,11 +322,11 @@ def tile_moe_shr_lin_relu2_kernel(tc, xT, w, b, gate, offs, pos1, pos2, out):
 
         def sum_turned(u):
             turned[u] = psum.tile([P, BANK], F32, name="ps")
-            for j in range(0, u[2], P):
-                for i, term in enumerate((*terms[u], shared_term(*u))):
+            for i, term in enumerate((shared_term(*u), *terms[u])):
+                for j in range(0, u[2], P):
                     nc.tensor.matmul(
                         turned[u][:, j : j + P], term[:, j : j + P], ident[:],
-                        start=(i == 0), stop=(i == 2), is_transpose=True,
+                        start=(i == 0 and j == 0), stop=(i == 2 and j == u[2] - P), is_transpose=True,
                     )
 
         def empty_turned(u):

@@ -25,21 +25,21 @@ PAIRS = E // 2
 CHUNK = 1024
 HALF = T // 2
 THIRD = 384
-LOADS = {3: ((384, T), (0, 384)), 2: ((0, T),), 0: ((0, T),), 1: ((0, 640), (640, T))}
-ON_SCALAR = {2: (HALF, T), 0: (0, HALF), 1: (0, 640)}
-ON_GPSIMD = {2: (0, HALF), 0: (HALF, T), 1: (640, T)}
+LOADS = {3: ((384, T), (0, 384)), 2: ((0, T),), 0: ((0, T),), 1: ((0, HALF), (HALF, T))}
+ON_SCALAR = {2: (HALF, T), 0: (0, HALF), 1: (0, HALF)}
+ON_GPSIMD = {2: (0, HALF), 0: (HALF, T), 1: (HALF, T)}
 KIB = 1024
 
-RAW_X = {2: 0, 1: 8, 0: 16, 3: 24}
-SHARED_BF = {1: 160, 0: 32}
+RAW_X = {2: 0, 1: 8, 0: 16}
+SHARED_BF = {1: 24, 0: 32}
 PICKED = {(1, 0): 40, (1, CHUNK): 48, (0, 0): 56, (0, CHUNK): 64}
 RAW_W = [72 + 8 * e for e in range(E + 1)]
-CAST_W = [144, 148, 152, 156, 56, 60, 40, 44, RAW_W[4]]
-SLOT_BF = {(1, 0): 6, (1, CHUNK): 14, (0, 0): RAW_W[2], (0, CHUNK): RAW_W[3]}
+CAST_W = [144, 148, 152, 156, 56, 60, 40, 44, RAW_W[3]]
+SLOT_BF = {(1, 0): 6, (1, CHUNK): 14, (0, 0): RAW_W[2], (0, CHUNK): RAW_W[4]}
 SHARED_CODES = RAW_W[7]
-GATES = RAW_W[0]
+GATES = 160
 Y = [RAW_W[1], 48]
-YS = 64
+YS = 72
 TERMS = RAW_W[5]
 TERMS_LAST = 144
 
@@ -60,7 +60,8 @@ def tile_moe_shr_lin_relu2_kernel(tc, xT, w, b, gate, offs, pos1, pos2, out):
         pos2_t = lists.tile([P, T // 16], U16, name="pos2_t")
         pos = (pos1_t, pos2_t)
 
-        planes = keep.tile([P, 4 * T], U32, name="planes")
+        planes_and_rows = keep.tile([P, 6 * T], F32, name="planes_and_rows")
+        planes = planes_and_rows[:].bitcast(U32)
         wcodes = [keep.tile([P, 2 * N], U32, name=f"wcodes{e}", align_bytes=64) for e in range(E + 1)]
         wscales = [keep.tile([P, 2 * N], U8, name=f"wscales{e}", align_bytes=64) for e in range(E + 1)]
         xcodes = [keep.tile([P, S], U32, name=f"xcodes{g}", align_bytes=64) for g in range(2)]
@@ -78,9 +79,13 @@ def tile_moe_shr_lin_relu2_kernel(tc, xT, w, b, gate, offs, pos1, pos2, out):
             rows = xT[K_PASS * g : K_PASS * (g + 1), :].rearrange("(p j) t -> p j t", j=4)
             shift = 0
             for c0, c1 in LOADS[s]:
-                x_raw[s, c0, c1] = place(f"x_raw{s}_{c0}", RAW_X[s], [P, 2, c1 - c0], F32, shift)
-                nc.sync.dma_start(x_raw[s, c0, c1][:], rows[:, 2 * h : 2 * h + 2, c0:c1])
-                shift += 8 * (c1 - c0)
+                if s == 3:
+                    flat = planes_and_rows[:, 4 * T + shift : 4 * T + shift + 2 * (c1 - c0)]
+                else:
+                    flat = place(f"x_raw{s}_{c0}", RAW_X[s], [P, 2 * (c1 - c0)], F32, 4 * shift)[:]
+                x_raw[s, c0, c1] = flat.rearrange("p (e t) -> p e t", e=2)
+                nc.sync.dma_start(x_raw[s, c0, c1], rows[:, 2 * h : 2 * h + 2, c0:c1])
+                shift += 2 * (c1 - c0)
 
         def load_w(e):
             w_raw[e] = place(f"w_raw{e}", RAW_W[e], [P, 8 * N], F32)
@@ -128,15 +133,13 @@ def tile_moe_shr_lin_relu2_kernel(tc, xT, w, b, gate, offs, pos1, pos2, out):
 
         picked = {}
 
-        def gather(s, c0, n):
+        def gather(s, c0):
             g, h = divmod(s, 2)
-            first = c0 - c0 % CHUNK
-            if (g, first) not in picked:
-                picked[g, first] = place(f"picked{g}_{first}", PICKED[g, first], [P, 2 * CHUNK], U32)
-            window = planes[:, s * T : min(s + 2, 4) * T]
-            c = CHUNK * h + c0 - first
-            dst = picked[g, first][:, c : c + n]
-            nc.vector.tensor_copy(dst, window.indirect(offs_t[:, c0 // 16 : (c0 + n) // 16]))
+            if (g, c0) not in picked:
+                picked[g, c0] = place(f"picked{g}_{c0}", PICKED[g, c0], [P, 2 * CHUNK], U32)
+            window = planes[:, s * T : (s + 2) * T]
+            dst = picked[g, c0][:, CHUNK * h : CHUNK * (h + 1)]
+            nc.vector.tensor_copy(dst, window.indirect(offs_t[:, c0 // 16 : (c0 + CHUNK) // 16]))
 
         def side_by_side_on_vector(dst, both):
             src = both.bitcast(BF16).rearrange("p h (c e) -> p c h e", e=2)
@@ -153,9 +156,10 @@ def tile_moe_shr_lin_relu2_kernel(tc, xT, w, b, gate, offs, pos1, pos2, out):
         def side_by_side_on_gpsimd(dst, both):
             nc.gpsimd.tensor_copy(dst.bitcast(U32).rearrange("p (c h) -> p c h", h=2), both.rearrange("p h c -> p c h"))
 
-        def regroup(side_by_side, g, c0):
-            x_bf[g, c0] = place(f"x_bf{g}_{c0}", SLOT_BF[g, c0], [P, 4 * CHUNK], BF16)
-            side_by_side(x_bf[g, c0][:], picked[g, c0][:].rearrange("p (h c) -> p h c", h=2))
+        def regroup(side_by_side, g, c0, a=0, z=CHUNK):
+            if (g, c0) not in x_bf:
+                x_bf[g, c0] = place(f"x_bf{g}_{c0}", SLOT_BF[g, c0], [P, 4 * CHUNK], BF16)
+            side_by_side(x_bf[g, c0][:, 4 * a : 4 * z], picked[g, c0][:].rearrange("p (h c) -> p h c", h=2)[:, :, a:z])
 
         def quant_x(g, c0):
             cols = slice(c0, c0 + CHUNK)
@@ -231,20 +235,21 @@ def tile_moe_shr_lin_relu2_kernel(tc, xT, w, b, gate, offs, pos1, pos2, out):
                 cast_x(gpsimd_copy, s, *ON_GPSIMD[s])
             regroup_shared(side_by_side_on_scalar, g, *ON_SCALAR[g + 1])
             regroup_shared(side_by_side_on_gpsimd, g, *ON_GPSIMD[g + 1])
-        for c0 in range(0, S, HALF):
-            gather(3, c0, HALF)
-        for c0 in range(0, S, CHUNK):
-            gather(2, c0, CHUNK)
-        for c0 in range(0, S, CHUNK):
-            gather(0, c0, CHUNK)
-            gather(1, c0, CHUNK)
+        for s in (3, 2):
+            for c0 in (0, CHUNK):
+                gather(s, c0)
+        for c0 in (0, CHUNK):
+            for s in (0, 1):
+                gather(s, c0)
         for e in (0, 1, 3):
             cast_w_on_gpsimd(e)
         regroup(side_by_side_on_scalar, 1, 0)
         regroup(side_by_side_on_scalar, 1, CHUNK)
         cast_w(nc.scalar.copy, 2)
         regroup(side_by_side_on_scalar, 0, 0)
-        for e in range(4, E):
+        cast_w(nc.scalar.copy, 4)
+        regroup(side_by_side_on_scalar, 0, CHUNK, 0, BANK)
+        for e in range(5, E):
             cast_w(nc.scalar.copy, e)
         quant_x(1, 0)
         quant_w(0)
@@ -252,8 +257,8 @@ def tile_moe_shr_lin_relu2_kernel(tc, xT, w, b, gate, offs, pos1, pos2, out):
         quant_w(2)
         quant_x(0, 0)
         quant_w(3)
-        regroup(side_by_side_on_vector, 0, CHUNK)
         quant_x(1, CHUNK)
+        regroup(side_by_side_on_vector, 0, CHUNK, BANK, CHUNK)
         quant_w(4)
         quant_x(0, CHUNK)
         quant_w(5)
@@ -269,18 +274,17 @@ def tile_moe_shr_lin_relu2_kernel(tc, xT, w, b, gate, offs, pos1, pos2, out):
                 for e in range(e0, e0 + 4):
                     multiply(e, m)
 
-        for m in range(2):
-            relu(0, m)
-            relu(1, m)
-        for m in range(2):
-            square(y_pairs(m, 0, 2))
+        relu(0, 0)
+        relu(1, 0)
+        relu(0, 1)
         relu(2, 0)
+        square(y_pairs(0, 0, 2))
         relu(3, 0)
         square(y_pairs(0, 2, 3))
-        relu(2, 1)
         square(y_pairs(0, 3, 4))
-        relu(3, 1)
-        square(y_pairs(1, 2, 3))
+        for k in range(1, PAIRS):
+            relu(k, 1)
+        square(y_pairs(1, 0, 3))
         square(y_pairs(1, 3, 4))
         for m in range(2):
             for half in range(2):
@@ -315,10 +319,14 @@ def tile_moe_shr_lin_relu2_kernel(tc, xT, w, b, gate, offs, pos1, pos2, out):
 
         terms, turned = {}, {}
         units = [(0, 0, BANK), (0, BANK, BANK), (1, 0, THIRD)]
-        for i, u in enumerate(units):
-            terms[u] = [place(f"terms{i}{r}", TERMS + 4 * i + 2 * r, [P, u[2]], F32)[:] for r in range(2)]
-            for r in range(2):
-                fetch(terms[u][r], r, *u)
+        whole = [place(f"terms0{r}", TERMS + 4 * r, [P, T], F32) for r in range(2)]
+        for r in range(2):
+            fetch(whole[r][:], r, 0, 0, T)
+        for u in units[:2]:
+            terms[u] = [whole[r][:, u[1] : u[1] + BANK] for r in range(2)]
+        terms[units[2]] = [place(f"terms2{r}", TERMS + 8 + 2 * r, [P, THIRD], F32)[:] for r in range(2)]
+        for r in range(2):
+            fetch(terms[units[2]][r], r, *units[2])
 
         def sum_turned(u):
             turned[u] = psum.tile([P, BANK], F32, name="ps")

@@ -29,6 +29,7 @@ LOADS = {3: ((384, T), (0, 384)), 2: ((0, T),), 0: ((0, T),), 1: ((0, HALF), (HA
 ON_SCALAR = {2: (HALF, T), 0: (0, HALF), 1: (0, HALF)}
 ON_GPSIMD = {2: (0, HALF), 0: (HALF, T), 1: (HALF, T)}
 KIB = 1024
+BY_PASS = range(2, E)
 
 RAW_X = {2: 0, 1: 8, 0: 16}
 SHARED_BF = {1: 24, 0: 32}
@@ -88,11 +89,11 @@ def tile_moe_shr_lin_relu2_kernel(tc, xT, w, b, gate, offs, pos1, pos2, out):
                 shift += 2 * (c1 - c0)
 
         def load_w(e):
-            w_raw[e] = place(f"w_raw{e}", RAW_W[e], [P, 8 * N], F32)
-            nc.sync.dma_start(
-                w_raw[e][:].rearrange("p (g j n) -> p g j n", g=2, j=4),
-                w[e].rearrange("(g p j) n -> p g j n", p=P, j=4),
-            )
+            passes = ((0, 1), (1, 2)) if e in BY_PASS else ((0, 2),)
+            for g0, g1 in passes:
+                w_raw[e, g0, g1] = place(f"w_raw{e}{g0}", RAW_W[e] + 4 * g0, [P, g1 - g0, 4, N], F32)
+                rows = w[e, K_PASS * g0 : K_PASS * g1, :]
+                nc.sync.dma_start(w_raw[e, g0, g1][:], rows.rearrange("(g p j) n -> p g j n", p=P, j=4))
 
         load_x(3)
         nc.sync.dma_start(offs_t[:], offs)
@@ -120,13 +121,17 @@ def tile_moe_shr_lin_relu2_kernel(tc, xT, w, b, gate, offs, pos1, pos2, out):
 
         def cast_w(copy, e):
             w_bf[e] = place(f"w_bf{e}", CAST_W[e], [P, 8 * N], BF16)
-            src = w_raw[e][:].rearrange("p (g j c i) -> p g c j i", g=2, j=4, i=2)
-            copy(w_bf[e][:].rearrange("p (g c i j) -> p g c j i", g=2, i=2, j=4), src)
+            for ee, g0, g1 in w_raw:
+                if ee == e:
+                    dst = w_bf[e][:, 4 * N * g0 : 4 * N * g1].rearrange("p (g c i j) -> p g c j i", c=N // 2, i=2, j=4)
+                    copy(dst, w_raw[e, g0, g1][:].rearrange("p g j (c i) -> p g c j i", i=2))
 
         def cast_w_on_gpsimd(e):
             w_bf[e] = place(f"w_bf{e}", CAST_W[e], [P, 8 * N], BF16)
-            src = w_raw[e][:].rearrange("p (g j n) -> p g n j", g=2, j=4)
-            gpsimd_copy(w_bf[e][:].rearrange("p (g n j) -> p g n j", g=2, j=4), src)
+            for ee, g0, g1 in w_raw:
+                if ee == e:
+                    dst = w_bf[e][:, 4 * N * g0 : 4 * N * g1].rearrange("p (g n j) -> p g n j", n=N, j=4)
+                    gpsimd_copy(dst, w_raw[e, g0, g1][:].rearrange("p g j n -> p g n j"))
 
         def quant_w(e):
             nc.vector.quantize_mx(out=wcodes[e][:].bitcast(FP8X4), scales=wscales[e][:], in_=w_bf[e][:])
@@ -328,14 +333,14 @@ def tile_moe_shr_lin_relu2_kernel(tc, xT, w, b, gate, offs, pos1, pos2, out):
         for r in range(2):
             fetch(terms[units[2]][r], r, *units[2])
 
-        def sum_turned(u):
-            turned[u] = psum.tile([P, BANK], F32, name="ps")
-            for i, term in enumerate((shared_term(*u), *terms[u])):
-                for j in range(0, u[2], P):
-                    nc.tensor.matmul(
-                        turned[u][:, j : j + P], term[:, j : j + P], ident[:],
-                        start=(i == 0 and j == 0), stop=(i == 2 and j == u[2] - P), is_transpose=True,
-                    )
+        def add_turned(u, term, first, last):
+            if first:
+                turned[u] = psum.tile([P, BANK], F32, name="ps")
+            for j in range(0, u[2], P):
+                nc.tensor.matmul(
+                    turned[u][:, j : j + P], term[:, j : j + P], ident[:],
+                    start=(first and j == 0), stop=(last and j == u[2] - P), is_transpose=True,
+                )
 
         def empty_turned(u):
             nc.scalar.copy(terms[u][1], turned[u][:, 0 : u[2]])
@@ -349,12 +354,14 @@ def tile_moe_shr_lin_relu2_kernel(tc, xT, w, b, gate, offs, pos1, pos2, out):
             nc.scalar.copy(terms[u][0], turned[u][:, 0 : u[2]])
             store(terms[u][0], *u)
 
-        sum_turned(units[0])
-        sum_turned(units[1])
+        for i in range(3):
+            for u in units[:2]:
+                add_turned(u, (*terms[u], shared_term(*u))[i], i == 0, i == 2)
         empty_turned(units[0])
         turn_back(units[0])
         relu_shared(1, 1)
-        sum_turned(units[2])
+        for i in range(3):
+            add_turned(units[2], (shared_term(*units[2]), *terms[units[2]])[i], i == 0, i == 2)
         empty_turned(units[1])
         turn_back(units[1])
         square(ys(1, 1))

@@ -11,6 +11,7 @@ FLOPS = 2 * K * N * (S + T)
 F32 = mybir.dt.float32
 BF16 = mybir.dt.bfloat16
 U32 = mybir.dt.uint32
+I32 = mybir.dt.int32
 U16 = mybir.dt.uint16
 U8 = mybir.dt.uint8
 FP8X4 = mybir.dt.float8_e4m3fn_x4
@@ -25,6 +26,7 @@ PAIRS = E // 2
 CHUNK = 1024
 HALF = T // 2
 THIRD = 384
+ON_VECTOR = 576
 LOADS = {3: ((384, T), (0, 384)), 2: ((0, T),), 0: ((0, T),), 1: ((0, HALF), (HALF, T))}
 ON_SCALAR = {2: (HALF, T), 0: (0, HALF), 1: (0, HALF)}
 ON_GPSIMD = {2: (0, HALF), 0: (HALF, T), 1: (HALF, T)}
@@ -34,13 +36,13 @@ BY_PASS = range(2, E)
 RAW_X = {2: 0, 1: 8, 0: 16}
 SHARED_BF = {1: 24, 0: 32}
 PICKED = {(1, 0): 40, (1, CHUNK): 48, (0, 0): 56, (0, CHUNK): 64}
-RAW_W = [72 + 8 * e for e in range(E + 1)]
-CAST_W = [144, 148, 152, 156, 56, 60, 40, 44, RAW_W[3]]
-SLOT_BF = {(1, 0): 6, (1, CHUNK): 14, (0, 0): RAW_W[2], (0, CHUNK): RAW_W[4]}
+RAW_W = [80, 72] + [72 + 8 * e for e in range(2, E + 1)]
+CAST_W = [144, 148, 152, 156, 40, 44, 56, 60, RAW_W[3]]
+SLOT_BF = {(1, 0): 4, (1, CHUNK): 14, (0, 0): RAW_W[2] - 4, (0, CHUNK): RAW_W[4] - 4}
 SHARED_CODES = RAW_W[7]
 GATES = 160
 Y = [RAW_W[1], 48]
-YS = 72
+YS = RAW_W[0]
 TERMS = RAW_W[5]
 TERMS_LAST = 144
 
@@ -147,8 +149,10 @@ def tile_moe_shr_lin_relu2_kernel(tc, xT, w, b, gate, offs, pos1, pos2, out):
             nc.vector.tensor_copy(dst, window.indirect(offs_t[:, c0 // 16 : (c0 + CHUNK) // 16]))
 
         def side_by_side_on_vector(dst, both):
-            src = both.bitcast(BF16).rearrange("p h (c e) -> p c h e", e=2)
-            nc.vector.tensor_copy(dst.rearrange("p (c h e) -> p c h e", h=2, e=2), src)
+            nc.vector.tensor_copy(
+                dst.bitcast(I32).rearrange("p (c i h) -> p c h i", i=2, h=2),
+                both.bitcast(I32).rearrange("p h (c i) -> p c h i", i=2),
+            )
 
         def side_by_side_on_scalar(dst, both):
             nc.scalar.copy(
@@ -253,7 +257,7 @@ def tile_moe_shr_lin_relu2_kernel(tc, xT, w, b, gate, offs, pos1, pos2, out):
         cast_w(nc.scalar.copy, 2)
         regroup(side_by_side_on_scalar, 0, 0)
         cast_w(nc.scalar.copy, 4)
-        regroup(side_by_side_on_scalar, 0, CHUNK, 0, BANK)
+        regroup(side_by_side_on_scalar, 0, CHUNK, 0, CHUNK - ON_VECTOR)
         for e in range(5, E):
             cast_w(nc.scalar.copy, e)
         quant_x(1, 0)
@@ -263,7 +267,7 @@ def tile_moe_shr_lin_relu2_kernel(tc, xT, w, b, gate, offs, pos1, pos2, out):
         quant_x(0, 0)
         quant_w(3)
         quant_x(1, CHUNK)
-        regroup(side_by_side_on_vector, 0, CHUNK, BANK, CHUNK)
+        regroup(side_by_side_on_vector, 0, CHUNK, CHUNK - ON_VECTOR, CHUNK)
         quant_w(4)
         quant_x(0, CHUNK)
         quant_w(5)

@@ -18,6 +18,7 @@ FP8X4 = mybir.dt.float8_e4m3fn_x4
 
 RELU = mybir.ActivationFunctionType.Relu
 SQUARE = mybir.ActivationFunctionType.Square
+COPY = mybir.ActivationFunctionType.Copy
 MULT, ADD = mybir.AluOpType.mult, mybir.AluOpType.add
 
 K_PASS = 512
@@ -27,7 +28,9 @@ CHUNK = 1024
 HALF = T // 2
 THIRD = 384
 ON_VECTOR = 576
-LOADS = {3: ((384, T), (0, 384)), 2: ((0, T),), 0: ((0, T),), 1: ((0, HALF), (HALF, T))}
+EARLY = C
+EARLY_ROWS = 144
+LOADS = {2: ((0, T),), 0: ((0, T),), 1: ((0, HALF), (HALF, T))}
 ON_SCALAR = {2: (HALF, T), 0: (0, HALF), 1: (0, HALF)}
 ON_GPSIMD = {2: (0, HALF), 0: (HALF, T), 1: (HALF, T)}
 KIB = 1024
@@ -82,10 +85,7 @@ def tile_moe_shr_lin_relu2_kernel(tc, xT, w, b, gate, offs, pos1, pos2, out):
             rows = xT[K_PASS * g : K_PASS * (g + 1), :].rearrange("(p j) t -> p j t", j=4)
             shift = 0
             for c0, c1 in LOADS[s]:
-                if s == 3:
-                    flat = planes_and_rows[:, 4 * T + shift : 4 * T + shift + 2 * (c1 - c0)]
-                else:
-                    flat = place(f"x_raw{s}_{c0}", RAW_X[s], [P, 2 * (c1 - c0)], F32, 4 * shift)[:]
+                flat = place(f"x_raw{s}_{c0}", RAW_X[s], [P, 2 * (c1 - c0)], F32, 4 * shift)[:]
                 x_raw[s, c0, c1] = flat.rearrange("p (e t) -> p e t", e=2)
                 nc.sync.dma_start(x_raw[s, c0, c1], rows[:, 2 * h : 2 * h + 2, c0:c1])
                 shift += 2 * (c1 - c0)
@@ -97,7 +97,10 @@ def tile_moe_shr_lin_relu2_kernel(tc, xT, w, b, gate, offs, pos1, pos2, out):
                 rows = w[e, K_PASS * g0 : K_PASS * g1, :]
                 nc.sync.dma_start(w_raw[e, g0, g1][:], rows.rearrange("(g p j) n -> p g j n", p=P, j=4))
 
-        load_x(3)
+        first_rows = planes_and_rows[:, 4 * T : 6 * T].rearrange("p (e t) -> p e t", e=2)
+        rows = xT[K_PASS:K, :].rearrange("(p j) t -> p j t", j=4)
+        for c0, c1 in ((384, T), (0, 384)):
+            nc.sync.dma_start(first_rows[:, :, c0:c1], rows[:, 2:4, c0:c1])
         nc.sync.dma_start(offs_t[:], offs)
         for s in (2, 0, 1):
             load_x(s)
@@ -114,9 +117,12 @@ def tile_moe_shr_lin_relu2_kernel(tc, xT, w, b, gate, offs, pos1, pos2, out):
             nc.gpsimd.tensor_scalar(dst, src, 1.0, 0.0, MULT, ADD)
 
         def cast_x(copy, s, c0, c1):
-            l0, l1 = [(a, z) for a, z in LOADS[s] if a <= c0 < z][0]
             words = planes[:, s * T + c0 : s * T + c1]
-            rows = x_raw[s, l0, l1][:, :, c0 - l0 : c1 - l0]
+            if s == 3:
+                rows = first_rows[:, :, c0:c1]
+            else:
+                l0, l1 = [(a, z) for a, z in LOADS[s] if a <= c0 < z][0]
+                rows = x_raw[s, l0, l1][:, :, c0 - l0 : c1 - l0]
             copy(words.bitcast(BF16).rearrange("p (t e) -> p t e", e=2), rows.rearrange("p e t -> p t e"))
 
         w_bf = {}
@@ -140,13 +146,25 @@ def tile_moe_shr_lin_relu2_kernel(tc, xT, w, b, gate, offs, pos1, pos2, out):
 
         picked = {}
 
-        def gather(s, c0):
+        def picked_words(s, c0):
             g, h = divmod(s, 2)
             if (g, c0) not in picked:
                 picked[g, c0] = place(f"picked{g}_{c0}", PICKED[g, c0], [P, 2 * CHUNK], U32)
+            return picked[g, c0][:, CHUNK * h : CHUNK * (h + 1)]
+
+        def gather(s, c0, a=0):
             window = planes[:, s * T : (s + 2) * T]
-            dst = picked[g, c0][:, CHUNK * h : CHUNK * (h + 1)]
-            nc.vector.tensor_copy(dst, window.indirect(offs_t[:, c0 // 16 : (c0 + CHUNK) // 16]))
+            nc.vector.tensor_copy(picked_words(s, c0)[:, a:CHUNK], window.indirect(offs_t[:, (c0 + a) // 16 : (c0 + CHUNK) // 16]))
+
+        def gather_early():
+            early = place("early", EARLY_ROWS, [P, 2 * EARLY], F32)
+            for j in range(2):
+                for c0 in range(0, EARLY, C):
+                    window = planes_and_rows[:, (4 + j) * T : (5 + j) * T]
+                    dst = early[:, j * EARLY + c0 : j * EARLY + c0 + C]
+                    nc.scalar.activation(dst, window.indirect(offs_t[:, c0 // 16 : (c0 + C) // 16]), COPY)
+            pairs = picked_words(3, 0)[:, 0:EARLY].bitcast(BF16).rearrange("p (t e) -> p t e", e=2)
+            nc.scalar.copy(pairs, early[:].rearrange("p (e t) -> p t e", e=2))
 
         def side_by_side_on_vector(dst, both):
             nc.vector.tensor_copy(
@@ -238,6 +256,7 @@ def tile_moe_shr_lin_relu2_kernel(tc, xT, w, b, gate, offs, pos1, pos2, out):
         cast_x(nc.vector.tensor_copy, 3, 384, T)
         cast_x(nc.vector.tensor_copy, 3, 128, 384)
         cast_x(nc.scalar.copy, 3, 0, 128)
+        gather_early()
         for g in (1, 0):
             for s in (2,) if g else (0, 1):
                 cast_x(nc.scalar.copy, s, *ON_SCALAR[s])
@@ -246,7 +265,7 @@ def tile_moe_shr_lin_relu2_kernel(tc, xT, w, b, gate, offs, pos1, pos2, out):
             regroup_shared(side_by_side_on_gpsimd, g, *ON_GPSIMD[g + 1])
         for s in (3, 2):
             for c0 in (0, CHUNK):
-                gather(s, c0)
+                gather(s, c0, EARLY if (s, c0) == (3, 0) else 0)
         for c0 in (0, CHUNK):
             for s in (0, 1):
                 gather(s, c0)

@@ -27,21 +27,20 @@ PAIRS = E // 2
 CHUNK = 1024
 HALF = T // 2
 THIRD = 384
-ON_VECTOR = 576
 EARLY = C
 EARLY_ROWS = 144
 LOADS = {2: ((0, T),), 0: ((0, T),), 1: ((0, HALF), (HALF, T))}
 ON_SCALAR = {2: (HALF, T), 0: (0, HALF), 1: (0, HALF)}
 ON_GPSIMD = {2: (0, HALF), 0: (HALF, T), 1: (HALF, T)}
 KIB = 1024
-BY_PASS = range(2, E)
+BY_PASS = (1, 3, 4, 5, 6, 7)
 
 RAW_X = {2: 0, 1: 8, 0: 16}
 SHARED_BF = {1: 24, 0: 32}
 PICKED = {(1, 0): 40, (1, CHUNK): 48, (0, 0): 56, (0, CHUNK): 64}
 RAW_W = [80, 72] + [72 + 8 * e for e in range(2, E + 1)]
-CAST_W = [144, 148, 152, 156, 40, 44, 56, 60, RAW_W[3]]
-SLOT_BF = {(1, 0): 4, (1, CHUNK): 14, (0, 0): RAW_W[2] - 4, (0, CHUNK): RAW_W[4] - 4}
+CAST_W = [144, 148, 152, 156, 40, 44, 56, 60, SHARED_BF[0]]
+SLOT_BF = {(1, 0): 4, (1, CHUNK): 14, (0, 0): 48, (0, CHUNK): RAW_W[3]}
 SHARED_CODES = RAW_W[7]
 GATES = 160
 Y = [RAW_W[1], 48]
@@ -108,10 +107,11 @@ def tile_moe_shr_lin_relu2_kernel(tc, xT, w, b, gate, offs, pos1, pos2, out):
             load_w(e)
         nc.sync.dma_start(bias[:], b.rearrange("(m p) e -> p m e", p=P))
         load_w(E)
-        gates = place("gates", GATES, [P, 2 * T], F32)
-        nc.sync.dma_start(gates[:].rearrange("p (r t) -> p r t", r=2), gate[:, 0:P, :].rearrange("r p t -> p r t"))
         nc.sync.dma_start(pos1_t[:], pos1)
         nc.sync.dma_start(pos2_t[:], pos2)
+        gates = place("gates", GATES, [P, 2 * T], F32)
+        for r in range(2):
+            nc.sync.dma_start(gates[:, T * r : T * (r + 1)], gate[r, 0:P, :])
 
         def gpsimd_copy(dst, src):
             nc.gpsimd.tensor_scalar(dst, src, 1.0, 0.0, MULT, ADD)
@@ -127,22 +127,25 @@ def tile_moe_shr_lin_relu2_kernel(tc, xT, w, b, gate, offs, pos1, pos2, out):
 
         w_bf = {}
 
-        def cast_w(copy, e):
-            w_bf[e] = place(f"w_bf{e}", CAST_W[e], [P, 8 * N], BF16)
+        def cast_w(copy, e, passes=(0, 1)):
+            if e not in w_bf:
+                w_bf[e] = place(f"w_bf{e}", CAST_W[e], [P, 8 * N], BF16)
             for ee, g0, g1 in w_raw:
-                if ee == e:
+                if ee == e and g0 in passes:
                     dst = w_bf[e][:, 4 * N * g0 : 4 * N * g1].rearrange("p (g c i j) -> p g c j i", c=N // 2, i=2, j=4)
                     copy(dst, w_raw[e, g0, g1][:].rearrange("p g j (c i) -> p g c j i", i=2))
 
-        def cast_w_on_gpsimd(e):
+        def cast_w_on_gpsimd(e, passes=(0, 1)):
             w_bf[e] = place(f"w_bf{e}", CAST_W[e], [P, 8 * N], BF16)
             for ee, g0, g1 in w_raw:
-                if ee == e:
+                if ee == e and g0 in passes:
                     dst = w_bf[e][:, 4 * N * g0 : 4 * N * g1].rearrange("p (g n j) -> p g n j", n=N, j=4)
                     gpsimd_copy(dst, w_raw[e, g0, g1][:].rearrange("p g j n -> p g n j"))
 
-        def quant_w(e):
-            nc.vector.quantize_mx(out=wcodes[e][:].bitcast(FP8X4), scales=wscales[e][:], in_=w_bf[e][:])
+        def quant_w(e, g0=0, g1=2):
+            cols = slice(N * g0, N * g1)
+            values = w_bf[e][:, 4 * N * g0 : 4 * N * g1]
+            nc.vector.quantize_mx(out=wcodes[e][:, cols].bitcast(FP8X4), scales=wscales[e][:, cols], in_=values)
 
         picked = {}
 
@@ -269,34 +272,37 @@ def tile_moe_shr_lin_relu2_kernel(tc, xT, w, b, gate, offs, pos1, pos2, out):
         for c0 in (0, CHUNK):
             for s in (0, 1):
                 gather(s, c0)
-        for e in (0, 1, 3):
-            cast_w_on_gpsimd(e)
+        cast_w_on_gpsimd(0)
+        cast_w_on_gpsimd(1, (0,))
+        cast_w_on_gpsimd(2)
         regroup(side_by_side_on_scalar, 1, 0)
         regroup(side_by_side_on_scalar, 1, CHUNK)
-        cast_w(nc.scalar.copy, 2)
+        cast_w(nc.scalar.copy, 1, (1,))
         regroup(side_by_side_on_scalar, 0, 0)
-        cast_w(nc.scalar.copy, 4)
-        regroup(side_by_side_on_scalar, 0, CHUNK, 0, CHUNK - ON_VECTOR)
-        for e in range(5, E):
+        for e in range(3, E):
             cast_w(nc.scalar.copy, e)
         quant_x(1, 0)
         quant_w(0)
         quant_w(1)
-        quant_w(2)
-        quant_x(0, 0)
-        quant_w(3)
         quant_x(1, CHUNK)
-        regroup(side_by_side_on_vector, 0, CHUNK, CHUNK - ON_VECTOR, CHUNK)
-        quant_w(4)
+        quant_x(0, 0)
+        quant_w(2)
+        regroup(side_by_side_on_vector, 0, CHUNK)
+        quant_w(3)
         quant_x(0, CHUNK)
+        quant_w(4)
         quant_w(5)
         quant_w(6)
         quant_w(7)
-        cast_w(nc.vector.tensor_copy, E)
         scodes = place("scodes", SHARED_CODES, [P, 2 * T], U32)
-        quant_shared(1)
-        quant_w(E)
         quant_shared(0)
+        quant_shared(1)
+        w_bf[E] = place("w_bf_shared", CAST_W[E], [P, 8 * N], BF16)
+        for g in range(2):
+            dst = w_bf[E][:, 4 * N * g : 4 * N * (g + 1)].rearrange("p (c i j) -> p c j i", i=2, j=4)
+            nc.vector.tensor_copy(dst, w_raw[E, 0, 2][:, g].rearrange("p j (c i) -> p c j i", i=2))
+        quant_w(E, 0, 1)
+        quant_w(E, 1, 2)
         for e0 in range(0, E, 4):
             for m in range(2):
                 for e in range(e0, e0 + 4):
@@ -305,8 +311,8 @@ def tile_moe_shr_lin_relu2_kernel(tc, xT, w, b, gate, offs, pos1, pos2, out):
         relu(0, 0)
         relu(1, 0)
         relu(0, 1)
-        relu(2, 0)
         square(y_pairs(0, 0, 2))
+        relu(2, 0)
         relu(3, 0)
         square(y_pairs(0, 2, 3))
         square(y_pairs(0, 3, 4))

@@ -27,20 +27,21 @@ PAIRS = E // 2
 CHUNK = 1024
 HALF = T // 2
 THIRD = 384
+ON_VECTOR = 768
 EARLY = C
 EARLY_ROWS = 144
 LOADS = {2: ((0, T),), 0: ((0, T),), 1: ((0, HALF), (HALF, T))}
 ON_SCALAR = {2: (HALF, T), 0: (0, HALF), 1: (0, HALF)}
 ON_GPSIMD = {2: (0, HALF), 0: (HALF, T), 1: (HALF, T)}
 KIB = 1024
-BY_PASS = (1, 3, 4, 5, 6, 7)
+BY_PASS = (1, 2, 4, 5, 6, 7)
 
 RAW_X = {2: 0, 1: 8, 0: 16}
 SHARED_BF = {1: 24, 0: 32}
 PICKED = {(1, 0): 40, (1, CHUNK): 48, (0, 0): 56, (0, CHUNK): 64}
-RAW_W = [80, 72] + [72 + 8 * e for e in range(2, E + 1)]
+RAW_W = [80, 72, 88, 104, 96] + [72 + 8 * e for e in range(5, E + 1)]
 CAST_W = [144, 148, 152, 156, 40, 44, 56, 60, SHARED_BF[0]]
-SLOT_BF = {(1, 0): 4, (1, CHUNK): 14, (0, 0): 48, (0, CHUNK): RAW_W[3]}
+SLOT_BF = {(1, 0): 4, (1, CHUNK): 14, (0, 0): 48, (0, CHUNK): RAW_W[4] - 4}
 SHARED_CODES = RAW_W[7]
 GATES = 160
 Y = [RAW_W[1], 48]
@@ -89,12 +90,14 @@ def tile_moe_shr_lin_relu2_kernel(tc, xT, w, b, gate, offs, pos1, pos2, out):
                 nc.sync.dma_start(x_raw[s, c0, c1], rows[:, 2 * h : 2 * h + 2, c0:c1])
                 shift += 2 * (c1 - c0)
 
+        def load_passes(e, g0, g1):
+            w_raw[e, g0, g1] = place(f"w_raw{e}{g0}", RAW_W[e] + 4 * g0, [P, g1 - g0, 4, N], F32)
+            rows = w[e, K_PASS * g0 : K_PASS * g1, :]
+            nc.sync.dma_start(w_raw[e, g0, g1][:], rows.rearrange("(g p j) n -> p g j n", p=P, j=4))
+
         def load_w(e):
-            passes = ((0, 1), (1, 2)) if e in BY_PASS else ((0, 2),)
-            for g0, g1 in passes:
-                w_raw[e, g0, g1] = place(f"w_raw{e}{g0}", RAW_W[e] + 4 * g0, [P, g1 - g0, 4, N], F32)
-                rows = w[e, K_PASS * g0 : K_PASS * g1, :]
-                nc.sync.dma_start(w_raw[e, g0, g1][:], rows.rearrange("(g p j) n -> p g j n", p=P, j=4))
+            for g0, g1 in ((0, 1), (1, 2)) if e in BY_PASS else ((0, 2),):
+                load_passes(e, g0, g1)
 
         first_rows = planes_and_rows[:, 4 * T : 6 * T].rearrange("p (e t) -> p e t", e=2)
         rows = xT[K_PASS:K, :].rearrange("(p j) t -> p j t", j=4)
@@ -103,7 +106,12 @@ def tile_moe_shr_lin_relu2_kernel(tc, xT, w, b, gate, offs, pos1, pos2, out):
         nc.sync.dma_start(offs_t[:], offs)
         for s in (2, 0, 1):
             load_x(s)
-        for e in range(E):
+        load_w(0)
+        load_w(1)
+        load_passes(2, 0, 1)
+        load_w(3)
+        load_passes(2, 1, 2)
+        for e in range(4, E):
             load_w(e)
         nc.sync.dma_start(bias[:], b.rearrange("(m p) e -> p m e", p=P))
         load_w(E)
@@ -274,12 +282,16 @@ def tile_moe_shr_lin_relu2_kernel(tc, xT, w, b, gate, offs, pos1, pos2, out):
                 gather(s, c0)
         cast_w_on_gpsimd(0)
         cast_w_on_gpsimd(1, (0,))
-        cast_w_on_gpsimd(2)
+        cast_w_on_gpsimd(2, (0,))
+        cast_w_on_gpsimd(3)
         regroup(side_by_side_on_scalar, 1, 0)
         regroup(side_by_side_on_scalar, 1, CHUNK)
         cast_w(nc.scalar.copy, 1, (1,))
         regroup(side_by_side_on_scalar, 0, 0)
-        for e in range(3, E):
+        cast_w(nc.scalar.copy, 2, (1,))
+        cast_w(nc.scalar.copy, 4)
+        regroup(side_by_side_on_scalar, 0, CHUNK, 0, CHUNK - ON_VECTOR)
+        for e in range(5, E):
             cast_w(nc.scalar.copy, e)
         quant_x(1, 0)
         quant_w(0)
@@ -287,10 +299,10 @@ def tile_moe_shr_lin_relu2_kernel(tc, xT, w, b, gate, offs, pos1, pos2, out):
         quant_x(1, CHUNK)
         quant_x(0, 0)
         quant_w(2)
-        regroup(side_by_side_on_vector, 0, CHUNK)
         quant_w(3)
-        quant_x(0, CHUNK)
+        regroup(side_by_side_on_vector, 0, CHUNK, CHUNK - ON_VECTOR, CHUNK)
         quant_w(4)
+        quant_x(0, CHUNK)
         quant_w(5)
         quant_w(6)
         quant_w(7)

from contextlib import ExitStack

import concourse.mybir as mybir
from concourse.masks import make_identity

K, T, E, C, N = 1024, 1024, 8, 256, 256
S = E * C
P = 128
FLOPS = 2 * K * N * (S + T)

F32 = mybir.dt.float32
BF16 = mybir.dt.bfloat16
U32 = mybir.dt.uint32
I32 = mybir.dt.int32
U16 = mybir.dt.uint16
U8 = mybir.dt.uint8
FP8X4 = mybir.dt.float8_e4m3fn_x4

RELU = mybir.ActivationFunctionType.Relu
SQUARE = mybir.ActivationFunctionType.Square
COPY = mybir.ActivationFunctionType.Copy
MULT, ADD = mybir.AluOpType.mult, mybir.AluOpType.add

K_PASS = 512
BANK = 512
PAIRS = E // 2
CHUNK = 1024
HALF = T // 2
THIRD = 384
ON_VECTOR = 768
EARLY = C
EARLY_ROWS = 144
LOADS = {2: ((0, T),), 0: ((0, T),), 1: ((0, HALF), (HALF, T))}
ON_SCALAR = {2: (HALF, T), 0: (0, HALF), 1: (0, HALF)}
ON_GPSIMD = {2: (0, HALF), 0: (HALF, T), 1: (HALF, T)}
KIB = 1024
BY_PASS = (1, 2, 4, 5, 6, 7)

RAW_X = {2: 0, 1: 8, 0: 16}
SHARED_BF = {1: 24, 0: 32}
PICKED = {(1, 0): 40, (1, CHUNK): 48, (0, 0): 56, (0, CHUNK): 64}
RAW_W = [80, 72, 88, 104, 96] + [72 + 8 * e for e in range(5, E + 1)]
CAST_W = [144, 148, 152, 156, 40, 44, 56, 60, SHARED_BF[0]]
SLOT_BF = {(1, 0): 4, (1, CHUNK): 14, (0, 0): 48, (0, CHUNK): RAW_W[4] - 4}
SHARED_CODES = RAW_W[7]
GATES = 160
Y = [RAW_W[1], 48]
YS = RAW_W[0]
TERMS = RAW_W[5]
TERMS_LAST = 144


def tile_moe_shr_lin_relu2_kernel(tc, xT, w, b, gate, offs, pos1, pos2, out):
    nc = tc.nc
    with ExitStack() as ctx:
        lists = ctx.enter_context(tc.tile_pool(name="lists", bufs=1))
        keep = ctx.enter_context(tc.tile_pool(name="keep", bufs=1))
        placed = ctx.enter_context(tc.tile_pool(name="placed", bufs=1))
        psum = ctx.enter_context(tc.psum_pool(name="psum", bufs=8))

        def place(name, kib, shape, dtype, shift=0):
            return placed.tile(shape, dtype, name=name, offset=kib * KIB + shift, align_bytes=64)

        offs_t = lists.tile([P, S // 16], U16, name="offs_t")
        pos1_t = lists.tile([P, T // 16], U16, name="pos1_t")
        pos2_t = lists.tile([P, T // 16], U16, name="pos2_t")
        pos = (pos1_t, pos2_t)

        planes_and_rows = keep.tile([P, 6 * T], F32, name="planes_and_rows")
        planes = planes_and_rows[:].bitcast(U32)
        wcodes = [keep.tile([P, 2 * N], U32, name=f"wcodes{e}", align_bytes=64) for e in range(E + 1)]
        wscales = [keep.tile([P, 2 * N], U8, name=f"wscales{e}", align_bytes=64) for e in range(E + 1)]
        xcodes = [keep.tile([P, S], U32, name=f"xcodes{g}", align_bytes=64) for g in range(2)]
        xscales = [keep.tile([P, S], U8, name=f"xscales{g}", align_bytes=64) for g in range(2)]
        sscales = [keep.tile([P, T], U8, name=f"sscales{g}", align_bytes=64) for g in range(2)]
        bias = keep.tile([P, 2, E + 1], F32, name="bias")

        ident = keep.tile([P, P], F32, name="ident")
        make_identity(nc, ident[:])

        x_raw, w_raw = {}, {}

        def load_x(s):
            g, h = divmod(s, 2)
            rows = xT[K_PASS * g : K_PASS * (g + 1), :].rearrange("(p j) t -> p j t", j=4)
            shift = 0
            for c0, c1 in LOADS[s]:
                flat = place(f"x_raw{s}_{c0}", RAW_X[s], [P, 2 * (c1 - c0)], F32, 4 * shift)[:]
                x_raw[s, c0, c1] = flat.rearrange("p (e t) -> p e t", e=2)
                nc.sync.dma_start(x_raw[s, c0, c1], rows[:, 2 * h : 2 * h + 2, c0:c1])
                shift += 2 * (c1 - c0)

        def load_passes(e, g0, g1):
            w_raw[e, g0, g1] = place(f"w_raw{e}{g0}", RAW_W[e] + 4 * g0, [P, g1 - g0, 4, N], F32)
            rows = w[e, K_PASS * g0 : K_PASS * g1, :]
            nc.sync.dma_start(w_raw[e, g0, g1][:], rows.rearrange("(g p j) n -> p g j n", p=P, j=4))

        def load_w(e):
            for g0, g1 in ((0, 1), (1, 2)) if e in BY_PASS else ((0, 2),):
                load_passes(e, g0, g1)

        first_rows = planes_and_rows[:, 4 * T : 6 * T].rearrange("p (e t) -> p e t", e=2)
        rows = xT[K_PASS:K, :].rearrange("(p j) t -> p j t", j=4)
        for c0, c1 in ((384, T), (0, 384)):
            nc.sync.dma_start(first_rows[:, :, c0:c1], rows[:, 2:4, c0:c1])
        nc.sync.dma_start(offs_t[:], offs)
        for s in (2, 0, 1):
            load_x(s)
        load_w(0)
        load_w(1)
        load_passes(2, 0, 1)
        load_w(3)
        load_passes(2, 1, 2)
        for e in range(4, E):
            load_w(e)
        nc.sync.dma_start(bias[:], b.rearrange("(m p) e -> p m e", p=P))
        load_w(E)
        nc.sync.dma_start(pos1_t[:], pos1)
        nc.sync.dma_start(pos2_t[:], pos2)
        gates = place("gates", GATES, [P, 2 * T], F32)
        for r in range(2):
            nc.sync.dma_start(gates[:, T * r : T * (r + 1)], gate[r, 0:P, :])

        def gpsimd_copy(dst, src):
            nc.gpsimd.tensor_scalar(dst, src, 1.0, 0.0, MULT, ADD)

        def cast_x(copy, s, c0, c1):
            words = planes[:, s * T + c0 : s * T + c1]
            if s == 3:
                rows = first_rows[:, :, c0:c1]
            else:
                l0, l1 = [(a, z) for a, z in LOADS[s] if a <= c0 < z][0]
                rows = x_raw[s, l0, l1][:, :, c0 - l0 : c1 - l0]
            copy(words.bitcast(BF16).rearrange("p (t e) -> p t e", e=2), rows.rearrange("p e t -> p t e"))

        w_bf = {}

        def cast_w(copy, e, passes=(0, 1)):
            if e not in w_bf:
                w_bf[e] = place(f"w_bf{e}", CAST_W[e], [P, 8 * N], BF16)
            for ee, g0, g1 in w_raw:
                if ee == e and g0 in passes:
                    dst = w_bf[e][:, 4 * N * g0 : 4 * N * g1].rearrange("p (g c i j) -> p g c j i", c=N // 2, i=2, j=4)
                    copy(dst, w_raw[e, g0, g1][:].rearrange("p g j (c i) -> p g c j i", i=2))

        def cast_w_on_gpsimd(e, passes=(0, 1)):
            w_bf[e] = place(f"w_bf{e}", CAST_W[e], [P, 8 * N], BF16)
            for ee, g0, g1 in w_raw:
                if ee == e and g0 in passes:
                    dst = w_bf[e][:, 4 * N * g0 : 4 * N * g1].rearrange("p (g n j) -> p g n j", n=N, j=4)
                    gpsimd_copy(dst, w_raw[e, g0, g1][:].rearrange("p g j n -> p g n j"))

        def quant_w(e, g0=0, g1=2):
            cols = slice(N * g0, N * g1)
            values = w_bf[e][:, 4 * N * g0 : 4 * N * g1]
            nc.vector.quantize_mx(out=wcodes[e][:, cols].bitcast(FP8X4), scales=wscales[e][:, cols], in_=values)

        picked = {}

        def picked_words(s, c0):
            g, h = divmod(s, 2)
            if (g, c0) not in picked:
                picked[g, c0] = place(f"picked{g}_{c0}", PICKED[g, c0], [P, 2 * CHUNK], U32)
            return picked[g, c0][:, CHUNK * h : CHUNK * (h + 1)]

        def gather(s, c0, a=0):
            window = planes[:, s * T : (s + 2) * T]
            nc.vector.tensor_copy(picked_words(s, c0)[:, a:CHUNK], window.indirect(offs_t[:, (c0 + a) // 16 : (c0 + CHUNK) // 16]))

        def gather_early():
            early = place("early", EARLY_ROWS, [P, 2 * EARLY], F32)
            for j in range(2):
                for c0 in range(0, EARLY, C):
                    window = planes_and_rows[:, (4 + j) * T : (5 + j) * T]
                    dst = early[:, j * EARLY + c0 : j * EARLY + c0 + C]
                    nc.scalar.activation(dst, window.indirect(offs_t[:, c0 // 16 : (c0 + C) // 16]), COPY)
            pairs = picked_words(3, 0)[:, 0:EARLY].bitcast(BF16).rearrange("p (t e) -> p t e", e=2)
            nc.scalar.copy(pairs, early[:].rearrange("p (e t) -> p t e", e=2))

        def side_by_side_on_vector(dst, both):
            nc.vector.tensor_copy(
                dst.bitcast(I32).rearrange("p (c i h) -> p c h i", i=2, h=2),
                both.bitcast(I32).rearrange("p h (c i) -> p c h i", i=2),
            )

        def side_by_side_on_scalar(dst, both):
            nc.scalar.copy(
                dst.bitcast(U32).rearrange("p (c i h) -> p c h i", i=2, h=2),
                both.rearrange("p h (c i) -> p c h i", i=2),
            )

        x_bf = {}

        def side_by_side_on_gpsimd(dst, both):
            nc.gpsimd.tensor_copy(dst.bitcast(U32).rearrange("p (c h) -> p c h", h=2), both.rearrange("p h c -> p c h"))

        def regroup(side_by_side, g, c0, a=0, z=CHUNK):
            if (g, c0) not in x_bf:
                x_bf[g, c0] = place(f"x_bf{g}_{c0}", SLOT_BF[g, c0], [P, 4 * CHUNK], BF16)
            side_by_side(x_bf[g, c0][:, 4 * a : 4 * z], picked[g, c0][:].rearrange("p (h c) -> p h c", h=2)[:, :, a:z])

        def quant_x(g, c0):
            cols = slice(c0, c0 + CHUNK)
            nc.vector.quantize_mx(out=xcodes[g][:, cols].bitcast(FP8X4), scales=xscales[g][:, cols], in_=x_bf[g, c0][:])

        banks = {}

        def multiply(e, m):
            k, i = divmod(e, 2)
            if i == 0:
                banks[k, m] = psum.tile([P, BANK], F32, name="ps")
            for g in (1, 0):
                w0 = N * g + P * m
                nc.tensor.matmul_mx(
                    out=banks[k, m][:, C * i : C * (i + 1)],
                    lhsT=wcodes[e][:, w0 : w0 + P].bitcast(FP8X4),
                    lhsT_scale=wscales[e][:, w0 : w0 + P],
                    rhs=xcodes[g][:, C * e : C * (e + 1)].bitcast(FP8X4),
                    rhs_scale=xscales[g][:, C * e : C * (e + 1)],
                    start=(g == 1),
                    stop=(g == 0),
                )

        y = {}

        def relu(k, m):
            if m not in y:
                y[m] = place(f"y{m}", Y[m], [P, S], F32)
            for i in range(2):
                e = 2 * k + i
                nc.scalar.activation(
                    y[m][:, C * e : C * (e + 1)], banks[k, m][:, C * i : C * (i + 1)], RELU, bias=bias[:, m, e : e + 1]
                )

        def square(v):
            nc.scalar.activation(v, v, SQUARE)

        def y_pairs(m, k0, k1):
            return y[m][:, BANK * k0 : BANK * k1]

        s_bf = {}

        def regroup_shared(side_by_side, g, c0, c1):
            if g not in s_bf:
                s_bf[g] = place(f"s_bf{g}", SHARED_BF[g], [P, 4 * T], BF16)
            both = planes[:, 2 * g * T : 2 * (g + 1) * T].rearrange("p (h c) -> p h c", h=2)
            side_by_side(s_bf[g][:, 4 * c0 : 4 * c1], both[:, :, c0:c1])

        def quant_shared(g):
            nc.vector.quantize_mx(out=scodes[:, T * g : T * (g + 1)].bitcast(FP8X4), scales=sscales[g][:], in_=s_bf[g][:])

        def multiply_shared(m, half):
            banks[PAIRS, m, half] = psum.tile([P, BANK], F32, name="ps")
            for g in (1, 0):
                w0 = N * g + P * m
                t0 = BANK * half
                nc.tensor.matmul_mx(
                    out=banks[PAIRS, m, half][:],
                    lhsT=wcodes[E][:, w0 : w0 + P].bitcast(FP8X4),
                    lhsT_scale=wscales[E][:, w0 : w0 + P],
                    rhs=scodes[:, T * g + t0 : T * g + t0 + BANK].bitcast(FP8X4),
                    rhs_scale=sscales[g][:, t0 : t0 + BANK],
                    start=(g == 1),
                    stop=(g == 0),
                )

        cast_x(nc.vector.tensor_copy, 3, 384, T)
        cast_x(nc.vector.tensor_copy, 3, 128, 384)
        cast_x(nc.scalar.copy, 3, 0, 128)
        gather_early()
        for g in (1, 0):
            for s in (2,) if g else (0, 1):
                cast_x(nc.scalar.copy, s, *ON_SCALAR[s])
                cast_x(gpsimd_copy, s, *ON_GPSIMD[s])
            regroup_shared(side_by_side_on_scalar, g, *ON_SCALAR[g + 1])
            regroup_shared(side_by_side_on_gpsimd, g, *ON_GPSIMD[g + 1])
        for s in (3, 2):
            for c0 in (0, CHUNK):
                gather(s, c0, EARLY if (s, c0) == (3, 0) else 0)
        for c0 in (0, CHUNK):
            for s in (0, 1):
                gather(s, c0)
        cast_w_on_gpsimd(0)
        cast_w_on_gpsimd(1, (0,))
        cast_w_on_gpsimd(2, (0,))
        cast_w_on_gpsimd(3)
        regroup(side_by_side_on_scalar, 1, 0)
        regroup(side_by_side_on_scalar, 1, CHUNK)
        cast_w(nc.scalar.copy, 1, (1,))
        regroup(side_by_side_on_scalar, 0, 0)
        cast_w(nc.scalar.copy, 2, (1,))
        cast_w(nc.scalar.copy, 4)
        regroup(side_by_side_on_scalar, 0, CHUNK, 0, CHUNK - ON_VECTOR)
        for e in range(5, E):
            cast_w(nc.scalar.copy, e)
        quant_x(1, 0)
        quant_w(0)
        quant_w(1)
        quant_x(1, CHUNK)
        quant_x(0, 0)
        quant_w(2)
        quant_w(3)
        regroup(side_by_side_on_vector, 0, CHUNK, CHUNK - ON_VECTOR, CHUNK)
        quant_w(4)
        quant_x(0, CHUNK)
        quant_w(5)
        quant_w(6)
        quant_w(7)
        scodes = place("scodes", SHARED_CODES, [P, 2 * T], U32)
        quant_shared(0)
        quant_shared(1)
        w_bf[E] = place("w_bf_shared", CAST_W[E], [P, 8 * N], BF16)
        for g in range(2):
            dst = w_bf[E][:, 4 * N * g : 4 * N * (g + 1)].rearrange("p (c i j) -> p c j i", i=2, j=4)
            nc.vector.tensor_copy(dst, w_raw[E, 0, 2][:, g].rearrange("p j (c i) -> p c j i", i=2))
        quant_w(E, 0, 1)
        quant_w(E, 1, 2)
        for e0 in range(0, E, 4):
            for m in range(2):
                for e in range(e0, e0 + 4):
                    multiply(e, m)

        relu(0, 0)
        relu(1, 0)
        relu(0, 1)
        square(y_pairs(0, 0, 2))
        relu(2, 0)
        relu(3, 0)
        square(y_pairs(0, 2, 3))
        square(y_pairs(0, 3, 4))
        for k in range(1, PAIRS):
            relu(k, 1)
        square(y_pairs(1, 0, 3))
        square(y_pairs(1, 3, 4))
        for m in range(2):
            for half in range(2):
                multiply_shared(m, half)
        ys_all = place("ys", YS, [P, 2 * T], F32)

        def ys(m, half):
            return ys_all[:, T * m + BANK * half : T * m + BANK * (half + 1)]

        def relu_shared(m, half):
            nc.scalar.activation(ys(m, half), banks[PAIRS, m, half][:], RELU, bias=bias[:, m, E : E + 1])

        relu_shared(0, 0)
        relu_shared(0, 1)
        square(ys(0, 0))
        relu_shared(1, 0)
        square(ys(0, 1))
        square(ys(1, 0))

        def fetch(dst, r, m, c0, n):
            weight = gates[:, T * r + c0 : T * r + c0 + n]
            nc.vector.tensor_tensor(dst, y[m][:].indirect(pos[r][:, c0 // 16 : (c0 + n) // 16]), weight, MULT)

        def shared_term(m, c0, n):
            return ys_all[:, T * m + c0 : T * m + c0 + n]

        def add_into(dst, other):
            nc.vector.tensor_tensor(dst, dst, other, ADD)

        def store(src, m, c0, n):
            nc.sync.dma_start(out[m * P : (m + 1) * P, c0 : c0 + n], src)

        terms, turned = {}, {}
        units = [(0, 0, BANK), (0, BANK, BANK), (1, 0, THIRD)]
        whole = [place(f"terms0{r}", TERMS + 4 * r, [P, T], F32) for r in range(2)]
        for r in range(2):
            fetch(whole[r][:], r, 0, 0, T)
        for u in units[:2]:
            terms[u] = [whole[r][:, u[1] : u[1] + BANK] for r in range(2)]
        terms[units[2]] = [place(f"terms2{r}", TERMS + 8 + 2 * r, [P, THIRD], F32)[:] for r in range(2)]
        for r in range(2):
            fetch(terms[units[2]][r], r, *units[2])

        def add_turned(u, term, first, last):
            if first:
                turned[u] = psum.tile([P, BANK], F32, name="ps")
            for j in range(0, u[2], P):
                nc.tensor.matmul(
                    turned[u][:, j : j + P], term[:, j : j + P], ident[:],
                    start=(first and j == 0), stop=(last and j == u[2] - P), is_transpose=True,
                )

        def empty_turned(u):
            nc.scalar.copy(terms[u][1], turned[u][:, 0 : u[2]])

        def turn_back(u):
            turned[u] = psum.tile([P, BANK], F32, name="ps")
            for j in range(0, u[2], P):
                nc.tensor.transpose(turned[u][:, j : j + P], terms[u][1][:, j : j + P], ident[:])

        def store_turned(u):
            nc.scalar.copy(terms[u][0], turned[u][:, 0 : u[2]])
            store(terms[u][0], *u)

        for i in range(3):
            for u in units[:2]:
                add_turned(u, (*terms[u], shared_term(*u))[i], i == 0, i == 2)
        empty_turned(units[0])
        turn_back(units[0])
        relu_shared(1, 1)
        for i in range(3):
            add_turned(units[2], (shared_term(*units[2]), *terms[units[2]])[i], i == 0, i == 2)
        empty_turned(units[1])
        turn_back(units[1])
        square(ys(1, 1))
        store_turned(units[0])
        empty_turned(units[2])
        turn_back(units[2])
        store_turned(units[1])
        store_turned(units[2])

        rest = T - THIRD
        t = place("terms_last", TERMS_LAST, [P, 2 * rest], F32)
        first, second = t[:, 0:rest], t[:, rest : 2 * rest]
        pieces = ((0, rest - C), (rest - C, C))
        fetch(first, 0, 1, THIRD, rest)
        fetch(second[:, 0 : rest - C], 1, 1, THIRD, rest - C)
        add_into(first, shared_term(1, THIRD, rest))
        fetch(second[:, rest - C : rest], 1, 1, T - C, C)
        total = place("total", TERMS + 4 * 2 + 2, [P, rest], F32)
        for c0, n in pieces:
            cols = slice(c0, c0 + n)
            nc.vector.tensor_tensor(total[:, cols], first[:, cols], second[:, cols], ADD)
            store(total[:, cols], 1, THIRD + c0, n)
